import numpy as np, ml_dtypes
CORES = [3,11,19,27,35,43,51,59]
N = 8
BF = ml_dtypes.bfloat16
LA, SUB, W, V, VIS, TRY, R1, R2 = 192, 16, 3072, 4096, 4, 3, 8, 13
A = [6, 4, 4, 3]
def levels(rng, n, lo, hi):
    return np.minimum((np.exp2(lo + (hi - lo) * rng.random((N, 8, 1, n))) * rng.random((N, 8, 16, n))).astype(np.int64), 255)
def slots(rng):
    share = rng.choice(np.array([0.3, 0.6, 0.9, 1.0]), (N, 8, 1, LA))
    return np.where(rng.random((N, 8, 16, LA)) < share, rng.integers(0, W, (N, 8, 16, LA)), -1)
def parts(rng):
    return (levels(rng, W, 6.5, 9.0), levels(rng, V, 5.5, 9.0), slots(rng), levels(rng, LA, 6.5, 9.0), rng.integers(1, 256, (N, 8, 16)), rng.integers(0, 256, (N, 8, 16)))
def pack(x, c, s, z, w, p):
    b = lambda v: np.ascontiguousarray(v.reshape(N, 128, -1)).astype(np.float32).astype(BF)
    i = lambda v: np.ascontiguousarray(v.reshape(N, 128, -1)).astype(np.int32)
    return {"x0": b(x), "cl": b(c), "sl": i(s), "z0": b(z), "wt": i(w), "kp": i(p)}
def setup_inputs(rng):
    return pack(*parts(rng))
def setup_inputs_spread(rng):
    x, c, s, z, w, p = parts(rng)
    x, c, z = levels(rng, W, 0.0, 9.0), levels(rng, V, 0.0, 9.0), levels(rng, LA, 0.0, 9.0)
    w = np.clip(np.exp2(8 * rng.random(w.shape)).astype(np.int64), 1, 255); p = np.clip(np.exp2(8 * rng.random(p.shape)).astype(np.int64) - 1, 0, 255)
    return pack(x, c, s, z, w, p)
def setup_inputs_ends(rng):
    e = lambda n, d: 255 * (rng.random((N, 8, 16, n)) < rng.choice(np.array(d), (N, 8, 1, n))).astype(np.int64)
    x, c, z = e(W, [0.3, 0.6, 0.9]), e(V, [0.0, 0.5, 0.9, 1.0]), e(LA, [0.3, 0.6, 0.9])
    r = rng.random((N, 8, 16, LA))
    s = np.where(r < 0.35, -1, np.where(r < 0.7, W - 1, np.where(r < 0.8, 0, rng.integers(0, W, r.shape))))
    w = np.where(rng.random((N, 8, 16)) < 0.5, 1, 255); w[:, :, 13:15] = 1; w[:, :, 15] = 255; w[:, 6] = 255
    p = 255 * rng.integers(0, 2, (N, 8, 16)); p[:, 7, 0] = 255; p[:, 7, 15] = 255; p[:, 7, 1] = 0
    x[..., W - 1] = 255
    for i in (0, LA - 1):
        z[..., i] = 0; z[:, :, 13:, i] = 255; s[:, :, 0, i] = W - 1
    for i in (1, LA - 2): z[..., i] = 255
    for i in (2, LA - 3): z[..., i] = 0
    return pack(x, c, s, z, w, p)
def setup_inputs_corners(rng):
    x, c, s, z, w, p = parts(rng); x[..., 0] = 255; x[..., W - 1] = 0
    kind = rng.integers(0, 10, (N, 8, 1, LA)); kind[..., :10] = np.arange(10); kind[..., LA - 10:] = np.arange(10)
    k = np.arange(16)[:, None]; o = np.argsort(rng.random((N, 8, 16, LA)), axis=2); any_ = rng.integers(0, W, s.shape)
    low = np.arange(LA) < LA // 2
    s = np.where(kind == 0, -1, s); s = np.where(kind == 1, any_, s)
    s = np.where(kind == 2, np.where(k == np.where(low, 13, 15), 0, W - 1), s)
    s = np.where(kind == 3, np.where(o < TRY, 0, W - 1), s); s = np.where(kind == 4, np.where(o < TRY + 1, 0, W - 1), s)
    s = np.where(kind == 5, np.where(k == 15, any_, -1), s); s = np.where(kind == 6, np.where(k == 15, -1, any_), s)
    s = np.where(kind == 7, SUB * np.arange(LA) + any_ % SUB, s); s = np.where(kind == 8, any_[:, :, :1], s)
    z = np.where(kind == 1, 255, z); z = np.where((kind >= 2) & (kind <= 4), np.minimum(z, 254), z); z = np.where((kind == 2) & low, 254, z)
    for q in range(N):
        g = rng.permutation(8)
        c[q, g[:2]] = 0; c[q, g[2:4]] = 255
        w[q, g[0]] = 1; w[q, g[2]] = 255; w[q, g[4]] = 255; w[q, g[5]] = 1; p[q, g[3]] = 0; p[q, g[5]] = 255; p[q, g[6]] = 0
    return pack(x, c, s, z, w, p)
def setup_inputs_ties(rng):
    x, c, s, z, w, p = parts(rng)
    x, c, z = 85 * (x >> 6), 85 * (c >> 6), 85 * (z >> 6)
    x[..., 1::2] = x[..., ::2]
    same = np.take_along_axis(x, np.maximum(s[:, :, 3:4], 0), 3)
    z = np.where(rng.random((N, 8, 1, LA)) < 0.5, same, z)
    return pack(x, c, s, z, w, p)
def setup_inputs_bits(rng):
    x, c, s, z, w, p = parts(rng); k = np.arange(16)[:, None]
    one = k == rng.integers(0, 16, (N, 8, 1, 1))
    x[..., 0] = 255; x[..., W - 2] = 0; x[..., W - 1:] = np.where(one, 255, 0)
    kind = rng.choice(np.array([0, 0, 1, 2, 3, 3]), (N, 1, 1, LA))
    m = np.where(kind == 0, 8, 1 + 2 * rng.integers(0, 4, kind.shape)); on = np.argsort(rng.random((N, 8, 1, LA)), axis=1) < m
    first = np.where(kind == 1, 0, TRY - 1)
    v = np.where(k < first, W - 1, np.where(k == first, 0, s))
    v = np.where(on, v, np.where(rng.random((N, 8, 1, LA)) < 0.5, -1, W - 2))
    s = np.where(kind < 3, v, s)
    high = 255 - (rng.random((N, 8, 16, LA)) < rng.choice(np.array([0.0, 0.5, 1.0]), (N, 1, 1, LA))).astype(np.int64)
    z = np.where(kind < 3, np.where(one, 254, high), z)
    w[:, 7] = 255
    return pack(x, c, s, z, w, p)
def check_inputs(d):
    bad = []
    for k, lo, hi in (("x0", 0, 255), ("cl", 0, 255), ("sl", -1, W - 1), ("z0", 0, 255), ("wt", 1, 255), ("kp", 0, 255)):
        v = np.asarray(d[k]).astype(np.float32)
        if np.min(v) < lo or np.max(v) > hi or np.any(v != np.floor(v)): bad.append("range of " + k)
    return bad
def hashes(v, w, p, t):
    u = np.add.reduce(w * v, axis=2) & (V - 1)
    return u, ((u * u >> 5)[:, :, None] + p * u[:, :, None] + 97 * t) & (V - 1)
def reference(x0, cl, sl, z0, wt, kp):
    x = x0.astype(np.float32).astype(np.int32).reshape(N, 8, 16, W); c = cl.astype(np.float32).astype(np.int32).reshape(N, 8, 16, V)
    z = z0.astype(np.float32).astype(np.int32).reshape(N, 8, 16, LA); s = sl.astype(np.int32).reshape(N, 8, 16, LA)
    w = wt.astype(np.int32).reshape(N, 8, 16, 1); p = kp.astype(np.int32).reshape(N, 8, 16, 1)
    bit = np.zeros((N, LA), np.int64); k16 = np.arange(16)[:, None]
    for t in range(VIS):
        J = (np.arange(N) + 1 + t % (N - 1)) % N
        filled = s >= 0
        old = np.take_along_axis(x, np.maximum(s, 0).reshape(N, 8, 1, 16 * LA), 3).reshape(N, 8, 16, 16, LA)
        m = np.minimum(z[:, :, :, None], old)
        free = filled & (np.add.reduce(m, axis=2) < np.add.reduce(old, axis=2))
        done = np.zeros((N, 8, LA), bool); best = z; put = np.zeros((N, 8, LA), np.int64)
        for trial in range(TRY):
            has = np.any(free, axis=2) & ~done; k = np.argmax(free, axis=2)
            cand = np.take_along_axis(m, k[:, :, None, None], 3)[:, :, :, 0]
            h = hashes(cand, w[J], p[J], t)[1]
            b = np.take_along_axis(c[J], h.reshape(N, 8, 1, 16 * LA), 3).reshape(N, 8, 16, 16, LA)
            met = np.add.reduce((b <= cand[:, :, :, None]).astype(np.int32), axis=2) >= R1
            neg = has & (np.add.reduce(met.astype(np.int32), axis=2) >= A[t] + bit[J][:, None])
            bit[J] = np.add.reduce(neg.astype(np.int64), axis=1) & 1
            best = np.where(neg[:, :, None], cand, best); put = np.where(neg, k, put); done = done | neg
            free = free & (k16 != k[:, :, None])
        put = np.where(done, put, np.where(np.any(~filled, axis=2), np.argmax(~filled, axis=2), t))
        n = SUB * np.arange(LA) + (hashes(best, w, p, t)[0] & (SUB - 1))
        near = filled & (np.add.reduce((old <= best[:, :, :, None]).astype(np.int32), axis=2) >= R2)
        v = np.maximum(best, np.maximum.reduce(np.where(near[:, :, None], old, 0), axis=3))
        h0 = hashes(v, w, p, t)[1][:, :, :1]
        z = np.abs(v - np.take_along_axis(c, h0, 3))
        np.put_along_axis(x, np.ascontiguousarray(np.broadcast_to(n[:, :, None], (N, 8, 16, LA))), best, 3)
        s = np.where(k16 == put[:, :, None], n[:, :, None], s)
    return {"yx": x.reshape(N, 128, W).astype(np.float32).astype(BF), "yl": s.reshape(N, 128, LA).astype(np.float32), "yz": z.reshape(N, 128, LA).astype(np.float32).astype(BF)}

@@ -1,0 +1,675 @@
+from concourse.mybir import AluOpType as OP, ActivationFunctionType as AF
+
+N, LA, W, V, VIS = 8, 192, 3072, 4096, 4
+A = [6, 4, 4, 3]
+ZB = 3072
+L, C, W3 = 192, 12, 36
+NB = 8
+SO = 4
+M0 = 10
+GRP = ((0, 2), (2, 3))
+CHUNKS = (((0, 4), (4, 16)), ((0, 16),))
+GV = ((0, 2), ())
+TOL, LEAD, LAT = 0.02, 5.0, 0.15
+CY, GA = 0.00083, 1.5
+
+SCRATCH = {}
+for _t, _l in (
+        ("bfloat16", (("X", W + 16), ("CL", V), ("ones", 128), ("neg", 2048), ("R", 2048), ("SLh", 144), ("c8L", W3), ("I", 128), ("nI", 128),
+                      ("I64", 128), ("I3", 128), ("I2", 128), ("I1", 128), ("spk", 144), ("SLa", 144), ("SL", 144), ("SLL", 144), ("BOa", 128), ("BO", 128),
+                      ("Tri", 128), ("Q16", 128), ("GR", 128), ("GRh", 128), ("LI3b", W3), ("LIb", C), ("c3L", C), ("kpd", 16), ("DX", 576), ("DK", 576),
+                      ("Oa", 17 * L), ("Ob", 17 * L), ("Ca", 4 * L), ("Cb", 4 * L), ("cmp", 16 * L), ("op", L), ("le", 3 * L), ("G", 48 * L), ("SG", 16 * L),
+                      ("ge", 3 * L), ("nb", 6 * C), ("M", L), ("nn", L), ("acc", 768), ("fo", 384), ("cc", L), ("df", L))),
+        ("float32", (("cmk0", 128), ("cmk1", 128), ("PM00", 128), ("PM01", 128), ("PM10", 128), ("PM11", 128), ("p15f", 1), ("kempty", 1), ("thrn", 1),
+                     ("thrc", 1), ("cols", 1), ("recb", 12), ("LI3f", W3), ("KIL", L), ("sad", LA), ("sae", LA), ("T1", LA), ("T2", LA), ("T3", LA), ("T4", LA),
+                     ("T5", LA), ("T6", LA), ("kpf", 1), ("WK0", 24), ("B0", 12), ("kL", W3), ("pen", W3), ("KU", 576), ("cm", W3), ("cd", 2 * C), ("s", L),
+                     ("eq", L), ("dd", L), ("ed", L), ("mx", 15 * C), ("fe", 4 * C), ("pu", 3 * C), ("nf", C))),
+        ("int32", (("pc", 1), ("p15", 1), ("g16", 12), ("p15t", 12), ("LI", 12), ("e12", 12), ("q12", 12), ("sln", LA), ("wti", 1), ("kpi", 1),
+                   ("ui", W3), ("um", W3), ("sq", W3), ("ba", W3), ("Hs", 576), ("Hm", 576), ("bt", 3 * C), ("ci", 8 * C), ("ni", 2 * C))),
+        ("uint16", (("TW", 18), ("TK", 12), ("off", W3), ("ho", 576), ("bo", C), ("ch", C), ("s16", L), ("n16", C)))):
+    for _n, _c in _l:
+        SCRATCH[_n] = ("sbuf", [128, _c], _t)
+for _q in range(1, 5):
+    SCRATCH["BK%d" % _q] = ("sbuf", [128, V], "bfloat16")
+    SCRATCH["WK%d" % _q] = ("sbuf", [128, 24], "float32")
+for _q in range(5):
+    SCRATCH["SW%d" % _q] = ("sbuf", [128, 144], "bfloat16")
+    SCRATCH["KX%d" % _q] = ("sbuf", [128, 576], "float32")
+for _t in range(1, VIS):
+    SCRATCH["bs%d" % _t] = ("sbuf", [128, 12], "float32")
+    SCRATCH["bl%d" % _t] = ("sbuf", [128, 12], "float32")
+for _n, _c in (("pb0", 512), ("pbA", 1024), ("pbR0", 1024), ("pbR1", 1024)):
+    SCRATCH[_n] = ("psum", [128, _c], "float32")
+OWN = ("X", "CL", "sln", "wti", "kpi", "T1", "WK", "BK", "bs", "bl", "Ca", "Cb", "pb", "pbA", "pbR")
+LOGICAL, PLACE, _at = dict(SCRATCH), {}, {}
+for _n, (_w, _s, _d) in list(SCRATCH.items()):
+    if _n.rstrip("0123456789") in OWN or _n in OWN:
+        continue
+    _p = "pool_" + _d
+    _u = 16 if _d in ("float32", "int32") else 32
+    PLACE[_n] = (_p, _at.get(_p, 0))
+    _at[_p] = (_at.get(_p, 0) + _s[1] + _u - 1) // _u * _u
+    del SCRATCH[_n]
+for _p in _at:
+    SCRATCH[_p] = ("sbuf", [128, _at[_p]], _p[5:])
+
+SEMAPHORES = ["eV", "eS", "eP", "eG", "sent", "dsl", "dx", "dz", "dcl", "dcm", "dwt", "dkp", "dyx", "dyl", "dyz", "aC1", "aD2", "aD3", "aD4"]
+SEMAPHORES += ["aB%d" % q for q in range(1, 5)] + ["aW%d" % q for q in range(1, 5)] + ["ab%d" % t for t in range(1, VIS)]
+
+
+def rank_program(g, core, T, topo):
+    rank = T.rank_of(core)
+    if rank is None:
+        return
+    build(g, rank, T, topo)
+
+
+def build(g, rank, T, topo, report=None):
+    ops, wr, rd, bank, early = [], {}, {}, {}, [0.0]
+
+    def B(name, lo=0, hi=None, step=1, p=(0, 128)):
+        if hi is None:
+            hi = LOGICAL[name][1][1]
+        buf, at = PLACE.get(name, (name, 0))
+        x = T[buf][p[0]:p[1], at + lo:at + hi] if step == 1 else T[buf][p[0]:p[1], at + lo:at + hi:step]
+        return (name, lo, hi, x, (hi - lo + step - 1) // step)
+
+    def add(eng, call, outs, ins, cost, sem=None, amt=1, lat=LAT):
+        i, deps = len(ops), {}
+
+        def dep(j, wait):
+            if j != i:
+                deps[j] = deps.get(j, False) or wait
+        for reg, isw in [(r, False) for r in ins] + [(r, True) for r in outs]:
+            name, lo, hi = reg[0], reg[1], reg[2]
+            psum = name[:2] == "pb"
+            for (a, b, j) in wr.get(name, []):
+                if a < hi and lo < b:
+                    dep(j, not (psum and eng == "P" and ops[j]["eng"] == "P"))
+            if isw:
+                for (a, b, j) in rd.get(name, []):
+                    if a < hi and lo < b:
+                        dep(j, True)
+            if psum:
+                for b in range(lo // 512, (hi - 1) // 512 + 1):
+                    e, run, prev = bank.setdefault((name, b), (eng, [], []))
+                    if e != eng:
+                        e, run, prev = bank[(name, b)] = (eng, [], run)
+                    for j in prev:
+                        dep(j, True)
+                    if eng == "P" and run:
+                        dep(run[-1], False)
+                    if i not in run:
+                        run.append(i)
+        for reg in ins:
+            rd.setdefault(reg[0], []).append((reg[1], reg[2], i))
+        for reg in outs:
+            name, lo, hi = reg[0], reg[1], reg[2]
+            if reg[4] == hi - lo:
+                wr[name] = [x for x in wr.get(name, []) if not (lo <= x[0] and x[1] <= hi)]
+                rd[name] = [x for x in rd.get(name, []) if not (lo <= x[0] and x[1] <= hi)]
+            wr.setdefault(name, []).append((lo, hi, i))
+        ops.append({"eng": eng, "call": call, "deps": deps, "cost": cost, "sem": sem, "amt": amt, "lat": lat, "early": early[0]})
+        return i
+
+    def order_after(i, j):
+        ops[i]["deps"].setdefault(j, False)
+
+    def two(*rs):
+        return all(LOGICAL[r[0]][2] in ("bfloat16", "uint16") for r in rs)
+
+    def cyc(n):
+        return 0.02 + max(64, n) * CY
+
+    def cp(o, i):
+        return add("V", lambda: g.vector.tensor_copy(o[3], i[3]), [o], [i], cyc(i[4] * (0.5 if two(o, i) else 1)))
+
+    def tt(o, a, b, op):
+        n = a[4] if (a[0][:2] == "pb" or b[0][:2] == "pb") else 2 * a[4]
+        return add("V", lambda: g.vector.tensor_tensor(o[3], a[3], b[3], op), [o], [a, b], cyc(n))
+
+    def tsc(o, i, s1, s2, op0, op1=None):
+        ins = [i] + [s for s in (s1, s2) if isinstance(s, tuple)]
+        v1 = s1[3] if isinstance(s1, tuple) else s1
+        v2 = s2[3] if isinstance(s2, tuple) else s2
+        if op1 is None:
+            f = lambda: g.vector.tensor_scalar(o[3], i[3], v1, None, op0)
+        else:
+            f = lambda: g.vector.tensor_scalar(o[3], i[3], v1, v2, op0, op1)
+        return add("V", f, [o], ins, cyc(i[4] * (0.5 if two(o, i) else 1)))
+
+    def gtt(o, w, off, b, op):
+        return add("V", lambda: g.vector.tensor_tensor(o[3], w[3].indirect(off[3]), b[3], op), [o], [w, off, b], 0.05 + o[4] * GA * CY)
+
+    def gcp(o, w, off):
+        return add("V", lambda: g.vector.tensor_copy(o[3], w[3].indirect(off[3])), [o], [w, off], 0.05 + o[4] * GA * CY)
+
+    def scat(w, off, i):
+        return add("V", lambda: g.vector.tensor_copy(w[3].indirect(off[3]), i[3]), [(w[0], w[1], w[2], w[3], -1)], [off, i], 0.05 + i[4] * 3 * CY)
+
+    def mem(o, c):
+        return add("V", lambda: g.vector.memset(o[3], c), [o], [], cyc(o[4] * 0.5))
+
+    def act(o, i, f, bias=None, scale=1.0):
+        ins = [i] + [s for s in (bias, scale) if isinstance(s, tuple)]
+        if bias is None:
+            h = lambda: g.scalar.activation(o[3], i[3], f, scale=scale)
+        else:
+            h = lambda: g.scalar.activation(o[3], i[3], f, bias=bias[3], scale=scale)
+        return add("S", h, [o], ins, 0.05 + max(64, i[4]) * CY)
+
+    def gact(o, w, off):
+        return add("S", lambda: g.scalar.activation(o[3], w[3].indirect(off[3]), AF.Copy), [o], [w, off], 0.065 + o[4] * GA * CY)
+
+    def mm(o, l, r, start, stop, f32=False):
+        return add("P", lambda: g.tensor.matmul(o[3], l[3], r[3], start, stop), [o], [l, r], max(64, r[4]) * 0.00042 * (4 if f32 else 1))
+
+    E = lambda r, nm="SL": B(nm, 15 - r, 143 - r)
+
+    def rows(o, nm, src, lo, width, extra=()):
+        for r in range(16):
+            mm(o, E(r, nm), B(src, lo + r, lo + width, 16), r == 0, r == 15 and not extra)
+        for x, (l, r) in enumerate(extra):
+            mm(o, l, r, False, x == len(extra) - 1)
+
+    def dma(q, o, i, sem, us):
+        eng = {"Y": g.sync, "S": g.scalar}[q]
+        return add(q, lambda: eng.dma_start(o[3], i[3]), [o] if o[0] in LOGICAL else [], [i] if i[0] in LOGICAL else [], 0.06, sem=sem, amt=16, lat=us)
+
+    def D(name, lo, hi):
+        return (name, lo, hi, T[name][:, lo:hi] if hi - lo < T[name].shape[1] else T[name][:], hi - lo)
+
+    sent = [0]
+
+    def send(o, i, dst, sem, us):
+        src_core, dst_core = T.cores[rank], T.cores[dst]
+        m, n = topo.mask(src_core, dst_core), len(topo.engines(src_core, dst_core))
+        rid, pid, _se = topo.addr(dst_core)
+        j = add("G", lambda: g.remote_dma(out_ap=o[3], in_ap=i[3], remote_sem=T.sem[sem], local_sem=T.sem.sent, pid=pid, routing_id=rid, dma_engine_mask=m),
+                [], [i], 0.5, sem="-", amt=0)
+        sent[0] += n
+        k = add("R" + sem, None, [o], [], 0.0, sem=sem, amt=n, lat=us)
+        ops[k]["deps"][j] = False
+        return j
+
+    def asel(o, i, pat, cop, fill, base, cmul):
+        return add("G", lambda: g.affine_select(o[3], i[3], pat, cop, fill, base, cmul), [o], [i], 0.17 + 2 * o[4] * CY)
+
+    def iota(o, pat, base, cmul, flag=False):
+        if flag:
+            f = lambda: g.iota(o[3], pat, base, cmul, allow_small_or_imprecise_dtypes=True)
+        else:
+            f = lambda: g.iota(o[3], pat, base, cmul)
+        return add("G", f, [o], [], 0.13 + 2 * o[4] * CY)
+
+    pairs = [0]
+
+    def pair():
+        pairs[0] += 1
+        return "pbR%d" % (pairs[0] % 2)
+
+    def clause_order():
+        order, vs, ss = [], list(range(M0)), list(range(M0, 16))
+        while vs or ss:
+            if ss and (not vs or (16 - M0 - len(ss)) * M0 <= (M0 - len(vs)) * (16 - M0)):
+                order.append(ss.pop(0))
+            else:
+                order.append(vs.pop(0))
+        return order
+
+    dma("Y", B("sln"), D("sl", 0, LA), "dsl", 2.2)
+    dma("S", B("CL", 0, V // 2), D("cl", 0, V // 2), "dcl", 4.0)
+    dma("S", B("CL", V // 2, V), D("cl", V // 2, V), "dcm", 6.0)
+    dma("Y", B("X", 0, W), D("x0", 0, W), "dx", 5.0)
+    dma("Y", B("kpi"), D("kp", 0, 1), "dkp", 2.2)
+    dma("Y", B("wti"), D("wt", 0, 1), "dwt", 2.2)
+    dma("Y", B("Ca", 3 * L, 4 * L), D("z0", 0, LA), "dz", 2.2)
+
+    mem(B("spk", 0, 144), 0.0)
+    mem(B("cmk0"), 0.0)
+    mem(B("cmk1"), 0.0)
+    mem(B("ones"), 1.0)
+    mem(B("spk", 15, 144, 16), 1.0)
+    for a in range(4):
+        mem(B("cmk0", 32 * a, 32 * a + 16), 1.0)
+        mem(B("cmk1", 32 * a + 16, 32 * a + 32), 1.0)
+    mem(B("neg"), -512.0)
+    iota(B("pc"), [[0, 1]], 0, 1)
+    for g2 in range(2):
+        for c2 in range(2):
+            asel(B("PM%d%d" % (g2, c2)), B("cmk%d" % g2), [[-1, 128]], OP.is_equal, 0.0, 16 * (g2 - c2), 1)
+    iota(B("g16"), [[16, 12]], 0, 0)
+    asel(B("BOa"), B("ones"), [[-16, 8], [0, 16]], OP.is_ge, 0.0, 0, 1)
+    asel(B("BO"), B("BOa"), [[16, 8], [0, 16]], OP.is_ge, 0.0, 15, -1)
+    low = (0, 16)
+    asel(B("Q16", 0, 128, 1, low), B("ones", 0, 128, 1, low), [[0, 8], [-1, 16]], OP.is_equal, 0.0, 0, 1)
+    asel(B("I"), B("ones"), [[-1, 128]], OP.is_equal, 0.0, 0, 1)
+    asel(B("SLa"), B("spk"), [[-16, 9], [0, 16]], OP.is_ge, 0.0, 0, 1)
+    asel(B("SL"), B("SLa"), [[16, 9], [0, 16]], OP.is_ge, 0.0, 15, -1)
+    asel(B("Tri"), B("BO"), [[1, 128]], OP.is_ge, 0.0, 0, -1)
+    iota(B("KIL"), [[L, 16], [0, C]], 0, 0, True)
+    mm(B("pbR1", 512, 640), B("Q16", 0, 128, 1, low), B("Q16", 0, 128, 1, low), True, True)
+    cp(B("GR"), B("pbR1", 512, 640))
+    tsc(B("p15"), B("pc"), 15, None, OP.bitwise_and)
+    cp(B("p15f"), B("p15"))
+    tsc(B("kempty"), B("p15f"), -1.0, float(ZB + 16), OP.mult, OP.add)
+    cp(B("sad"), B("sln"))
+    tsc(B("sae"), B("sad"), 0.0, B("kempty"), OP.is_lt, OP.mult)
+    tt(B("T1"), B("sad"), B("sae"), OP.add)
+    add("V", lambda: g.vector.transpose(B("T2")[3], B("T1")[3]), [B("T2")], [B("T1")], cyc(192))
+    for g2 in range(2):
+        for b in range(6):
+            cp(B("T3", g2 * 96 + b, g2 * 96 + 96, 6), B("T2", 32 * b + 16 * g2, 32 * b + 16 * g2 + 16))
+    for c2 in range(2):
+        for g2 in range(2):
+            mm(B("pbR0", c2 * 96, c2 * 96 + 96), B("PM%d%d" % (g2, c2)), B("T3", g2 * 96, g2 * 96 + 96), g2 == 0, g2 == 1, True)
+    for c2 in range(2):
+        cp(B("s", c2, L, 2), B("pbR0", c2 * 96, c2 * 96 + 96))
+    cp(B("s16"), B("s"))
+    mem(B("X", W, W + 16), 0.0)
+    mem(B("Oa", 16 * L, 17 * L), 0.0)
+    mem(B("Ob", 16 * L, 17 * L), 0.0)
+    cp(B("WK0", 0, 1), B("wti"))
+    cp(B("kpf"), B("kpi"))
+    tsc(B("kpd"), B("GR", 0, 16), B("kpf"), None, OP.mult)
+    mm(B("pbR1", 0, 16), B("BO"), B("kpd"), True, True)
+    cp(B("WK0", 1, 17), B("pbR1", 0, 16))
+    cp(B("WK0", 17, 18), B("kpi"))
+    mem(B("WK0", 18, 24), 0.0)
+    send(B("BK1", 0, V // 2), B("CL", 0, V // 2), (rank - 1) % N, "aC1", 9.0)
+    send(B("BK1", V // 2, V), B("CL", V // 2, V), (rank - 1) % N, "aB1", 12.0)
+    for q in range(1, 5):
+        last = send(B("WK%d" % q), B("WK0"), (rank - q) % N, "aW%d" % q, 4.0)
+    order_after(asel(B("R"), B("neg"), [[-1, 16], [-16, 8], [0, 16]], OP.is_equal, 0.0, 0, 1), last)
+
+    def book(q):
+        x = 97 * (q - 1)
+        a = send(B("BK%d" % q, 0, V - x), B("CL", x, V), (rank - q) % N, "aB%d" % q, 14.0)
+        return a, send(B("BK%d" % q, V - x, V), B("CL", 0, x), (rank - q) % N, "aD%d" % q, 14.0)
+
+    book(2)
+    tsc(B("nI"), B("I"), -1.0, None, OP.mult)
+    tsc(B("GRh"), B("GR"), -0.5, None, OP.mult)
+    for nm, v in (("I64", -64.0), ("I3", -3.0 * L), ("I2", -2.0 * L), ("I1", -1.0 * L)):
+        tsc(B(nm), B("I"), v, None, OP.mult)
+    tsc(B("SLL"), B("SL"), L / 2.0, None, OP.mult)
+    tsc(B("SLh"), B("SL"), 0.25, None, OP.mult)
+    mem(B("c8L"), 8.0 * L)
+    mem(B("c8L", C, 3 * C), 0.0)
+    mem(B("p15t"), 0)
+    tsc(B("LI"), B("p15t"), B("p15f"), None, OP.add)
+    tt(B("LI"), B("LI"), B("g16"), OP.add)
+    tsc(B("recb"), B("LI"), 16.0, None, OP.mult)
+    for nm, w in (("TW", 2 * C), ("TK", C)):
+        tsc(B("q12"), B("LI"), 1.0 / w, -0.5 + 0.5 / w, OP.mult, OP.add)
+        tsc(B("e12"), B("q12"), float(-w), None, OP.mult)
+        tt(B("q12"), B("e12"), B("LI"), OP.add)
+        cp(B(nm, 0, 12), B("q12"))
+        if nm == "TW":
+            cp(B(nm, 12, 18), B("q12", 0, 6))
+    for j in range(3):
+        cp(B("LI3f", j * C, (j + 1) * C), B("LI"))
+        cp(B("LI3b", j * C, (j + 1) * C), B("LI"))
+    cp(B("LIb"), B("LI"))
+    mem(B("c3L"), 3.0 * L)
+    tsc(B("thrn"), B("p15f"), float(16 - 2 * SO) - 0.5, -3.0, OP.is_ge, OP.mult)
+    tsc(B("thrn"), B("thrn"), 12.5, None, OP.add)
+    tsc(B("thrc"), B("p15f"), M0 - 0.5, 8.0, OP.is_ge, OP.mult)
+    tsc(B("thrc"), B("thrc"), -7.5, None, OP.add)
+    mem(B("cols"), 0.5)
+    mem(B("B0"), 0.0)
+    for a, b in GRP:
+        w = (b - a) * C
+        for x, m in enumerate(clause_order()):
+            lo = 16 * a * C + x * w
+            act(B("DX", lo, lo + w), B("LI3f", 0, w), AF.Identity, B("GR", m, m + 1), 0.0)
+    tsc(B("SW0"), B("SL"), B("WK0", 0, 1), None, OP.mult)
+    half = B("cols")
+    Ob = lambda t: "Oa" if t % 2 == 0 else "Ob"
+    Cb = lambda t: "Ca" if t % 2 == 0 else "Cb"
+
+    def judge(q):
+        tsc(B("SW%d" % q), B("SL"), B("WK%d" % q, 0, 1), None, OP.mult)
+        tsc(B("DK"), B("DX"), B("WK%d" % q, 17, 18), None, OP.mult)
+        bk = pair()
+        for at, lo, hi in ((128, 0, 384), (512, 384, 576)):
+            mm(B(bk, at, at + hi - lo), B("BO"), B("DK", lo, hi), True, True)
+        act(B("KX%d" % q), B(bk, 128, 704), AF.Copy)
+
+    def gather(t):
+        last = {}
+        for b in range(NB // 2):
+            o, off = B(Ob(t), 768 * b, 768 * b + 768), B("s16", 48 * b, 48 * b + 48)
+            j = gcp(o, B("X"), off) if b in GV[min(t, 1)] else gact(o, B("X"), off)
+            e = ops[j]["eng"]
+            if e in last:
+                order_after(j, last[e])
+            last[e] = j
+
+    def test(t, src, lo, opv, fS, scale, bias):
+        for a in range(2):
+            mm(B("pb0", a * L, (a + 1) * L), B("I"), B(src, lo, lo + L), True, True)
+        vb, sb, ks = list(range(NB - SO)), list(range(NB - SO, NB, 2)), []
+        for x, b in enumerate(vb):
+            tt(B("cmp", 384 * b, 384 * b + 384), B(Ob(t), 384 * b, 384 * b + 384), B("pb0", 0, 384), opv)
+            ks += [2 * b, 2 * b + 1]
+            if x % 2 == 1 and x // 2 < len(sb):
+                b = sb[x // 2]
+                bk = pair()
+                for y in range(2):
+                    at = 128 + 384 * y
+                    mm(B(bk, at, at + 384), B("I"), B(Ob(t), 384 * (b + y), 384 * (b + y) + 384), True, False)
+                    for a in range(2):
+                        mm(B(bk, at + a * L, at + (a + 1) * L), B("nI"), B(src, lo, lo + L), False, a == 1)
+                act(B("cmp", 384 * b, 384 * b + 768), B(bk, 128, 896), fS, bias, scale)
+                ks += range(2 * b, 2 * b + 4)
+        cnt = B("pbA", 0, L)
+        for x, k in enumerate(ks):
+            mm(cnt, E(k), B("cmp", k * L, (k + 1) * L), x == 0, x == 15)
+        return cnt
+
+    def opened(t):
+        cnt = test(t, Cb(t), 3 * L, OP.is_gt, AF.Relu, 1.0, None)
+        act(B("op"), cnt, AF.Sign)
+        pr, pv = B("pbA", 800, 800 + L), B("pb0", 0, L)
+        mm(pr, B("Tri"), B("op"), True, True)
+        mm(pv, B("Tri"), B("op"), True, True)
+        act(B("le", 0, L), pr, AF.Sign, half, -1.0)
+        for j in (1, 2):
+            tsc(B("le", j * L, (j + 1) * L), pv, j + 0.5, 2.0, OP.is_le, OP.mult)
+
+    def small(u):
+        n = (GRP[u][1] - GRP[u][0]) * C
+        return B("pb0", 384, 384 + n) if u == 0 else B("pbA", 704, 704 + n)
+
+    def cands(t, u):
+        zc = Cb(t)
+        a, b = GRP[u]
+        sl = lambda n: B(n, a * C, b * C)
+        o = small(u)
+        rows(o, "SLL", "le", a * L, (b - a) * L, ((B("I"), sl("LI3b")), (B("I"), sl("c8L"))))
+        cp(sl("off"), o)
+        for j in range(a, b):
+            gtt(B(zc, j * L, (j + 1) * L), B(Ob(t), 0, 17 * L), B("off", j * C, (j + 1) * C), B(zc, 3 * L, 4 * L), OP.min)
+        tt(sl("kL"), o, sl("LI3f"), OP.subtract)
+        tsc(sl("pen"), sl("kL"), 15.0 * L, A[t] / 2.0 - 4 - 15.0 * L, OP.max, OP.add)
+        o = small(u)
+        rows(o, "SW%d" % (t + 1), zc, a * L, (b - a) * L)
+        cp(sl("ui"), o)
+        tsc(sl("um"), sl("ui"), V - 1, None, OP.bitwise_and)
+        tt(sl("sq"), sl("um"), sl("um"), OP.mult)
+        tsc(sl("ba"), sl("sq"), 5, None, OP.arith_shift_right)
+
+    def empties(t):
+        fe = lambda a: B("fe", a * C, (a + 1) * C)
+        m = lambda a, b: B("mx", a * C, b * C)
+        tt(m(0, 8), B("s", 0, 8 * C), B("s", 8 * C, 16 * C), OP.max)
+        tt(m(8, 12), m(0, 4), m(4, 8), OP.max)
+        tt(m(12, 14), m(8, 10), m(10, 12), OP.max)
+        tt(m(14, 15), m(12, 13), m(13, 14), OP.max)
+        tsc(fe(0), m(14, 15), float(ZB), None, OP.is_ge)
+        tsc(fe(1), m(14, 15), -1.0 * L, float(L * (ZB + 15 - t)), OP.mult, OP.add)
+        tt(fe(2), fe(0), fe(1), OP.mult)
+        tsc(fe(3), fe(2), float(L * t), None, OP.add)
+
+    def clauses(t, u):
+        q, cand, order = t + 1, Cb(t), clause_order()
+        a, b = GRP[u]
+        w, n = (b - a) * C, (b - a) * L
+        cnt = B("pbA", 512 * u, 512 * u + n)
+        last = None
+        for c0, c1 in CHUNKS[u]:
+            lo, hi = 16 * a * C + c0 * w, 16 * a * C + c1 * w
+            r = lambda nm: B(nm, lo, hi)
+            tw = B("TW" if b - a == 2 else "TK", 0, (c1 - c0) * w // 16)
+            j = gtt(r("KU"), B("um", a * C, b * C), tw, r("KX%d" % q), OP.mult)
+            if last is not None:
+                order_after(j, last)
+            gtt(r("Hs"), B("ba", a * C, b * C), tw, r("KU"), OP.add)
+            tsc(r("Hm"), r("Hs"), V - 1, None, OP.bitwise_and)
+            last = cp(r("ho"), r("Hm"))
+        sg = 0
+        for x, m in enumerate(order):
+            off = B("ho", 16 * a * C + x * w, 16 * a * C + (x + 1) * w)
+            gm = B("G", m * 3 * L + a * L, m * 3 * L + b * L)
+            if m < M0:
+                gtt(gm, B("BK%d" % q), off, B(cand, a * L, b * L), OP.is_le)
+            else:
+                s0 = (sg % 8) * 384
+                sg += 1
+                gact(B("SG", s0, s0 + n), B("BK%d" % q), off)
+                pairs[0] += 1
+                bk, at = "pbR%d" % (pairs[0] % 2), 512 * (pairs[0] // 2 % 2)
+                mm(B(bk, at, at + n), B("I"), B("SG", s0, s0 + n), True, False)
+                mm(B(bk, at, at + n), B("nI"), B(cand, a * L, b * L), False, True)
+                act(gm, B(bk, at, at + n), AF.Sign, half, -1.0)
+            mm(cnt, E(m), gm, x == 0, x == 15)
+        act(B("ge", a * L, b * L), cnt, AF.Sign, B("thrc"))
+        if u == 0 and t < VIS - 1:
+            judge(q + 1)
+        rows(small(u), "SLh", "ge", a * L, n)
+
+    def trials(t, u):
+        nj = lambda j: B("nb", 2 * j * C, (2 * j + 1) * C)
+        a, b = GRP[u]
+        cn = small(u)
+        x = 0
+        if u == 0:
+            thr, x = B("cd", 0, C), C
+            tt(thr, B("pen", 0, C), B("B0") if t == 0 else B("bl%d" % t), OP.add)
+            tt(nj(0), B(cn[0], cn[1], cn[1] + C), thr, OP.is_ge)
+        tt(B("cm", a * C + x, b * C), B(cn[0], cn[1] + x, cn[2]), B("pen", a * C + x, b * C), OP.subtract)
+        pn, pd = B("pb0", 432, 432 + C), B("pb0", 448, 448 + C)
+        for j in range(a, b):
+            if j:
+                qn, d = B("bt", (j - 1) * C, j * C), B("cd", C, 2 * C)
+                tsc(qn, pn, 0.25, None, OP.add)
+                tt(d, B("cm", j * C, (j + 1) * C), pd, OP.add)
+                tt(nj(j), d, qn, OP.is_ge)
+            if j < 2 or t < VIS - 1:
+                mm(pn, B("GRh"), nj(j), True, True)
+            if j < 2:
+                mm(pd, B("GRh"), nj(j), True, False)
+                for i in range(j + 1):
+                    mm(pd, B("I64"), nj(i), False, i == j)
+        if b < 3:
+            return
+        bo = B("pb0", 464, 464 + C)
+        mm(bo, B("I"), B("LIb"), True, False)
+        mm(bo, B("I"), B("c3L"), False, False)
+        for j in range(3):
+            mm(bo, B("I%d" % (3 - j)), nj(j), False, j == 2)
+        x = cp(B("bo"), bo)
+        if t < VIS - 1:
+            pi, pj = B("bt", 2 * C, 3 * C), B("ci", 6 * C, 7 * C)
+            order_after(tsc(pi, pn, -2.0, None, OP.mult), x)
+            tsc(pj, pi, 1, None, OP.bitwise_and)
+            tsc(B("bs%d" % (t + 1)), pj, 0.5, None, OP.mult)
+        gact(B("M"), B(Cb(t), 0, 4 * L), B("bo"))
+
+    def visit_bits(t):
+        k = send(B("bl%d" % (t + 1)), B("bs%d" % (t + 1)), (rank - 1) % N, "ab%d" % (t + 1), 4.0)
+        if t < 2:
+            for b in book(t + 3):
+                order_after(b, k)
+
+    def post(t):
+        nb = lambda j, a, b: B("nb", (2 * j + a) * C, (2 * j + b) * C)
+        um = B("pbA", 992, 992 + C)
+        rows(um, "SW0", "M", 0, L)
+        ni = lambda a: B("ni", a * C, (a + 1) * C)
+        cp(ni(0), um)
+        tsc(ni(1), ni(0), 15, None, OP.bitwise_and)
+        tt(B("nf"), ni(1), B("recb"), OP.add)
+        cp(B("n16"), B("nf"))
+        scat(B("X"), B("n16"), B("M"))
+        for j in range(3):
+            tt(nb(j, 1, 2), nb(j, 0, 1), B("kL", j * C, (j + 1) * C), OP.mult)
+        for j in range(3):
+            mm(B("pb0", 480, 480 + 2 * C), B("I"), nb(j, 0, 2), j == 0, j == 2)
+        pu = lambda a: B("pu", a * C, (a + 1) * C)
+        fe = B("fe", 3 * C, 4 * C)
+        tt(pu(0), B("pb0", 480, 480 + C), fe, OP.mult)
+        tt(pu(1), B("pb0", 480 + C, 480 + 2 * C), pu(0), OP.subtract)
+        tt(pu(2), pu(1), fe, OP.add)
+        gtt(B("eq"), pu(2), B("TK"), B("KIL"), OP.is_equal)
+        gtt(B("dd"), B("nf"), B("TK"), B("s"), OP.subtract)
+        tt(B("ed"), B("eq"), B("dd"), OP.mult)
+        tt(B("s"), B("s"), B("ed"), OP.add)
+        if t < VIS - 1:
+            cp(B("s16"), B("s"))
+
+    def near(t):
+        cnt = test(t, "M", 0, OP.is_le, AF.Sign, -1.0, half)
+        act(B("nn"), cnt, AF.Relu, B("thrn"), -1.0)
+        for b in range(0, NB, 2):
+            bk = pair()
+            for x in range(2):
+                at = 128 + 384 * x
+                mm(B(bk, at, at + 384), B("I"), B(Ob(t), 384 * (b + x), 384 * (b + x) + 384), True, False)
+                for a in range(2):
+                    k = 2 * (b + x) + a
+                    mm(B(bk, at + a * L, at + (a + 1) * L), B("R", 128 * k, 128 * k + 128), B("nn"), False, a == 1)
+            if b == 0:
+                act(B("acc"), B(bk, 128, 896), AF.Relu)
+            else:
+                tt(B("acc"), B(bk, 128, 896), B("acc"), OP.max)
+        tt(B("fo"), B("acc", 0, 384), B("acc", 384, 768), OP.max)
+        tt(B("cc"), B("fo", 0, L), B("fo", L, 2 * L), OP.max)
+        tt(B("cc"), B("cc"), B("M"), OP.max)
+        uc = B("pbA", 1008, 1008 + C)
+        rows(uc, "SW0", "cc", 0, L)
+        ci = lambda a: B("ci", a * C, (a + 1) * C)
+        cp(ci(0), uc)
+        tsc(ci(1), ci(0), V - 1, None, OP.bitwise_and)
+        tt(ci(2), ci(1), ci(1), OP.mult)
+        tsc(ci(3), ci(1), B("WK0", 1, 2), 97.0 * t, OP.mult, OP.add)
+        tsc(ci(4), ci(2), 5, None, OP.arith_shift_right)
+        tt(ci(5), ci(3), ci(4), OP.add)
+        tsc(ci(0), ci(5), V - 1, None, OP.bitwise_and)
+        cp(B("ch"), ci(0))
+        gtt(B("df"), B("CL"), B("ch"), B("cc"), OP.subtract)
+        act(B(Cb(t + 1), 3 * L, 4 * L), B("df"), AF.Abs)
+
+    gather(0)
+    judge(1)
+    for t in range(VIS):
+        opened(t)
+        cands(t, 0)
+        cands(t, 1)
+        empties(t)
+        for u in range(2):
+            clauses(t, u)
+            trials(t, u)
+        if t < VIS - 1:
+            visit_bits(t)
+        early[0] = LEAD
+        post(t)
+        early[0] = 0.0
+        near(t)
+        if t < VIS - 1:
+            gather(t + 1)
+
+    dma("Y", D("yx", 0, W), B("X", 0, W), "dyx", 5.0)
+    for c2 in range(2):
+        cp(B("T3", c2 * 96, c2 * 96 + 96), B("s", c2, L, 2))
+    for g2 in range(2):
+        for c2 in range(2):
+            mm(B("pbR0", g2 * 96, g2 * 96 + 96), B("PM%d%d" % (c2, g2)), B("T3", c2 * 96, c2 * 96 + 96), c2 == 0, c2 == 1, True)
+    for g2 in range(2):
+        for b in range(6):
+            cp(B("T4", 32 * b + 16 * g2, 32 * b + 16 * g2 + 16), B("pbR0", g2 * 96 + b, g2 * 96 + 96, 6))
+    add("V", lambda: g.vector.transpose(B("T5")[3], B("T4")[3]), [B("T5")], [B("T4")], cyc(192))
+    tsc(B("T6"), B("T5"), float(ZB), B("kempty"), OP.is_ge, OP.mult)
+    tt(B("T1"), B("T5"), B("T6"), OP.subtract)
+    dma("Y", D("yl", 0, LA), B("T1"), "dyl", 2.2)
+    dma("Y", D("yz", 0, LA), B(Cb(VIS), 3 * L, 4 * L), "dyz", 2.2)
+
+    order = schedule(ops)
+    emit(g, T, ops, order, sent[0])
+    if report is not None:
+        report.append((ops, order))
+
+
+def schedule(ops):
+    n = len(ops)
+    succ, left, tail = [[] for _ in range(n)], [0] * n, [0.0] * n
+    for i, o in enumerate(ops):
+        left[i] = len(o["deps"])
+        for j in o["deps"]:
+            succ[j].append(i)
+    for i in range(n - 1, -1, -1):
+        tail[i] = ops[i]["cost"] + ops[i]["lat"] + max([tail[s] for s in succ[i]] + [0.0])
+    for i in range(n):
+        tail[i] += ops[i]["early"]
+    free, est = {}, [0.0] * n
+    ready, order = [i for i in range(n) if left[i] == 0], []
+    while ready:
+        st = [(max(free.get(ops[i]["eng"], 0.0), est[i]), i) for i in ready]
+        t0 = min(st)[0]
+        i = -max((tail[i], -i) for s, i in st if s <= t0 + TOL)[1]
+        o = ops[i]
+        s = max(free.get(o["eng"], 0.0), est[i])
+        o["start"], o["end"] = s, s + o["cost"]
+        free[o["eng"]] = o["end"]
+        order.append(i)
+        ready.remove(i)
+        for k in succ[i]:
+            wait = ops[k]["eng"] != o["eng"] or ops[k]["deps"][i]
+            est[k] = max(est[k], o["end"] + (o["lat"] if wait else 0.0))
+            left[k] -= 1
+            if left[k] == 0:
+                ready.append(k)
+    return order
+
+
+def emit(g, T, ops, order, nsent):
+    queue = {"V": g.vector, "S": g.scalar, "P": g.tensor, "G": g, "Y": g.sync}
+    need = set()
+    for o in ops:
+        for j, w in o["deps"].items():
+            if w:
+                need.add(j)
+    total, mark, know, snap = {}, {}, {}, {}
+    for i in order:
+        o = ops[i]
+        e = o["eng"]
+        if e[0] == "R":
+            total[o["sem"]] = o["amt"]
+            mark[i] = (o["sem"], o["amt"])
+            snap[i] = {}
+            continue
+        k = know.setdefault(e, {})
+        want = {}
+        for j, w in o["deps"].items():
+            if w:
+                s, v = mark[j]
+                if k.get(s, 0) < v and want.get(s, (0, 0))[0] < v:
+                    want[s] = (v, j)
+        for s in list(want):
+            if any(s2 != s and snap[want[s2][1]].get(s, 0) >= want[s][0] for s2 in want):
+                del want[s]
+        for s, (v, j) in want.items():
+            queue[e].wait_ge(T.sem[s], v)
+            k[s] = max(k.get(s, 0), v)
+            for s2, v2 in snap[j].items():
+                k[s2] = max(k.get(s2, 0), v2)
+        ins = o["call"]()
+        if o["sem"] == "-":
+            continue
+        if o["sem"] is not None:
+            ins.then_inc(T.sem[o["sem"]], o["amt"])
+            total[o["sem"]] = o["amt"]
+            mark[i] = (o["sem"], o["amt"])
+        elif i in need:
+            s = "e" + e
+            ins.then_inc(T.sem[s], 1)
+            total[s] = total.get(s, 0) + 1
+            mark[i] = (s, total[s])
+        else:
+            continue
+        snap[i] = dict(k)
+    for s, v in total.items():
+        if know.get("G", {}).get(s, 0) < v:
+            g.wait_ge(T.sem[s], v)
+    g.wait_ge(T.sem.sent, nsent)

@@ -1,46 +1,49 @@
+from concourse.bass import DstId, RemoteDMATransfer
 from concourse.mybir import AluOpType as OP, ActivationFunctionType as AF
 
 N, LA, W, V, VIS = 8, 192, 3072, 4096, 4
 A = [6, 4, 4, 3]
 ZB = 3072
-L, C, W3 = 192, 12, 36
-NB = 8
-SO = 4
-M0 = 10
-GRP = ((0, 2), (2, 3))
-CHUNKS = (((0, 4), (4, 16)), ((0, 16),))
-GV = ((0, 2), ())
-TOL, LEAD, LAT = 0.02, 5.0, 0.15
+H, C = 96, 6
+BW = 4 * H
+PAR = {"so": [2, 2], "sn": [3, 3], "m0": [10, 10], "gv": [0, 0], "gv0": [2, 2], "th": "S", "mg": "S", "chunks": 2, "lat": 0.12, "nr": 6, "xat": 1, "passes": 3,
+       "b": {"ga": [0, 0], "ca": [0, 0], "cl": [-5, -10], "tr": [5, 5], "po": [0, 5], "ne": [0, 0]}}
 CY, GA = 0.00083, 1.5
+PLAN = []
+CORES = [3, 11, 19, 27, 35, 43, 51, 59]
+CUT = V // 2
+PIECES = ((CUT, 3 * V // 4), (3 * V // 4, V), (0, V // 4), (V // 4, CUT))
 
 SCRATCH = {}
+_two = lambda l: tuple((n + str(h), c) for n, c in l for h in range(2))
 for _t, _l in (
-        ("bfloat16", (("X", W + 16), ("CL", V), ("ones", 128), ("neg", 2048), ("R", 2048), ("SLh", 144), ("c8L", W3), ("I", 128), ("nI", 128),
-                      ("I64", 128), ("I3", 128), ("I2", 128), ("I1", 128), ("spk", 144), ("SLa", 144), ("SL", 144), ("SLL", 144), ("BOa", 128), ("BO", 128),
-                      ("Tri", 128), ("Q16", 128), ("GR", 128), ("GRh", 128), ("LI3b", W3), ("LIb", C), ("c3L", C), ("kpd", 16), ("DX", 576), ("DK", 576),
-                      ("Oa", 17 * L), ("Ob", 17 * L), ("Ca", 4 * L), ("Cb", 4 * L), ("cmp", 16 * L), ("op", L), ("le", 3 * L), ("G", 48 * L), ("SG", 16 * L),
-                      ("ge", 3 * L), ("nb", 6 * C), ("M", L), ("nn", L), ("acc", 768), ("fo", 384), ("cc", L), ("df", L))),
-        ("float32", (("cmk0", 128), ("cmk1", 128), ("PM00", 128), ("PM01", 128), ("PM10", 128), ("PM11", 128), ("p15f", 1), ("kempty", 1), ("thrn", 1),
-                     ("thrc", 1), ("cols", 1), ("recb", 12), ("LI3f", W3), ("KIL", L), ("sad", LA), ("sae", LA), ("T1", LA), ("T2", LA), ("T3", LA), ("T4", LA),
-                     ("T5", LA), ("T6", LA), ("kpf", 1), ("WK0", 24), ("B0", 12), ("kL", W3), ("pen", W3), ("KU", 576), ("cm", W3), ("cd", 2 * C), ("s", L),
-                     ("eq", L), ("dd", L), ("ed", L), ("mx", 15 * C), ("fe", 4 * C), ("pu", 3 * C), ("nf", C))),
-        ("int32", (("pc", 1), ("p15", 1), ("g16", 12), ("p15t", 12), ("LI", 12), ("e12", 12), ("q12", 12), ("sln", LA), ("wti", 1), ("kpi", 1),
-                   ("ui", W3), ("um", W3), ("sq", W3), ("ba", W3), ("Hs", 576), ("Hm", 576), ("bt", 3 * C), ("ci", 8 * C), ("ni", 2 * C))),
-        ("uint16", (("TW", 18), ("TK", 12), ("off", W3), ("ho", 576), ("bo", C), ("ch", C), ("s16", L), ("n16", C)))):
+        ("bfloat16", (("X", W + 16), ("CL", V), ("zl", LA), ("zo", LA), ("dfl", LA), ("d", 144), ("ch", 128), ("cl16", 128), ("neg", 2048), ("R", 2048), ("I", 128), ("nI", 128),
+                      ("I64", 128), ("I3", 128), ("I2", 128), ("I1", 128), ("SL", 144), ("SLL", 144), ("SLh", 144), ("BO", 128), ("GR", 128), ("PA", 128),
+                      ("Tg", 128), ("Tr0", 128), ("Tr1", 128), ("Tr2", 128), ("Tri", 128), ("LI3b", 3 * C), ("c8", 3 * C), ("c3", C), ("one", C), ("kpd", 16), ("DX", 48 * C), ("DK", 48 * C))
+         + _two((("Oa", 17 * H), ("Ob", 17 * H), ("Ca", 4 * H), ("Cb", 4 * H), ("cmp", 16 * H), ("op", H), ("le", 3 * H), ("G", 48 * H), ("SG", 12 * H),
+                 ("ge", 3 * H), ("nb", 3 * C), ("th", 3 * C), ("K4", 4 * C), ("pr", 8 * C), ("M", H), ("nn", H), ("acc", 2 * H), ("cc", H), ("df", H), ("eq", H), ("recb", C)))),
+        ("float32", (("PM00", 128), ("PM01", 128), ("PM10", 128), ("PM11", 128), ("pf", 8), ("pg", 16), ("c16", 3 * C), ("LI3f", 3 * C), ("KIL", H),
+                     ("sae", LA), ("T1", LA), ("T2", LA), ("T3", LA), ("T4", LA), ("T5", LA), ("T6", LA), ("T7", LA), ("s", LA), ("mx", 17 * 12), ("lf", 24))
+         + _two((("KU", 48 * C), ("cm", 2 * C), ("put", 2 * C), ("dd", H), ("ed", H), ("hf", 2 * C)))),
+        ("int32", (("pc", 4), ("sln", LA), ("li", 36))
+         + _two((("ui", 3 * C), ("um", 3 * C), ("sq", 3 * C), ("ba", 3 * C), ("Hs", 48 * C), ("Hm", 48 * C), ("ci", 4 * C), ("ni", 8 * C)))),
+        ("uint16", (("TW", 3 * C), ("TK", C), ("TL", C), ("TM", 3 * C), ("Tin", 12), ("Tout", 12), ("Tz", 12))
+         + _two((("Tzi", C), ("off", 3 * C), ("ho", 48 * C), ("bo", C), ("hc", C), ("s16", H), ("n16", C))))):
     for _n, _c in _l:
         SCRATCH[_n] = ("sbuf", [128, _c], _t)
 for _q in range(1, 5):
     SCRATCH["BK%d" % _q] = ("sbuf", [128, V], "bfloat16")
-    SCRATCH["WK%d" % _q] = ("sbuf", [128, 24], "float32")
+    SCRATCH["KX%d" % _q] = ("sbuf", [128, 48 * C], "float32")
 for _q in range(5):
+    SCRATCH["WK%d" % _q] = ("sbuf", [128, 4], "int32")
     SCRATCH["SW%d" % _q] = ("sbuf", [128, 144], "bfloat16")
-    SCRATCH["KX%d" % _q] = ("sbuf", [128, 576], "float32")
 for _t in range(1, VIS):
-    SCRATCH["bs%d" % _t] = ("sbuf", [128, 12], "float32")
-    SCRATCH["bl%d" % _t] = ("sbuf", [128, 12], "float32")
-for _n, _c in (("pb0", 512), ("pbA", 1024), ("pbR0", 1024), ("pbR1", 1024)):
-    SCRATCH[_n] = ("psum", [128, _c], "float32")
-OWN = ("X", "CL", "sln", "wti", "kpi", "T1", "WK", "BK", "bs", "bl", "Ca", "Cb", "pb", "pbA", "pbR")
+    for _h in range(2):
+        SCRATCH["bs%d%d" % (_t, _h)] = ("sbuf", [128, 8], "float32")
+        SCRATCH["bl%d%d" % (_t, _h)] = ("sbuf", [128, 8], "float32")
+for _n in ["pc0", "pc1"] + ["pr%d" % _b for _b in range(6)]:
+    SCRATCH["P" + _n] = ("psum", [128, 512], "float32")
+OWN = ("X", "CL", "zl", "zo", "sln", "wti", "kpi", "T7", "WK", "BK", "bs", "bl", "Ppc", "Ppr")
 LOGICAL, PLACE, _at = dict(SCRATCH), {}, {}
 for _n, (_w, _s, _d) in list(SCRATCH.items()):
     if _n.rstrip("0123456789") in OWN or _n in OWN:
@@ -53,36 +56,73 @@ for _n, (_w, _s, _d) in list(SCRATCH.items()):
 for _p in _at:
     SCRATCH[_p] = ("sbuf", [128, _at[_p]], _p[5:])
 
-SEMAPHORES = ["eV", "eS", "eP", "eG", "sent", "dsl", "dx", "dz", "dcl", "dcm", "dwt", "dkp", "dyx", "dyl", "dyz", "aC1", "aD2", "aD3", "aD4"]
-SEMAPHORES += ["aB%d" % q for q in range(1, 5)] + ["aW%d" % q for q in range(1, 5)] + ["ab%d" % t for t in range(1, VIS)]
+SEMAPHORES = ["eV", "eS", "eP", "eG", "sent", "dsl", "dx", "dz", "dwt", "dkp", "dyx", "dyl", "dyz"]
+SEMAPHORES += ["dc%d" % a for a in range(4)] + ["aC%d" % a for a in range(4)] + ["aH%d%d" % (q, a) for q in range(1, 5) for a in range(4)]
+SEMAPHORES += ["aB%d" % q for q in range(2, 5)] + ["aW%d" % q for q in range(1, 5)] + ["ab%d%d" % (t, h) for t in range(1, VIS) for h in range(2)]
+
+
+def helper(topo, core):
+    mate = [c for c in CORES if topo.mates(topo.chip(core), topo.chip(c))][0]
+    return [c for c in topo.cores_of(core) if topo.die(c) != topo.die(core) and topo.may_write(c, mate)][0]
 
 
 def rank_program(g, core, T, topo):
     rank = T.rank_of(core)
-    if rank is None:
-        return
-    build(g, rank, T, topo)
+    if rank is not None:
+        return build(g, rank, T, topo)
+    for rank, home in enumerate(T.cores):
+        if helper(topo, home) == core and CUT < V:
+            hand_on(g, rank, core, T, topo)
+
+
+def hand_on(g, rank, core, T, topo):
+    home, sent = T.cores[rank], 0
+    far = topo.engines(home, T.cores[(rank - 1) % N])
+    n = len([x for x in topo.engines(home, core) if x not in far])
+    for q in range(1, 5):
+        dst = T.cores[(rank - q) % N]
+        rid, pid, _se = topo.addr(dst)
+        for a, (lo, hi) in enumerate(PIECES):
+            if lo >= CUT:
+                if q == 1:
+                    g.wait_ge(T.sem["aC%d" % a], n)
+                g.remote_dma(out_ap=T["BK%d" % q][:, lo:hi], in_ap=T.CL[:, lo:hi], remote_sem=T.sem["aH%d%d" % (q, a)], local_sem=T.sem.sent, pid=pid, routing_id=rid,
+                             dma_engine_mask=topo.mask(core, dst))
+                sent += len(topo.engines(core, dst))
+    g.wait_ge(T.sem.sent, sent)
 
 
 def build(g, rank, T, topo, report=None):
-    ops, wr, rd, bank, early = [], {}, {}, {}, [0.0]
+    ops, wr, rd, bank, leases, chains, bias = [], {}, {}, {}, {}, {}, [0.0]
+    LAT = PAR["lat"]
+
+    def view(buf, p, a, b, step):
+        return T[buf][p[0]:p[1], a:b] if step == 1 else T[buf][p[0]:p[1], a:b:step]
 
     def B(name, lo=0, hi=None, step=1, p=(0, 128)):
+        if name in leases:
+            r = [name, lo, hi, None, (hi - lo + step - 1) // step]
+            leases[name]["regs"].append((r, p, step))
+            return r
         if hi is None:
             hi = LOGICAL[name][1][1]
         buf, at = PLACE.get(name, (name, 0))
-        x = T[buf][p[0]:p[1], at + lo:at + hi] if step == 1 else T[buf][p[0]:p[1], at + lo:at + hi:step]
-        return (name, lo, hi, x, (hi - lo + step - 1) // step)
+        return [name, lo, hi, view(buf, p, at + lo, at + hi, step), (hi - lo + step - 1) // step]
 
-    def add(eng, call, outs, ins, cost, sem=None, amt=1, lat=LAT):
-        i, deps = len(ops), {}
+    def lease():
+        name = "P#%d" % len(leases)
+        leases[name] = {"regs": [], "ops": []}
+        return name
+
+    def add(eng, call, outs, ins, cost, sem=None, amt=1, lat=None, after=()):
+        i, deps, mine = len(ops), {}, None
 
         def dep(j, wait):
             if j != i:
                 deps[j] = deps.get(j, False) or wait
         for reg, isw in [(r, False) for r in ins] + [(r, True) for r in outs]:
             name, lo, hi = reg[0], reg[1], reg[2]
-            psum = name[:2] == "pb"
+            psum = name[0] == "P" and name[1] in "p#"
             for (a, b, j) in wr.get(name, []):
                 if a < hi and lo < b:
                     dep(j, not (psum and eng == "P" and ops[j]["eng"] == "P"))
@@ -91,16 +131,20 @@ def build(g, rank, T, topo, report=None):
                     if a < hi and lo < b:
                         dep(j, True)
             if psum:
-                for b in range(lo // 512, (hi - 1) // 512 + 1):
-                    e, run, prev = bank.setdefault((name, b), (eng, [], []))
-                    if e != eng:
-                        e, run, prev = bank[(name, b)] = (eng, [], run)
-                    for j in prev:
-                        dep(j, True)
-                    if eng == "P" and run:
-                        dep(run[-1], False)
-                    if i not in run:
-                        run.append(i)
+                e, run, prev = bank.setdefault(name, (eng, [], []))
+                if e != eng:
+                    e, run, prev = bank[name] = (eng, [], run)
+                for j in prev:
+                    dep(j, True)
+                if eng == "P" and run:
+                    dep(run[-1], False)
+                if i not in run:
+                    run.append(i)
+                if name in leases and i not in leases[name]["ops"]:
+                    leases[name]["ops"].append(i)
+                    mine = name
+        for j in after:
+            dep(j, False)
         for reg in ins:
             rd.setdefault(reg[0], []).append((reg[1], reg[2], i))
         for reg in outs:
@@ -109,77 +153,89 @@ def build(g, rank, T, topo, report=None):
                 wr[name] = [x for x in wr.get(name, []) if not (lo <= x[0] and x[1] <= hi)]
                 rd[name] = [x for x in rd.get(name, []) if not (lo <= x[0] and x[1] <= hi)]
             wr.setdefault(name, []).append((lo, hi, i))
-        ops.append({"eng": eng, "call": call, "deps": deps, "cost": cost, "sem": sem, "amt": amt, "lat": lat, "early": early[0]})
+        ops.append({"eng": eng, "call": call, "deps": deps, "cost": cost, "sem": sem, "amt": amt, "lat": LAT if lat is None else lat, "lease": mine, "bias": bias[0],
+                    "lab": (outs or ins)[0][0]})
         return i
 
     def order_after(i, j):
         ops[i]["deps"].setdefault(j, False)
 
+    def chain(name, i):
+        if name in chains:
+            order_after(i, chains[name])
+        chains[name] = i
+        return i
+
     def two(*rs):
-        return all(LOGICAL[r[0]][2] in ("bfloat16", "uint16") for r in rs)
+        return all(r[0] in LOGICAL and LOGICAL[r[0]][2] in ("bfloat16", "uint16") for r in rs)
+
+    def psum(r):
+        return r[0] not in LOGICAL or LOGICAL[r[0]][0] == "psum"
 
     def cyc(n):
         return 0.02 + max(64, n) * CY
+
+    val = lambda s: s[3] if isinstance(s, list) else s
 
     def cp(o, i):
         return add("V", lambda: g.vector.tensor_copy(o[3], i[3]), [o], [i], cyc(i[4] * (0.5 if two(o, i) else 1)))
 
     def tt(o, a, b, op):
-        n = a[4] if (a[0][:2] == "pb" or b[0][:2] == "pb") else 2 * a[4]
-        return add("V", lambda: g.vector.tensor_tensor(o[3], a[3], b[3], op), [o], [a, b], cyc(n))
+        return add("V", lambda: g.vector.tensor_tensor(o[3], a[3], b[3], op), [o], [a, b], cyc(a[4] if psum(a) or psum(b) else 2 * a[4]))
 
     def tsc(o, i, s1, s2, op0, op1=None):
-        ins = [i] + [s for s in (s1, s2) if isinstance(s, tuple)]
-        v1 = s1[3] if isinstance(s1, tuple) else s1
-        v2 = s2[3] if isinstance(s2, tuple) else s2
+        ins = [i] + [s for s in (s1, s2) if isinstance(s, list)]
         if op1 is None:
-            f = lambda: g.vector.tensor_scalar(o[3], i[3], v1, None, op0)
+            f = lambda: g.vector.tensor_scalar(o[3], i[3], val(s1), None, op0)
         else:
-            f = lambda: g.vector.tensor_scalar(o[3], i[3], v1, v2, op0, op1)
+            f = lambda: g.vector.tensor_scalar(o[3], i[3], val(s1), val(s2), op0, op1)
         return add("V", f, [o], ins, cyc(i[4] * (0.5 if two(o, i) else 1)))
 
     def gtt(o, w, off, b, op):
         return add("V", lambda: g.vector.tensor_tensor(o[3], w[3].indirect(off[3]), b[3], op), [o], [w, off, b], 0.05 + o[4] * GA * CY)
 
-    def gcp(o, w, off):
-        return add("V", lambda: g.vector.tensor_copy(o[3], w[3].indirect(off[3])), [o], [w, off], 0.05 + o[4] * GA * CY)
-
     def scat(w, off, i):
-        return add("V", lambda: g.vector.tensor_copy(w[3].indirect(off[3]), i[3]), [(w[0], w[1], w[2], w[3], -1)], [off, i], 0.05 + i[4] * 3 * CY)
+        return add("V", lambda: g.vector.tensor_copy(w[3].indirect(off[3]), i[3]), [[w[0], w[1], w[2], w[3], -1]], [off, i], 0.05 + i[4] * 3 * CY)
 
     def mem(o, c):
         return add("V", lambda: g.vector.memset(o[3], c), [o], [], cyc(o[4] * 0.5))
 
-    def act(o, i, f, bias=None, scale=1.0):
-        ins = [i] + [s for s in (bias, scale) if isinstance(s, tuple)]
-        if bias is None:
-            h = lambda: g.scalar.activation(o[3], i[3], f, scale=scale)
-        else:
-            h = lambda: g.scalar.activation(o[3], i[3], f, bias=bias[3], scale=scale)
-        return add("S", h, [o], ins, 0.05 + max(64, i[4]) * CY)
+    def vtr(o, i):
+        return add("V", lambda: g.vector.transpose(o[3], i[3]), [o], [i], cyc(i[4]))
 
-    def gact(o, w, off):
-        return add("S", lambda: g.scalar.activation(o[3], w[3].indirect(off[3]), AF.Copy), [o], [w, off], 0.065 + o[4] * GA * CY)
+    def act(o, i, f, bias=0.0, scale=1.0):
+        ins = [i] + [s for s in (bias, scale) if isinstance(s, list)]
+        return add("S", lambda: g.scalar.activation(o[3], i[3], f, bias=val(bias), scale=val(scale)), [o], ins, 0.05 + max(64, i[4]) * CY)
 
-    def mm(o, l, r, start, stop, f32=False):
-        return add("P", lambda: g.tensor.matmul(o[3], l[3], r[3], start, stop), [o], [l, r], max(64, r[4]) * 0.00042 * (4 if f32 else 1))
+    def gat(e, o, w, off, f=AF.Copy):
+        if e == "V":
+            return add("V", lambda: g.vector.tensor_copy(o[3], w[3].indirect(off[3])), [o], [w, off], 0.05 + o[4] * GA * CY)
+        return add("S", lambda: g.scalar.activation(o[3], w[3].indirect(off[3]), f), [o], [w, off], 0.065 + o[4] * GA * CY)
+
+    def mm(o, l, r, start, stop, f32=False, after=()):
+        return add("P", lambda: g.tensor.matmul(o[3], l[3], r[3], start, stop), [o], [l, r], max(64, r[4]) * 0.00042 * (4 if f32 else 1), after=after)
+
+    def mms(o, terms):
+        for x, (l, r) in enumerate(terms):
+            mm(o, l, r, x == 0, x == len(terms) - 1)
 
     E = lambda r, nm="SL": B(nm, 15 - r, 143 - r)
 
     def rows(o, nm, src, lo, width, extra=()):
-        for r in range(16):
-            mm(o, E(r, nm), B(src, lo + r, lo + width, 16), r == 0, r == 15 and not extra)
-        for x, (l, r) in enumerate(extra):
-            mm(o, l, r, False, x == len(extra) - 1)
+        mms(o, [(E(r, nm), B(src, lo + r, lo + width, 16)) for r in range(16)] + list(extra))
 
     def dma(q, o, i, sem, us):
         eng = {"Y": g.sync, "S": g.scalar}[q]
-        return add(q, lambda: eng.dma_start(o[3], i[3]), [o] if o[0] in LOGICAL else [], [i] if i[0] in LOGICAL else [], 0.06, sem=sem, amt=16, lat=us)
+        return chain("d" + q, add(q, lambda: eng.dma_start(o[3], i[3]), [o] if o[0] in LOGICAL else [], [i], 0.06, sem=sem, amt=16, lat=us))
 
     def D(name, lo, hi):
-        return (name, lo, hi, T[name][:, lo:hi] if hi - lo < T[name].shape[1] else T[name][:], hi - lo)
+        return [name, lo, hi, T[name][:, lo:hi] if hi - lo < T[name].shape[1] else T[name][:], hi - lo]
 
     sent = [0]
+
+    def landed(j, o, sem, n, us):
+        sent[0] += n
+        add("R" + sem, None, [o], [], 0.0, sem=sem, amt=n, lat=us, after=(j,))
 
     def send(o, i, dst, sem, us):
         src_core, dst_core = T.cores[rank], T.cores[dst]
@@ -187,440 +243,493 @@ def build(g, rank, T, topo, report=None):
         rid, pid, _se = topo.addr(dst_core)
         j = add("G", lambda: g.remote_dma(out_ap=o[3], in_ap=i[3], remote_sem=T.sem[sem], local_sem=T.sem.sent, pid=pid, routing_id=rid, dma_engine_mask=m),
                 [], [i], 0.5, sem="-", amt=0)
-        sent[0] += n
-        k = add("R" + sem, None, [o], [], 0.0, sem=sem, amt=n, lat=us)
-        ops[k]["deps"][j] = False
+        landed(j, o, sem, n, us)
+        return j
+
+    me = T.cores[rank]
+
+    def hand(i, a):
+        far = topo.engines(me, T.cores[(rank - 1) % N])
+        es = [x for x in topo.engines(me, helper(topo, me)) if x not in far]
+        rid, pid, _se = topo.addr(helper(topo, me))
+        sent[0] += len(es)
+        return add("G", lambda: g.remote_dma(out_ap=i[3], in_ap=i[3], remote_sem=T.sem["aC%d" % a], local_sem=T.sem.sent, pid=pid, routing_id=rid,
+                                             dma_engine_mask=sum(1 << x for x in es)), [], [i], 0.5, sem="-", amt=0)
+
+    def send_each(i, jobs, us):
+        tr, cnt = [], []
+        for x, (o, dst, sem) in enumerate(jobs):
+            es = topo.engines(T.cores[rank], T.cores[dst])
+            k = len(es) // len(jobs)
+            rid, pid, _se = topo.addr(T.cores[dst])
+            tr.append(RemoteDMATransfer(dst_ids=[DstId(rid=rid, pnc=pid)], dma_engine_mask=sum(1 << e for e in es[x * k:x * k + k]), remote_sem=T.sem[sem], src=i[3], dst=o[3]))
+            cnt.append(k)
+        j = add("G", lambda: g.remote_dma_fused(tr, local_sem=T.sem.sent), [], [i], 0.7, sem="-", amt=0)
+        for (o, dst, sem), k in zip(jobs, cnt):
+            landed(j, o, sem, k, us)
         return j
 
     def asel(o, i, pat, cop, fill, base, cmul):
         return add("G", lambda: g.affine_select(o[3], i[3], pat, cop, fill, base, cmul), [o], [i], 0.17 + 2 * o[4] * CY)
 
-    def iota(o, pat, base, cmul, flag=False):
-        if flag:
-            f = lambda: g.iota(o[3], pat, base, cmul, allow_small_or_imprecise_dtypes=True)
-        else:
+    def iota(o, pat, base, cmul):
+        if LOGICAL[o[0]][2] == "int32":
             f = lambda: g.iota(o[3], pat, base, cmul)
+        else:
+            f = lambda: g.iota(o[3], pat, base, cmul, allow_small_or_imprecise_dtypes=True)
         return add("G", f, [o], [], 0.13 + 2 * o[4] * CY)
 
-    pairs = [0]
+    M0, SO, SN = PAR["m0"], PAR["so"], PAR["sn"]
 
-    def pair():
-        pairs[0] += 1
-        return "pbR%d" % (pairs[0] % 2)
+    dma("Y", B("sln"), D("sl", 0, LA), "dsl", 2.0)
+    dma("S", B("WK0", 1, 2), D("kp", 0, 1), "dkp", 2.0)
+    dma("S", B("WK0", 0, 1), D("wt", 0, 1), "dwt", 2.0)
+    for a, (lo, hi) in enumerate(PIECES):
+        if a == PAR["xat"]:
+            dma("Y", B("X", 0, W), D("x0", 0, W), "dx", 4.5)
+            dma("Y", B("zl"), D("z0", 0, LA), "dz", 4.5)
+        dma("Y", B("CL", lo, hi), D("cl", lo, hi), "dc%d" % a, 3.0 + a + (3.0 if a >= PAR["xat"] else 0.0))
 
-    def clause_order():
-        order, vs, ss = [], list(range(M0)), list(range(M0, 16))
-        while vs or ss:
-            if ss and (not vs or (16 - M0 - len(ss)) * M0 <= (M0 - len(vs)) * (16 - M0)):
-                order.append(ss.pop(0))
-            else:
-                order.append(vs.pop(0))
-        return order
-
-    dma("Y", B("sln"), D("sl", 0, LA), "dsl", 2.2)
-    dma("S", B("CL", 0, V // 2), D("cl", 0, V // 2), "dcl", 4.0)
-    dma("S", B("CL", V // 2, V), D("cl", V // 2, V), "dcm", 6.0)
-    dma("Y", B("X", 0, W), D("x0", 0, W), "dx", 5.0)
-    dma("Y", B("kpi"), D("kp", 0, 1), "dkp", 2.2)
-    dma("Y", B("wti"), D("wt", 0, 1), "dwt", 2.2)
-    dma("Y", B("Ca", 3 * L, 4 * L), D("z0", 0, LA), "dz", 2.2)
-
-    mem(B("spk", 0, 144), 0.0)
-    mem(B("cmk0"), 0.0)
-    mem(B("cmk1"), 0.0)
-    mem(B("ones"), 1.0)
-    mem(B("spk", 15, 144, 16), 1.0)
-    for a in range(4):
-        mem(B("cmk0", 32 * a, 32 * a + 16), 1.0)
-        mem(B("cmk1", 32 * a + 16, 32 * a + 32), 1.0)
-    mem(B("neg"), -512.0)
-    iota(B("pc"), [[0, 1]], 0, 1)
+    iota(B("pc", 0, 1), [[0, 1]], 0, 1)
+    iota(B("d"), [[1, 144]], 0, -1)
+    iota(B("c16"), [[16, 3 * C]], 0, 0)
+    iota(B("cl16"), [[0, 8], [1, 16]], 0, 0)
+    iota(B("ch"), [[1, 8], [0, 16]], 0, 0)
+    pc, pf, pg = (lambda a: B("pc", a, a + 1)), (lambda a: B("pf", a, a + 1)), (lambda a: B("pg", a, a + 1))
+    tsc(pc(1), pc(0), 15, None, OP.bitwise_and)
+    tsc(pc(2), pc(0), 4, None, OP.arith_shift_right)
+    tsc(pc(3), pc(0), 4, 1, OP.arith_shift_right, OP.bitwise_and)
+    cp(B("pf", 0, 4), B("pc", 0, 4))
+    row, grp, odd = pf(1), pf(2), pf(3)
+    even, kempty, half, r15, gth, sgn, r6, r16 = [pg(a) for a in range(8)]
+    thn, thrc = (pg(10), pg(11)), (pg(12), pg(13))
+    tsc(even, odd, -1.0, 1.0, OP.mult, OP.add)
+    tsc(kempty, row, -1.0, float(ZB + 16), OP.mult, OP.add)
     for g2 in range(2):
         for c2 in range(2):
-            asel(B("PM%d%d" % (g2, c2)), B("cmk%d" % g2), [[-1, 128]], OP.is_equal, 0.0, 16 * (g2 - c2), 1)
-    iota(B("g16"), [[16, 12]], 0, 0)
-    asel(B("BOa"), B("ones"), [[-16, 8], [0, 16]], OP.is_ge, 0.0, 0, 1)
-    asel(B("BO"), B("BOa"), [[16, 8], [0, 16]], OP.is_ge, 0.0, 15, -1)
-    low = (0, 16)
-    asel(B("Q16", 0, 128, 1, low), B("ones", 0, 128, 1, low), [[0, 8], [-1, 16]], OP.is_equal, 0.0, 0, 1)
-    asel(B("I"), B("ones"), [[-1, 128]], OP.is_equal, 0.0, 0, 1)
-    asel(B("SLa"), B("spk"), [[-16, 9], [0, 16]], OP.is_ge, 0.0, 0, 1)
-    asel(B("SL"), B("SLa"), [[16, 9], [0, 16]], OP.is_ge, 0.0, 15, -1)
-    asel(B("Tri"), B("BO"), [[1, 128]], OP.is_ge, 0.0, 0, -1)
-    iota(B("KIL"), [[L, 16], [0, C]], 0, 0, True)
-    mm(B("pbR1", 512, 640), B("Q16", 0, 128, 1, low), B("Q16", 0, 128, 1, low), True, True)
-    cp(B("GR"), B("pbR1", 512, 640))
-    tsc(B("p15"), B("pc"), 15, None, OP.bitwise_and)
-    cp(B("p15f"), B("p15"))
-    tsc(B("kempty"), B("p15f"), -1.0, float(ZB + 16), OP.mult, OP.add)
-    cp(B("sad"), B("sln"))
-    tsc(B("sae"), B("sad"), 0.0, B("kempty"), OP.is_lt, OP.mult)
-    tt(B("T1"), B("sad"), B("sae"), OP.add)
-    add("V", lambda: g.vector.transpose(B("T2")[3], B("T1")[3]), [B("T2")], [B("T1")], cyc(192))
-    for g2 in range(2):
-        for b in range(6):
-            cp(B("T3", g2 * 96 + b, g2 * 96 + 96, 6), B("T2", 32 * b + 16 * g2, 32 * b + 16 * g2 + 16))
-    for c2 in range(2):
+            tsc(B("PM%d%d" % (g2, c2)), B("d", 0, 128), 16.0 * (g2 - c2), (even, odd)[c2], OP.is_equal, OP.mult)
+
+    tsc(B("LI3f", 0, 3 * C), B("c16"), row, None, OP.add)
+    e = lambda w: B("LI3f", 0, w)
+
+    def quot(o, w, k):
+        tsc(o, e(w), 1.0 / k, -0.5 + 0.5 / k, OP.mult, OP.add)
+
+    def mixed(name, w, k, a, b):
+        quot(B("li", 18, 18 + w), w, k)
+        tsc(B("lf", 0, w), B("li", 18, 18 + w), float(b) / a, None, OP.mult)
+        tt(B("lf", 0, w), B("lf", 0, w), e(w), OP.add)
+        tsc(B(name, 0, w), B("lf", 0, w), float(a), None, OP.mult)
+    mixed("Tin", 12, 6, 32, -191)
+    for h in range(2):
+        tsc(r16, row, 16.0 * h, None, OP.add)
+        tsc(B("Tzi%d" % h), B("c16", 0, C), 2.0, r16, OP.mult, OP.add)
+        tsc(B("recb%d" % h), B("Tzi%d" % h), 16.0, None, OP.mult)
+    mixed("TW", 3 * C, 3 * C, 1, -3 * C)
+    mixed("TK", C, C, 1, -C)
+    tsc(B("TL"), B("TK"), float(C), None, OP.add)
+    for j in (1, 2):
+        cp(B("LI3f", j * C, (j + 1) * C), B("LI3f", 0, C))
+    cp(B("LI3b"), B("LI3f"))
+    tsc(B("sae"), B("sln"), 0.0, kempty, OP.is_lt, OP.mult)
+    tt(B("T1"), B("sln"), B("sae"), OP.add)
+    vtr(B("T2"), B("T1"))
+    gat("V", B("T3"), B("T2"), B("Tin"))
+    for h in range(2):
+        bk = lease()
         for g2 in range(2):
-            mm(B("pbR0", c2 * 96, c2 * 96 + 96), B("PM%d%d" % (g2, c2)), B("T3", g2 * 96, g2 * 96 + 96), g2 == 0, g2 == 1, True)
-    for c2 in range(2):
-        cp(B("s", c2, L, 2), B("pbR0", c2 * 96, c2 * 96 + 96))
-    cp(B("s16"), B("s"))
+            mm(B(bk, 0, H), B("PM%d%d" % (g2, h)), B("T3", g2 * H, g2 * H + H), g2 == 0, g2 == 1, True)
+        cp(B("s16%d" % h), B(bk, 0, H))
+        cp(B("s", h, LA, 2), B(bk, 0, H))
+        gat("S", B("Ca%d" % h, 3 * H, 4 * H), B("zl"), B("Tzi%d" % h))
+        for nm in ("Oa%d", "Ob%d"):
+            mem(B(nm % h, 16 * H, 17 * H), -1.0)
     mem(B("X", W, W + 16), 0.0)
-    mem(B("Oa", 16 * L, 17 * L), 0.0)
-    mem(B("Ob", 16 * L, 17 * L), 0.0)
-    cp(B("WK0", 0, 1), B("wti"))
-    cp(B("kpf"), B("kpi"))
-    tsc(B("kpd"), B("GR", 0, 16), B("kpf"), None, OP.mult)
-    mm(B("pbR1", 0, 16), B("BO"), B("kpd"), True, True)
-    cp(B("WK0", 1, 17), B("pbR1", 0, 16))
-    cp(B("WK0", 17, 18), B("kpi"))
-    mem(B("WK0", 18, 24), 0.0)
-    send(B("BK1", 0, V // 2), B("CL", 0, V // 2), (rank - 1) % N, "aC1", 9.0)
-    send(B("BK1", V // 2, V), B("CL", V // 2, V), (rank - 1) % N, "aB1", 12.0)
-    for q in range(1, 5):
-        last = send(B("WK%d" % q), B("WK0"), (rank - q) % N, "aW%d" % q, 4.0)
+    tsc(B("I"), B("d", 0, 128), 0.0, None, OP.is_equal)
+    tsc(r15, row, -1.0, 15.0, OP.mult, OP.add)
+    tsc(B("SL"), B("d"), r15, None, OP.is_equal)
+    tsc(B("BO"), B("ch"), grp, None, OP.is_equal)
+    tsc(B("GR"), B("cl16"), row, None, OP.is_equal)
+    tsc(B("Tg"), B("d", 0, 128), 0.0, None, OP.is_ge)
+    tt(B("Tri"), B("Tg"), B("BO"), OP.mult)
+    for j in range(3):
+        act(B("Tr%d" % j), B("Tri"), AF.Identity, 0.0, 1.0 / (j + 0.5))
+    for nm, v in (("nI", -1.0), ("I64", 64.0), ("I3", -3.0 * H), ("I2", -2.0 * H), ("I1", -1.0 * H)):
+        act(B(nm), B("I"), AF.Identity, 0.0, v)
+    act(B("SLL"), B("SL"), AF.Identity, 0.0, H / 2.0)
+    act(B("SLh"), B("SL"), AF.Identity, 0.0, 0.5)
+    mem(B("c8"), 8.0 * H)
+    mem(B("c3"), 3.0 * H)
+    mem(B("one"), 1.0)
+    mem(half, 0.5)
+    mem(B("neg"), -512.0)
+    for h in range(2):
+        tsc(thn[h], row, 16 - 4 * SN[h] - 0.5, -3.0, OP.is_ge, OP.mult)
+        tsc(thrc[h], row, M0[h] - 0.5, 8.0, OP.is_ge, OP.mult)
+    tsc(B("pg", 10, 12), B("pg", 10, 12), 12.5, None, OP.add)
+    tsc(B("pg", 12, 14), B("pg", 12, 14), -7.5, None, OP.add)
+    w_th = 0.5 if PAR["th"] == "S" else 1.0
+    tsc(gth, grp, 0.5, -1.0 if PAR["th"] == "S" else 1.0, OP.add, OP.mult)
+    tsc(sgn, odd, -2.0 * w_th, w_th, OP.mult, OP.add)
+    tsc(B("PA"), B("GR"), sgn, None, OP.mult)
+    cp(B("pf", 4, 6), B("WK0", 0, 2))
+    tsc(B("kpd", 0, 1), B("GR", 0, 1), pf(5), 32.0, OP.mult, OP.mult)
+    bk = lease()
+    mm(B(bk, 0, 1), B("BO"), B("kpd", 0, 1), True, True)
+    cp(pf(6), B(bk, 0, 1))
+    tsc(B("SW0"), B("SL"), pf(4), None, OP.mult)
+    chain("G", send_each(B("WK0", 0, 2), [(B("WK%d" % q, 0, 2), (rank - q) % N, "aW%d" % q) for q in range(1, 5)], 7.0))
+    for a, (lo, hi) in enumerate(PIECES):
+        if lo >= CUT:
+            last = chain("G", hand(B("CL", lo, hi), a))
+            for q in range(1, 5):
+                add("RaH%d%d" % (q, a), None, [B("BK%d" % q, lo, hi)], [], 0.0, sem="aH%d%d" % (q, a), amt=len(topo.engines(helper(topo, me), T.cores[(rank + q) % N])),
+                    lat=5.0 * q + 3, after=(last,))
+        else:
+            last = chain("G", send(B("BK1", lo, hi), B("CL", lo, hi), (rank - 1) % N, "aC%d" % a, 4.0))
+    iota(B("DX"), [[1, 16], [0, 3 * C]], 0, 0)
+    tsc(B("DX"), B("DX"), row, None, OP.is_equal)
     order_after(asel(B("R"), B("neg"), [[-1, 16], [-16, 8], [0, 16]], OP.is_equal, 0.0, 0, 1), last)
+    order_after(iota(B("KIL"), [[H, 16], [0, C]], 0, 0), last)
+    order_after(iota(B("li", 0, 12), [[1, C], [H, 2]], 0, 0), last)
+    tsc(r6, row, 6.0, None, OP.mult)
+    tsc(B("Tout"), B("li", 0, 12), r6, None, OP.add)
+    order_after(iota(B("li", 12, 24), [[16, C], [H, 2]], 0, 0), last)
+    tsc(B("Tz"), B("li", 12, 24), row, None, OP.add)
 
     def book(q):
-        x = 97 * (q - 1)
-        a = send(B("BK%d" % q, 0, V - x), B("CL", x, V), (rank - q) % N, "aB%d" % q, 14.0)
-        return a, send(B("BK%d" % q, V - x, V), B("CL", 0, x), (rank - q) % N, "aD%d" % q, 14.0)
+        return send(B("BK%d" % q, 0, CUT), B("CL", 0, CUT), (rank - q) % N, "aB%d" % q, 14.0)
+    order_after(book(2), last)
 
-    book(2)
-    tsc(B("nI"), B("I"), -1.0, None, OP.mult)
-    tsc(B("GRh"), B("GR"), -0.5, None, OP.mult)
-    for nm, v in (("I64", -64.0), ("I3", -3.0 * L), ("I2", -2.0 * L), ("I1", -1.0 * L)):
-        tsc(B(nm), B("I"), v, None, OP.mult)
-    tsc(B("SLL"), B("SL"), L / 2.0, None, OP.mult)
-    tsc(B("SLh"), B("SL"), 0.25, None, OP.mult)
-    mem(B("c8L"), 8.0 * L)
-    mem(B("c8L", C, 3 * C), 0.0)
-    mem(B("p15t"), 0)
-    tsc(B("LI"), B("p15t"), B("p15f"), None, OP.add)
-    tt(B("LI"), B("LI"), B("g16"), OP.add)
-    tsc(B("recb"), B("LI"), 16.0, None, OP.mult)
-    for nm, w in (("TW", 2 * C), ("TK", C)):
-        tsc(B("q12"), B("LI"), 1.0 / w, -0.5 + 0.5 / w, OP.mult, OP.add)
-        tsc(B("e12"), B("q12"), float(-w), None, OP.mult)
-        tt(B("q12"), B("e12"), B("LI"), OP.add)
-        cp(B(nm, 0, 12), B("q12"))
-        if nm == "TW":
-            cp(B(nm, 12, 18), B("q12", 0, 6))
-    for j in range(3):
-        cp(B("LI3f", j * C, (j + 1) * C), B("LI"))
-        cp(B("LI3b", j * C, (j + 1) * C), B("LI"))
-    cp(B("LIb"), B("LI"))
-    mem(B("c3L"), 3.0 * L)
-    tsc(B("thrn"), B("p15f"), float(16 - 2 * SO) - 0.5, -3.0, OP.is_ge, OP.mult)
-    tsc(B("thrn"), B("thrn"), 12.5, None, OP.add)
-    tsc(B("thrc"), B("p15f"), M0 - 0.5, 8.0, OP.is_ge, OP.mult)
-    tsc(B("thrc"), B("thrc"), -7.5, None, OP.add)
-    mem(B("cols"), 0.5)
-    mem(B("B0"), 0.0)
-    for a, b in GRP:
-        w = (b - a) * C
-        for x, m in enumerate(clause_order()):
-            lo = 16 * a * C + x * w
-            act(B("DX", lo, lo + w), B("LI3f", 0, w), AF.Identity, B("GR", m, m + 1), 0.0)
-    tsc(B("SW0"), B("SL"), B("WK0", 0, 1), None, OP.mult)
-    half = B("cols")
-    Ob = lambda t: "Oa" if t % 2 == 0 else "Ob"
-    Cb = lambda t: "Ca" if t % 2 == 0 else "Cb"
+    Ob = lambda t, h: "O" + "ab"[t % 2] + str(h)
+    Cb = lambda t, h: "C" + "ab"[t % 2] + str(h)
+    hb = lambda h: (lambda n, *a: B(n + str(h), *a))
 
     def judge(q):
-        tsc(B("SW%d" % q), B("SL"), B("WK%d" % q, 0, 1), None, OP.mult)
-        tsc(B("DK"), B("DX"), B("WK%d" % q, 17, 18), None, OP.mult)
-        bk = pair()
-        for at, lo, hi in ((128, 0, 384), (512, 384, 576)):
-            mm(B(bk, at, at + hi - lo), B("BO"), B("DK", lo, hi), True, True)
-        act(B("KX%d" % q), B(bk, 128, 704), AF.Copy)
+        cp(B("pg", 14, 16), B("WK%d" % q, 0, 2))
+        tsc(B("SW%d" % q), B("SL"), pg(14), None, OP.mult)
+        tsc(B("DK"), B("DX"), pg(15), None, OP.mult)
+        o = B(lease(), 0, 48 * C)
+        mm(o, B("BO"), B("DK"), True, True)
+        act(B("KX%d" % q), o, AF.Copy)
 
-    def gather(t):
-        last = {}
-        for b in range(NB // 2):
-            o, off = B(Ob(t), 768 * b, 768 * b + 768), B("s16", 48 * b, 48 * b + 48)
-            j = gcp(o, B("X"), off) if b in GV[min(t, 1)] else gact(o, B("X"), off)
-            e = ops[j]["eng"]
-            if e in last:
-                order_after(j, last[e])
-            last[e] = j
+    def gather(t, h):
+        nv, js = PAR["gv0" if t == 0 else "gv"][h], []
+        for b in range(4):
+            js.append(gat("V" if b < nv else "S", B(Ob(t, h), BW * b, BW * b + BW), B("X"), B("s16%d" % h, 24 * b, 24 * b + 24)))
+        return js
 
-    def test(t, src, lo, opv, fS, scale, bias):
-        for a in range(2):
-            mm(B("pb0", a * L, (a + 1) * L), B("I"), B(src, lo, lo + L), True, True)
-        vb, sb, ks = list(range(NB - SO)), list(range(NB - SO, NB, 2)), []
-        for x, b in enumerate(vb):
-            tt(B("cmp", 384 * b, 384 * b + 384), B(Ob(t), 384 * b, 384 * b + 384), B("pb0", 0, 384), opv)
-            ks += [2 * b, 2 * b + 1]
-            if x % 2 == 1 and x // 2 < len(sb):
-                b = sb[x // 2]
-                bk = pair()
-                for y in range(2):
-                    at = 128 + 384 * y
-                    mm(B(bk, at, at + 384), B("I"), B(Ob(t), 384 * (b + y), 384 * (b + y) + 384), True, False)
-                    for a in range(2):
-                        mm(B(bk, at + a * L, at + (a + 1) * L), B("nI"), B(src, lo, lo + L), False, a == 1)
-                act(B("cmp", 384 * b, 384 * b + 768), B(bk, 128, 896), fS, bias, scale)
-                ks += range(2 * b, 2 * b + 4)
-        cnt = B("pbA", 0, L)
-        for x, k in enumerate(ks):
-            mm(cnt, E(k), B("cmp", k * L, (k + 1) * L), x == 0, x == 15)
-        return cnt
+    def test(t, h, rec, ns, opv, fS, scale, bias, cnt, after=()):
+        O = Ob(t, h)
+        if ns < 4:
+            rep = lease()
+            for a in range(4):
+                mm(B(rep, a * H, (a + 1) * H), B("I"), rec, True, True, after=after)
+        order = []
+        for x in range(4):
+            order += [b for b in (x if x < 4 - ns else None, 4 - ns + x if x < ns else None) if b is not None]
+        for x, b in enumerate(order):
+            o = B("cmp%d" % h, BW * b, BW * b + BW)
+            if b < 4 - ns:
+                tt(o, B(O, BW * b, BW * b + BW), B(rep, 0, BW), opv)
+            else:
+                bk = lease()
+                mm(B(bk, 0, BW), B("I"), B(O, BW * b, BW * b + BW), True, False, after=[j for lo, hi, j in wr[rec[0]] if lo < rec[2] and rec[1] < hi])
+                for a in range(4):
+                    mm(B(bk, a * H, (a + 1) * H), B("nI"), rec, False, a == 3)
+                act(o, B(bk, 0, BW), fS, bias, scale)
+            for k in range(4 * b, 4 * b + 4):
+                mm(cnt, E(k), B("cmp%d" % h, k * H, (k + 1) * H), x == 0 and k == 4 * b, x == 3 and k == 4 * b + 3)
 
-    def opened(t):
-        cnt = test(t, Cb(t), 3 * L, OP.is_gt, AF.Relu, 1.0, None)
-        act(B("op"), cnt, AF.Sign)
-        pr, pv = B("pbA", 800, 800 + L), B("pb0", 0, L)
-        mm(pr, B("Tri"), B("op"), True, True)
-        mm(pv, B("Tri"), B("op"), True, True)
-        act(B("le", 0, L), pr, AF.Sign, half, -1.0)
-        for j in (1, 2):
-            tsc(B("le", j * L, (j + 1) * L), pv, j + 0.5, 2.0, OP.is_le, OP.mult)
-
-    def small(u):
-        n = (GRP[u][1] - GRP[u][0]) * C
-        return B("pb0", 384, 384 + n) if u == 0 else B("pbA", 704, 704 + n)
-
-    def cands(t, u):
-        zc = Cb(t)
-        a, b = GRP[u]
-        sl = lambda n: B(n, a * C, b * C)
-        o = small(u)
-        rows(o, "SLL", "le", a * L, (b - a) * L, ((B("I"), sl("LI3b")), (B("I"), sl("c8L"))))
-        cp(sl("off"), o)
-        for j in range(a, b):
-            gtt(B(zc, j * L, (j + 1) * L), B(Ob(t), 0, 17 * L), B("off", j * C, (j + 1) * C), B(zc, 3 * L, 4 * L), OP.min)
-        tt(sl("kL"), o, sl("LI3f"), OP.subtract)
-        tsc(sl("pen"), sl("kL"), 15.0 * L, A[t] / 2.0 - 4 - 15.0 * L, OP.max, OP.add)
-        o = small(u)
-        rows(o, "SW%d" % (t + 1), zc, a * L, (b - a) * L)
-        cp(sl("ui"), o)
-        tsc(sl("um"), sl("ui"), V - 1, None, OP.bitwise_and)
-        tt(sl("sq"), sl("um"), sl("um"), OP.mult)
-        tsc(sl("ba"), sl("sq"), 5, None, OP.arith_shift_right)
+    def cands(t, h, gathered):
+        b, zc = hb(h), Cb(t, h)
+        z = B(zc, 3 * H, 4 * H)
+        cnt = B("Ppc%d" % h, 320, 320 + H)
+        test(t, h, z, SO[h], OP.is_gt, AF.Relu, 1.0, 0.0, cnt, gathered[:1])
+        act(b("op"), cnt, AF.Sign)
+        bk = lease()
+        for j in range(3):
+            mm(B(bk, j * H, (j + 1) * H), B("Tr%d" % j), b("op"), True, True)
+        act(b("le"), B(bk, 0, 3 * H), AF.Sign, 1.0, -1.0)
+        o = B(lease(), 0, 3 * C)
+        rows(o, "SLL", "le%d" % h, 0, 3 * H, ((B("I"), B("LI3b")), (B("I"), B("c8"))))
+        cp(b("off"), o)
+        tt(b("K4", 0, 3 * C), o, B("LI3f"), OP.subtract)
+        for j in range(3):
+            gtt(B(zc, j * H, (j + 1) * H), B(Ob(t, h)), b("off", j * C, (j + 1) * C), z, OP.min)
+        o = B(lease(), 0, 3 * C)
+        rows(o, "SW%d" % (t + 1), zc, 0, 3 * H)
+        cp(b("ui"), o)
+        tsc(b("um"), b("ui"), V - 1, None, OP.bitwise_and)
+        tt(b("sq"), b("um"), b("um"), OP.mult)
+        tsc(b("ba"), b("sq"), 1.0 / 32, 97.0 * t - 0.375, OP.mult, OP.add)
+        bias[0] = PAR["b"]["cl"][h]
+        o = B(lease(), 0, 4 * C)
+        rows(o, "SW0", zc, 0, 4 * H)
+        cp(b("ni", 0, 4 * C), o)
+        tsc(b("ni", 4 * C, 8 * C), b("ni", 0, 4 * C), 15, None, OP.bitwise_and)
+        bias[0] = PAR["b"]["ca"][h]
 
     def empties(t):
-        fe = lambda a: B("fe", a * C, (a + 1) * C)
-        m = lambda a, b: B("mx", a * C, b * C)
-        tt(m(0, 8), B("s", 0, 8 * C), B("s", 8 * C, 16 * C), OP.max)
+        m = lambda a, b: B("mx", a * 12, b * 12)
+        tt(m(0, 8), B("s", 0, 96), B("s", 96, 192), OP.max)
         tt(m(8, 12), m(0, 4), m(4, 8), OP.max)
         tt(m(12, 14), m(8, 10), m(10, 12), OP.max)
         tt(m(14, 15), m(12, 13), m(13, 14), OP.max)
-        tsc(fe(0), m(14, 15), float(ZB), None, OP.is_ge)
-        tsc(fe(1), m(14, 15), -1.0 * L, float(L * (ZB + 15 - t)), OP.mult, OP.add)
-        tt(fe(2), fe(0), fe(1), OP.mult)
-        tsc(fe(3), fe(2), float(L * t), None, OP.add)
+        tsc(m(15, 16), m(14, 15), float(ZB), float(ZB + 15 - t), OP.is_lt, OP.mult)
+        tt(m(16, 17), m(14, 15), m(15, 16), OP.max)
+        for h in range(2):
+            act(B("K4%d" % h, 3 * C, 4 * C), B("mx", 192 + h, 204, 2), AF.Identity, float(H * (ZB + 15)), -1.0 * H)
 
-    def clauses(t, u):
-        q, cand, order = t + 1, Cb(t), clause_order()
-        a, b = GRP[u]
-        w, n = (b - a) * C, (b - a) * L
-        cnt = B("pbA", 512 * u, 512 * u + n)
-        last = None
-        for c0, c1 in CHUNKS[u]:
-            lo, hi = 16 * a * C + c0 * w, 16 * a * C + c1 * w
-            r = lambda nm: B(nm, lo, hi)
-            tw = B("TW" if b - a == 2 else "TK", 0, (c1 - c0) * w // 16)
-            j = gtt(r("KU"), B("um", a * C, b * C), tw, r("KX%d" % q), OP.mult)
+    def clauses(t, h):
+        b, q, cand, w, n = hb(h), t + 1, B(Cb(t, h), 0, 3 * H), 3 * C, 3 * H
+        cnt = B("Ppc%d" % h, 0, n)
+        last, nc = None, PAR["chunks"]
+        for c in range(nc):
+            r = lambda nm: B(nm, 16 * w * c // nc, 16 * w * (c + 1) // nc)
+            tw = B("TW", 0, w // nc)
+            j = gtt(r("KU%d" % h), b("um"), tw, r("KX%d" % q), OP.mult)
             if last is not None:
                 order_after(j, last)
-            gtt(r("Hs"), B("ba", a * C, b * C), tw, r("KU"), OP.add)
-            tsc(r("Hm"), r("Hs"), V - 1, None, OP.bitwise_and)
-            last = cp(r("ho"), r("Hm"))
-        sg = 0
-        for x, m in enumerate(order):
-            off = B("ho", 16 * a * C + x * w, 16 * a * C + (x + 1) * w)
-            gm = B("G", m * 3 * L + a * L, m * 3 * L + b * L)
-            if m < M0:
-                gtt(gm, B("BK%d" % q), off, B(cand, a * L, b * L), OP.is_le)
+            gtt(r("Hs%d" % h), b("ba"), tw, r("KU%d" % h), OP.add)
+            tsc(r("Hm%d" % h), r("Hs%d" % h), V - 1, None, OP.bitwise_and)
+            last = cp(r("ho%d" % h), r("Hm%d" % h))
+        nv, ns, m0 = 0, 0, M0[h]
+        bias[0] = PAR["b"]["cl"][h]
+        for m in range(16):
+            off, gm = b("ho", m * w, (m + 1) * w), b("G", m * n, (m + 1) * n)
+            if (16 - m) * (16 - m0) // 16 == (15 - m) * (16 - m0) // 16:
+                chain("cV", gtt(gm, B("BK%d" % q), off, cand, OP.is_le))
+                at, nv = nv, nv + 1
             else:
-                s0 = (sg % 8) * 384
-                sg += 1
-                gact(B("SG", s0, s0 + n), B("BK%d" % q), off)
-                pairs[0] += 1
-                bk, at = "pbR%d" % (pairs[0] % 2), 512 * (pairs[0] // 2 % 2)
-                mm(B(bk, at, at + n), B("I"), B("SG", s0, s0 + n), True, False)
-                mm(B(bk, at, at + n), B("nI"), B(cand, a * L, b * L), False, True)
-                act(gm, B(bk, at, at + n), AF.Sign, half, -1.0)
-            mm(cnt, E(m), gm, x == 0, x == 15)
-        act(B("ge", a * L, b * L), cnt, AF.Sign, B("thrc"))
-        if u == 0 and t < VIS - 1:
-            judge(q + 1)
-        rows(small(u), "SLh", "ge", a * L, n)
+                sg = b("SG", ns % 4 * n, (ns % 4 + 1) * n)
+                chain("cS", gat("S", sg, B("BK%d" % q), off))
+                o = B(lease(), 0, n)
+                mms(o, ((B("I"), sg), (B("nI"), cand)))
+                act(gm, o, AF.Sign, half, -1.0)
+                at, ns = m0 + ns, ns + 1
+            mm(cnt, E(at), gm, m == 0, m == 15)
+        bias[0] = PAR["b"]["tr"][h]
+        act(b("ge"), cnt, AF.Sign, thrc[h])
+        rows(B("Ppc%d" % h, n, n + w), "SLh", "ge%d" % h, 0, n)
 
-    def trials(t, u):
-        nj = lambda j: B("nb", 2 * j * C, (2 * j + 1) * C)
-        a, b = GRP[u]
-        cn = small(u)
-        x = 0
-        if u == 0:
-            thr, x = B("cd", 0, C), C
-            tt(thr, B("pen", 0, C), B("B0") if t == 0 else B("bl%d" % t), OP.add)
-            tt(nj(0), B(cn[0], cn[1], cn[1] + C), thr, OP.is_ge)
-        tt(B("cm", a * C + x, b * C), B(cn[0], cn[1] + x, cn[2]), B("pen", a * C + x, b * C), OP.subtract)
-        pn, pd = B("pb0", 432, 432 + C), B("pb0", 448, 448 + C)
-        for j in range(a, b):
-            if j:
-                qn, d = B("bt", (j - 1) * C, j * C), B("cd", C, 2 * C)
-                tsc(qn, pn, 0.25, None, OP.add)
-                tt(d, B("cm", j * C, (j + 1) * C), pd, OP.add)
-                tt(nj(j), d, qn, OP.is_ge)
-            if j < 2 or t < VIS - 1:
-                mm(pn, B("GRh"), nj(j), True, True)
+    def trials(t, h):
+        b = hb(h)
+        nj = lambda j: b("nb", j * C, (j + 1) * C)
+        cn = lambda a, e: B("Ppc%d" % h, 3 * H + a * C, 3 * H + e * C)
+        if t == 0:
+            tsc(nj(0), cn(0, 1), A[t] - 8.0, None, OP.is_ge)
+        else:
+            tt(nj(0), cn(0, 1), B("bl%d%d" % (t, h), 0, C), OP.is_ge)
+        act(b("cm"), cn(1, 3), AF.Identity, 8.0 - A[t])
+        for j in range(3):
+            if j == 2:
+                bk = lease()
+                mms(B(bk, 0, C), [(B("I1"), nj(2)), (B("I2"), nj(1)), (B("I3"), nj(0)), (B("I"), B("LI3b", 0, C)), (B("I"), B("c3"))])
+                mm(B(bk, 8, 8 + 3 * C), B("I"), b("nb"), True, True)
+                mms(B(bk, 8 + 3 * C, 8 + 4 * C), [(B("I"), B("one"))] + [(B("nI"), nj(i)) for i in range(3)])
+                cp(b("bo"), B(bk, 0, C))
+                tt(b("pr", 0, 4 * C), B(bk, 8, 8 + 4 * C), b("ni", 4 * C, 8 * C), OP.mult)
+                tt(b("pr", 4 * C, 8 * C), B(bk, 8, 8 + 4 * C), b("K4"), OP.mult)
+                gat(PAR["mg"], b("M"), B(Cb(t, h)), b("bo"))
+                if t == VIS - 1:
+                    break
+            o, th = B(lease(), 0, C), b("th", j * C, (j + 1) * C)
+            mm(o, B("GR"), nj(j), True, True)
+            if PAR["th"] == "S":
+                act(th, o, AF.Sign, gth)
+            else:
+                tsc(th, o, gth, None, OP.is_ge)
+            o = B(lease(), 0, C)
             if j < 2:
-                mm(pd, B("GRh"), nj(j), True, False)
-                for i in range(j + 1):
-                    mm(pd, B("I64"), nj(i), False, i == j)
-        if b < 3:
-            return
-        bo = B("pb0", 464, 464 + C)
-        mm(bo, B("I"), B("LIb"), True, False)
-        mm(bo, B("I"), B("c3L"), False, False)
-        for j in range(3):
-            mm(bo, B("I%d" % (3 - j)), nj(j), False, j == 2)
-        x = cp(B("bo"), bo)
-        if t < VIS - 1:
-            pi, pj = B("bt", 2 * C, 3 * C), B("ci", 6 * C, 7 * C)
-            order_after(tsc(pi, pn, -2.0, None, OP.mult), x)
-            tsc(pj, pi, 1, None, OP.bitwise_and)
-            tsc(B("bs%d" % (t + 1)), pj, 0.5, None, OP.mult)
-        gact(B("M"), B(Cb(t), 0, 4 * L), B("bo"))
-
-    def visit_bits(t):
-        k = send(B("bl%d" % (t + 1)), B("bs%d" % (t + 1)), (rank - 1) % N, "ab%d" % (t + 1), 4.0)
-        if t < 2:
-            for b in book(t + 3):
-                order_after(b, k)
-
-    def post(t):
-        nb = lambda j, a, b: B("nb", (2 * j + a) * C, (2 * j + b) * C)
-        um = B("pbA", 992, 992 + C)
-        rows(um, "SW0", "M", 0, L)
-        ni = lambda a: B("ni", a * C, (a + 1) * C)
-        cp(ni(0), um)
-        tsc(ni(1), ni(0), 15, None, OP.bitwise_and)
-        tt(B("nf"), ni(1), B("recb"), OP.add)
-        cp(B("n16"), B("nf"))
-        scat(B("X"), B("n16"), B("M"))
-        for j in range(3):
-            tt(nb(j, 1, 2), nb(j, 0, 1), B("kL", j * C, (j + 1) * C), OP.mult)
-        for j in range(3):
-            mm(B("pb0", 480, 480 + 2 * C), B("I"), nb(j, 0, 2), j == 0, j == 2)
-        pu = lambda a: B("pu", a * C, (a + 1) * C)
-        fe = B("fe", 3 * C, 4 * C)
-        tt(pu(0), B("pb0", 480, 480 + C), fe, OP.mult)
-        tt(pu(1), B("pb0", 480 + C, 480 + 2 * C), pu(0), OP.subtract)
-        tt(pu(2), pu(1), fe, OP.add)
-        gtt(B("eq"), pu(2), B("TK"), B("KIL"), OP.is_equal)
-        gtt(B("dd"), B("nf"), B("TK"), B("s"), OP.subtract)
-        tt(B("ed"), B("eq"), B("dd"), OP.mult)
-        tt(B("s"), B("s"), B("ed"), OP.add)
-        if t < VIS - 1:
-            cp(B("s16"), B("s"))
-
-    def near(t):
-        cnt = test(t, "M", 0, OP.is_le, AF.Sign, -1.0, half)
-        act(B("nn"), cnt, AF.Relu, B("thrn"), -1.0)
-        for b in range(0, NB, 2):
-            bk = pair()
-            for x in range(2):
-                at = 128 + 384 * x
-                mm(B(bk, at, at + 384), B("I"), B(Ob(t), 384 * (b + x), 384 * (b + x) + 384), True, False)
-                for a in range(2):
-                    k = 2 * (b + x) + a
-                    mm(B(bk, at + a * L, at + (a + 1) * L), B("R", 128 * k, 128 * k + 128), B("nn"), False, a == 1)
-            if b == 0:
-                act(B("acc"), B(bk, 128, 896), AF.Relu)
+                mms(o, [(B("PA"), th)] + [(B("I64"), nj(i)) for i in range(j + 1)])
+                tt(nj(j + 1), b("cm", j * C, (j + 1) * C), o, OP.is_ge)
             else:
-                tt(B("acc"), B(bk, 128, 896), B("acc"), OP.max)
-        tt(B("fo"), B("acc", 0, 384), B("acc", 384, 768), OP.max)
-        tt(B("cc"), B("fo", 0, L), B("fo", L, 2 * L), OP.max)
-        tt(B("cc"), B("cc"), B("M"), OP.max)
-        uc = B("pbA", 1008, 1008 + C)
-        rows(uc, "SW0", "cc", 0, L)
-        ci = lambda a: B("ci", a * C, (a + 1) * C)
-        cp(ci(0), uc)
-        tsc(ci(1), ci(0), V - 1, None, OP.bitwise_and)
-        tt(ci(2), ci(1), ci(1), OP.mult)
-        tsc(ci(3), ci(1), B("WK0", 1, 2), 97.0 * t, OP.mult, OP.add)
-        tsc(ci(4), ci(2), 5, None, OP.arith_shift_right)
-        tt(ci(5), ci(3), ci(4), OP.add)
-        tsc(ci(0), ci(5), V - 1, None, OP.bitwise_and)
-        cp(B("ch"), ci(0))
-        gtt(B("df"), B("CL"), B("ch"), B("cc"), OP.subtract)
-        act(B(Cb(t + 1), 3 * L, 4 * L), B("df"), AF.Abs)
+                mm(o, B("PA"), th, True, True)
+                act(B("bs%d%d" % (t + 1, h), 0, C), o, AF.Identity, A[t + 1] - 8.0)
+                k = send(B("bl%d%d" % (t + 1, h), 0, C), B("bs%d%d" % (t + 1, h), 0, C), (rank - 1) % N, "ab%d%d" % (t + 1, h), 4.0)
+                if t < 2 and h == 1:
+                    order_after(book(t + 3), k)
 
-    gather(0)
+    def post(t, h):
+        b = hb(h)
+        bk = lease()
+        mms(B(bk, 0, C), [(B("I"), b("pr", j * C, (j + 1) * C)) for j in range(4)] + [(B("I"), b("recb"))])
+        mms(B(bk, C, 2 * C), [(B("I"), b("pr", j * C, (j + 1) * C)) for j in range(4, 8)])
+        cp(b("n16"), B(bk, 0, C))
+        act(b("put"), B(bk, 0, 2 * C), AF.Copy)
+        s = B("s", h, LA, 2)
+        gtt(b("eq"), b("put"), B("TL"), B("KIL"), OP.is_equal)
+        gtt(b("dd"), b("put"), B("TK"), s, OP.subtract)
+        tt(b("ed"), b("eq"), b("dd"), OP.mult)
+        tt(s, s, b("ed"), OP.add)
+        if t < VIS - 1:
+            cp(b("s16"), s)
+
+    def near(t, h):
+        b, O = hb(h), Ob(t, h)
+        cnt = B("Ppc%d" % h, 416, 416 + H)
+        test(t, h, b("M"), SN[h], OP.is_le, AF.Sign, -1.0, half, cnt)
+        act(b("nn"), cnt, AF.Relu, thn[h], -1.0)
+        last = ()
+        for x in range(4):
+            bk = lease()
+            for a in range(4):
+                k = 4 * x + a
+                j = mm(B(bk, a * H, (a + 1) * H), B("R", 128 * k, 128 * k + 128), b("nn"), True, False, after=last)
+                mm(B(bk, a * H, (a + 1) * H), B("I"), B(O, k * H, (k + 1) * H), False, True)
+            last = (j,)
+            for y in range(2):
+                if x == 0 and y == 0:
+                    for a in range(2):
+                        tt(b("acc", a * H, (a + 1) * H), B(bk, a * H, (a + 1) * H), b("M"), OP.max)
+                else:
+                    tt(b("acc"), B(bk, 2 * y * H, (2 * y + 2) * H), b("acc"), OP.max)
+        tt(b("cc"), b("acc", 0, H), b("acc", H, 2 * H), OP.max)
+        o = B(lease(), 0, C)
+        rows(o, "SW0", "cc%d" % h, 0, H)
+        ci = lambda a: b("ci", a * C, (a + 1) * C)
+        cp(ci(0), o)
+        tsc(ci(1), ci(0), V - 1, None, OP.bitwise_and)
+        tsc(b("hf", 0, C), ci(1), pf(6), 1.0 / 32, OP.add, OP.mult)
+        tt(b("hf", C, 2 * C), b("hf", 0, C), ci(1), OP.mult)
+        tsc(ci(2), b("hf", C, 2 * C), 97.0 * t - 0.375, None, OP.add)
+        tsc(ci(3), ci(2), V - 1, None, OP.bitwise_and)
+        cp(b("hc"), ci(3))
+        if t < VIS - 1:
+            gtt(b("df"), B("CL"), b("hc"), b("cc"), OP.subtract)
+            act(B(Cb(t + 1, h), 3 * H, 4 * H), b("df"), AF.Abs)
+        else:
+            gtt(B("dfl", h * H, (h + 1) * H), B("CL"), b("hc"), b("cc"), OP.subtract)
+
     judge(1)
     for t in range(VIS):
-        opened(t)
-        cands(t, 0)
-        cands(t, 1)
+        got = []
+        for h in range(2):
+            bias[0] = PAR["b"]["ga"][h]
+            got.append(gather(t, h))
+        bias[0] = 0.0
         empties(t)
-        for u in range(2):
-            clauses(t, u)
-            trials(t, u)
+        for h in range(2):
+            bias[0] = PAR["b"]["ca"][h]
+            cands(t, h, got[h])
+            clauses(t, h)
+            trials(t, h)
+            bias[0] = PAR["b"]["po"][h]
+            post(t, h)
+        bias[0] = 0.0
         if t < VIS - 1:
-            visit_bits(t)
-        early[0] = LEAD
-        post(t)
-        early[0] = 0.0
-        near(t)
-        if t < VIS - 1:
-            gather(t + 1)
+            judge(t + 2)
+        for h in range(2):
+            bias[0] = PAR["b"]["po"][h]
+            scat(B("X"), B("n16%d" % h), B("M%d" % h))
+            bias[0] = PAR["b"]["ne"][h]
+            near(t, h)
+        bias[0] = 0.0
 
     dma("Y", D("yx", 0, W), B("X", 0, W), "dyx", 5.0)
-    for c2 in range(2):
-        cp(B("T3", c2 * 96, c2 * 96 + 96), B("s", c2, L, 2))
+    bk = lease()
     for g2 in range(2):
-        for c2 in range(2):
-            mm(B("pbR0", g2 * 96, g2 * 96 + 96), B("PM%d%d" % (c2, g2)), B("T3", c2 * 96, c2 * 96 + 96), c2 == 0, c2 == 1, True)
-    for g2 in range(2):
-        for b in range(6):
-            cp(B("T4", 32 * b + 16 * g2, 32 * b + 16 * g2 + 16), B("pbR0", g2 * 96 + b, g2 * 96 + 96, 6))
-    add("V", lambda: g.vector.transpose(B("T5")[3], B("T4")[3]), [B("T5")], [B("T4")], cyc(192))
-    tsc(B("T6"), B("T5"), float(ZB), B("kempty"), OP.is_ge, OP.mult)
-    tt(B("T1"), B("T5"), B("T6"), OP.subtract)
-    dma("Y", D("yl", 0, LA), B("T1"), "dyl", 2.2)
-    dma("Y", D("yz", 0, LA), B(Cb(VIS), 3 * L, 4 * L), "dyz", 2.2)
+        for c2 in (1, 0):
+            mm(B(bk, g2 * H, g2 * H + H), B("PM%d%d" % (c2, g2)), B("s", c2, LA, 2), c2 == 1, c2 == 0, True)
+    act(B("T3"), B(bk, 0, LA), AF.Copy)
+    gat("S", B("T4"), B("T3"), B("Tout"))
+    vtr(B("T5"), B("T4"))
+    tsc(B("T6"), B("T5"), float(ZB), kempty, OP.is_ge, OP.mult)
+    tt(B("T7"), B("T5"), B("T6"), OP.subtract)
+    dma("Y", D("yl", 0, LA), B("T7"), "dyl", 2.2)
+    gat("S", B("zo"), B("dfl"), B("Tz"), AF.Abs)
+    dma("Y", D("yz", 0, LA), B("zo"), "dyz", 2.2)
 
-    order = schedule(ops)
+    if not PLAN:
+        PLAN.append(schedule(ops, leases, bank))
+    order, where, extra = PLAN[0]
+    for i, j in extra:
+        ops[i]["deps"][j] = True
+    for name, b in where.items():
+        for r, p, step in leases[name]["regs"]:
+            r[3] = view("Ppr%d" % b, p, r[1], r[2], step)
     emit(g, T, ops, order, sent[0])
     if report is not None:
         report.append((ops, order))
 
 
-def schedule(ops):
+def place(ops, pred, succ, key):
+    left, est, start, busy = [len(p) for p in pred], [0.0] * len(ops), [0.0] * len(ops), {}
+    ready = sorted((key[i], i) for i in range(len(ops)) if left[i] == 0)
+    while ready:
+        i = ready.pop(0)[1]
+        c, s = ops[i]["cost"], est[i]
+        q = busy.setdefault(ops[i]["eng"], [])
+        lo, hi = 0, len(q)
+        while lo < hi:
+            mid = (lo + hi) // 2
+            if q[mid][1] <= s:
+                lo = mid + 1
+            else:
+                hi = mid
+        while lo < len(q) and q[lo][0] < s + c:
+            s = max(s, q[lo][1])
+            lo += 1
+        q.insert(lo, (s, s + c))
+        start[i] = s
+        for k, lat in succ[i]:
+            est[k] = max(est[k], s + c + lat)
+            left[k] -= 1
+            if left[k] == 0:
+                x = (key[k], k)
+                at = len(ready)
+                while at and ready[at - 1] > x:
+                    at -= 1
+                ready.insert(at, x)
+    return start, max(start[i] + ops[i]["cost"] + ops[i]["lat"] for i in range(len(ops)))
+
+
+def schedule(ops, leases, bank):
     n = len(ops)
-    succ, left, tail = [[] for _ in range(n)], [0] * n, [0.0] * n
+    pred, succ, tail = [[] for _ in range(n)], [[] for _ in range(n)], [0.0] * n
     for i, o in enumerate(ops):
-        left[i] = len(o["deps"])
-        for j in o["deps"]:
-            succ[j].append(i)
+        for j, w in o["deps"].items():
+            lat = ops[j]["lat"] if w or ops[j]["eng"] != o["eng"] else 0.0
+            pred[i].append((j, lat))
+            succ[j].append((i, lat))
     for i in range(n - 1, -1, -1):
-        tail[i] = ops[i]["cost"] + ops[i]["lat"] + max([tail[s] for s in succ[i]] + [0.0])
-    for i in range(n):
-        tail[i] += ops[i]["early"]
-    free, est = {}, [0.0] * n
+        tail[i] = ops[i]["cost"] + max([tail[k] + lat for k, lat in succ[i]] + [ops[i]["lat"]])
+    key, best = [-tail[i] - ops[i]["bias"] for i in range(n)], None
+    for _ in range(PAR["passes"]):
+        start, end = place(ops, pred, succ, key)
+        if best is None or end < best[0]:
+            best = (end, start)
+        back, _e = place(ops, succ, pred, [-(start[i] + ops[i]["cost"] + (0 if succ[i] else ops[i]["lat"])) for i in range(n)])
+        key = [-(back[i] + ops[i]["cost"]) for i in range(n)]
+    start = best[1]
+    left, free, est, where, extra = [len(p) for p in pred], {}, [0.0] * n, {}, []
+    holder, since, todo = [None] * PAR["nr"], [0.0] * PAR["nr"], {l: len(x["ops"]) for l, x in leases.items()}
     ready, order = [i for i in range(n) if left[i] == 0], []
     while ready:
-        st = [(max(free.get(ops[i]["eng"], 0.0), est[i]), i) for i in ready]
-        t0 = min(st)[0]
-        i = -max((tail[i], -i) for s, i in st if s <= t0 + TOL)[1]
+        idle = [b for b, l in enumerate(holder) if l is None or todo[l] == 0]
+        i = min((start[i], i) for i in ready if idle or ops[i]["lease"] is None or ops[i]["lease"] in where)[1]
         o = ops[i]
-        s = max(free.get(o["eng"], 0.0), est[i])
-        o["start"], o["end"] = s, s + o["cost"]
-        free[o["eng"]] = o["end"]
+        s, l = max(free.get(o["eng"], 0.0), est[i]), o["lease"]
+        if l is not None and l not in where:
+            b = min(idle, key=lambda x: since[x])
+            s = max(s, since[b])
+            if holder[b] is not None:
+                extra += [(i, j) for j in bank[holder[b]][1]]
+            holder[b], where[l] = l, b
+        end = free[o["eng"]] = s + o["cost"]
+        if l is not None:
+            todo[l] -= 1
+            since[where[l]] = max(since[where[l]], end + o["lat"])
         order.append(i)
         ready.remove(i)
-        for k in succ[i]:
-            wait = ops[k]["eng"] != o["eng"] or ops[k]["deps"][i]
-            est[k] = max(est[k], o["end"] + (o["lat"] if wait else 0.0))
+        for k, lat in succ[i]:
+            est[k] = max(est[k], end + lat)
             left[k] -= 1
             if left[k] == 0:
                 ready.append(k)
-    return order
+    PAR["ideal"] = (best[0], max(free.values()), max(tail))
+    return order, where, extra
 
 
 def emit(g, T, ops, order, nsent):

@@ -1,3 +1,4 @@
+import numpy as np
 from concourse.bass import DstId, RemoteDMATransfer
 from concourse.mybir import AluOpType as OP, ActivationFunctionType as AF
 
@@ -6,33 +7,35 @@ A = [6, 4, 4, 3]
 ZB = 3072
 H, C = 96, 6
 BW = 4 * H
-PAR = {"so": [2, 2], "sn": [3, 3], "m0": [10, 10], "gv": [0, 0], "gv0": [2, 2], "th": "S", "mg": "S", "chunks": 2, "lat": 0.12, "nr": 6, "xat": 1, "passes": 3,
-       "b": {"ga": [0, 0], "ca": [0, 0], "cl": [-5, -10], "tr": [5, 5], "po": [0, 5], "ne": [0, 0]}}
+PAR = {"so": [3, 2], "sn": [2, 2], "m0": [10, 10], "gv": [0, 3], "gv0": [1, 3], "qs": [1, 1, 1], "a1": "S", "df": [1, 1], "sq": [1, 0], "mg": "S", "chunks": 1, "lat": 0.16, "nr": 6, "xat": 1,
+       "passes": 3, "seed": 0, "grain": 40,
+       "b": {"ga": [3, 6], "ca": [18, 0], "cl": [-2, -16], "tr": [-10, 5], "po": [15, 14], "ne": [0, 6], "op": [0, 3], "ha": [6, 0], "uo": [1, -25], "su": [-6, -3], "mx": [-12, -6], "uc": [0, 15], "em": [-2, -3]}}
 CY, GA = 0.00083, 1.5
 PLAN = []
 CORES = [3, 11, 19, 27, 35, 43, 51, 59]
-CUT = V // 2
-PIECES = ((CUT, 3 * V // 4), (3 * V // 4, V), (0, V // 4), (V // 4, CUT))
+CUT = V // 2 + 128
+VX = V + 304
+PIECES = ((CUT, 3 * V // 4), (3 * V // 4, VX), (0, V // 4), (V // 4, CUT))
 
 SCRATCH = {}
 _two = lambda l: tuple((n + str(h), c) for n, c in l for h in range(2))
 for _t, _l in (
-        ("bfloat16", (("X", W + 16), ("CL", V), ("zl", LA), ("zo", LA), ("dfl", LA), ("d", 144), ("ch", 128), ("cl16", 128), ("neg", 2048), ("R", 2048), ("I", 128), ("nI", 128),
-                      ("I64", 128), ("I3", 128), ("I2", 128), ("I1", 128), ("SL", 144), ("SLL", 144), ("SLh", 144), ("BO", 128), ("GR", 128), ("PA", 128),
+        ("bfloat16", (("X", W + 16), ("CL", VX), ("zl", LA), ("zo", LA), ("dfl", LA), ("d", 144), ("ch", 128), ("cl16", 128), ("neg", 2048), ("R", 2048), ("I", 128), ("nI", 128),
+                      ("I64", 128), ("I3", 128), ("I2", 128), ("I1", 128), ("SL", 144), ("SLL", 144), ("SLh", 144), ("BO", 128), ("GR", 128), ("GRh", 128), ("eighth", C), ("c192", C), ("c0", 3 * C),
                       ("Tg", 128), ("Tr0", 128), ("Tr1", 128), ("Tr2", 128), ("Tri", 128), ("LI3b", 3 * C), ("c8", 3 * C), ("c3", C), ("one", C), ("kpd", 16), ("DX", 48 * C), ("DK", 48 * C))
          + _two((("Oa", 17 * H), ("Ob", 17 * H), ("Ca", 4 * H), ("Cb", 4 * H), ("cmp", 16 * H), ("op", H), ("le", 3 * H), ("G", 48 * H), ("SG", 12 * H),
-                 ("ge", 3 * H), ("nb", 3 * C), ("th", 3 * C), ("K4", 4 * C), ("pr", 8 * C), ("M", H), ("nn", H), ("acc", 2 * H), ("cc", H), ("df", H), ("eq", H), ("recb", C)))),
-        ("float32", (("PM00", 128), ("PM01", 128), ("PM10", 128), ("PM11", 128), ("pf", 8), ("pg", 16), ("c16", 3 * C), ("LI3f", 3 * C), ("KIL", H),
+                 ("ge", 3 * H), ("nb", 3 * C), ("cm", 2 * C), ("qb", 3 * C), ("K4", 4 * C), ("pr", 8 * C), ("M", H), ("nn", H), ("acc", 4 * H), ("cc", H), ("df", H), ("eq", H), ("recb", C)))),
+        ("float32", (("PM00", 128), ("PM01", 128), ("PM10", 128), ("PM11", 128), ("pf", 8), ("pg", 16), ("hk", 8), ("c16", 3 * C), ("LI3f", 3 * C), ("KIL", H),
                      ("sae", LA), ("T1", LA), ("T2", LA), ("T3", LA), ("T4", LA), ("T5", LA), ("T6", LA), ("T7", LA), ("s", LA), ("mx", 17 * 12), ("lf", 24))
-         + _two((("KU", 48 * C), ("cm", 2 * C), ("put", 2 * C), ("dd", H), ("ed", H), ("hf", 2 * C)))),
+         + _two((("KU", 48 * C), ("put", 2 * C), ("dd", H), ("ed", H), ("hf", 3 * C)))),
         ("int32", (("pc", 4), ("sln", LA), ("li", 36))
-         + _two((("ui", 3 * C), ("um", 3 * C), ("sq", 3 * C), ("ba", 3 * C), ("Hs", 48 * C), ("Hm", 48 * C), ("ci", 4 * C), ("ni", 8 * C)))),
+         + _two((("ui", 3 * C), ("um", 3 * C), ("sq", 3 * C), ("ba", 3 * C), ("Hs", 48 * C), ("Hm", 48 * C), ("ci", 4 * C), ("ni", 8 * C), ("qn", 3 * C)))),
         ("uint16", (("TW", 3 * C), ("TK", C), ("TL", C), ("TM", 3 * C), ("Tin", 12), ("Tout", 12), ("Tz", 12))
          + _two((("Tzi", C), ("off", 3 * C), ("ho", 48 * C), ("bo", C), ("hc", C), ("s16", H), ("n16", C))))):
     for _n, _c in _l:
         SCRATCH[_n] = ("sbuf", [128, _c], _t)
 for _q in range(1, 5):
-    SCRATCH["BK%d" % _q] = ("sbuf", [128, V], "bfloat16")
+    SCRATCH["BK%d" % _q] = ("sbuf", [128, VX], "bfloat16")
     SCRATCH["KX%d" % _q] = ("sbuf", [128, 48 * C], "float32")
 for _q in range(5):
     SCRATCH["WK%d" % _q] = ("sbuf", [128, 4], "int32")
@@ -56,7 +59,7 @@ for _n, (_w, _s, _d) in list(SCRATCH.items()):
 for _p in _at:
     SCRATCH[_p] = ("sbuf", [128, _at[_p]], _p[5:])
 
-SEMAPHORES = ["eV", "eS", "eP", "eG", "sent", "dsl", "dx", "dz", "dwt", "dkp", "dyx", "dyl", "dyz"]
+SEMAPHORES = ["eV", "eS", "eP", "eG", "sent", "dsl", "dx", "dz", "dwt", "dkp", "dcw", "dyx", "dyl", "dyz"]
 SEMAPHORES += ["dc%d" % a for a in range(4)] + ["aC%d" % a for a in range(4)] + ["aH%d%d" % (q, a) for q in range(1, 5) for a in range(4)]
 SEMAPHORES += ["aB%d" % q for q in range(2, 5)] + ["aW%d" % q for q in range(1, 5)] + ["ab%d%d" % (t, h) for t in range(1, VIS) for h in range(2)]
 
@@ -153,7 +156,7 @@ def build(g, rank, T, topo, report=None):
                 wr[name] = [x for x in wr.get(name, []) if not (lo <= x[0] and x[1] <= hi)]
                 rd[name] = [x for x in rd.get(name, []) if not (lo <= x[0] and x[1] <= hi)]
             wr.setdefault(name, []).append((lo, hi, i))
-        ops.append({"eng": eng, "call": call, "deps": deps, "cost": cost, "sem": sem, "amt": amt, "lat": LAT if lat is None else lat, "lease": mine, "bias": bias[0],
+        ops.append({"eng": eng, "call": call, "deps": deps, "cost": cost, "sem": sem, "amt": amt, "lat": LAT if lat is None else lat, "lease": mine, "bias": bias[0], "stage": i // PAR["grain"],
                     "lab": (outs or ins)[0][0]})
         return i
 
@@ -288,7 +291,9 @@ def build(g, rank, T, topo, report=None):
         if a == PAR["xat"]:
             dma("Y", B("X", 0, W), D("x0", 0, W), "dx", 4.5)
             dma("Y", B("zl"), D("z0", 0, LA), "dz", 4.5)
-        dma("Y", B("CL", lo, hi), D("cl", lo, hi), "dc%d" % a, 3.0 + a + (3.0 if a >= PAR["xat"] else 0.0))
+        dma("Y", B("CL", lo, min(hi, V)), D("cl", lo, min(hi, V)), "dc%d" % a, 3.0 + a + (3.0 if a >= PAR["xat"] else 0.0))
+        if hi > V:
+            dma("S", B("CL", V, hi), D("cl", 0, hi - V), "dcw", 3.0)
 
     iota(B("pc", 0, 1), [[0, 1]], 0, 1)
     iota(B("d"), [[1, 144]], 0, -1)
@@ -328,9 +333,6 @@ def build(g, rank, T, topo, report=None):
     mixed("TW", 3 * C, 3 * C, 1, -3 * C)
     mixed("TK", C, C, 1, -C)
     tsc(B("TL"), B("TK"), float(C), None, OP.add)
-    for j in (1, 2):
-        cp(B("LI3f", j * C, (j + 1) * C), B("LI3f", 0, C))
-    cp(B("LI3b"), B("LI3f"))
     tsc(B("sae"), B("sln"), 0.0, kempty, OP.is_lt, OP.mult)
     tt(B("T1"), B("sln"), B("sae"), OP.add)
     vtr(B("T2"), B("T1"))
@@ -354,12 +356,14 @@ def build(g, rank, T, topo, report=None):
     tt(B("Tri"), B("Tg"), B("BO"), OP.mult)
     for j in range(3):
         act(B("Tr%d" % j), B("Tri"), AF.Identity, 0.0, 1.0 / (j + 0.5))
-    for nm, v in (("nI", -1.0), ("I64", 64.0), ("I3", -3.0 * H), ("I2", -2.0 * H), ("I1", -1.0 * H)):
+    for nm, v in (("nI", -1.0), ("I64", -64.0), ("I3", -3.0 * H), ("I2", -2.0 * H), ("I1", -1.0 * H)):
         act(B(nm), B("I"), AF.Identity, 0.0, v)
     act(B("SLL"), B("SL"), AF.Identity, 0.0, H / 2.0)
-    act(B("SLh"), B("SL"), AF.Identity, 0.0, 0.5)
-    mem(B("c8"), 8.0 * H)
-    mem(B("c3"), 3.0 * H)
+    act(B("SLh"), B("SL"), AF.Identity, 0.0, 0.25)
+    for j in range(3):
+        act(B("c8", j * C, (j + 1) * C), B("c16", 0, C), AF.Identity, 8.0 * H)
+        act(B("c0", j * C, (j + 1) * C), B("c16", 0, C), AF.Copy)
+    act(B("c3"), B("c16", 0, C), AF.Identity, 3.0 * H)
     mem(B("one"), 1.0)
     mem(half, 0.5)
     mem(B("neg"), -512.0)
@@ -368,15 +372,18 @@ def build(g, rank, T, topo, report=None):
         tsc(thrc[h], row, M0[h] - 0.5, 8.0, OP.is_ge, OP.mult)
     tsc(B("pg", 10, 12), B("pg", 10, 12), 12.5, None, OP.add)
     tsc(B("pg", 12, 14), B("pg", 12, 14), -7.5, None, OP.add)
-    w_th = 0.5 if PAR["th"] == "S" else 1.0
-    tsc(gth, grp, 0.5, -1.0 if PAR["th"] == "S" else 1.0, OP.add, OP.mult)
-    tsc(sgn, odd, -2.0 * w_th, w_th, OP.mult, OP.add)
-    tsc(B("PA"), B("GR"), sgn, None, OP.mult)
+    act(B("GRh"), B("GR"), AF.Identity, 0.0, -0.5)
+    mem(B("eighth"), 0.125)
+    mem(B("c192"), 192.0)
     cp(B("pf", 4, 6), B("WK0", 0, 2))
     tsc(B("kpd", 0, 1), B("GR", 0, 1), pf(5), 32.0, OP.mult, OP.mult)
     bk = lease()
     mm(B(bk, 0, 1), B("BO"), B("kpd", 0, 1), True, True)
     cp(pf(6), B(bk, 0, 1))
+    tsc(pf(7), pf(6), 0.5 / V, None, OP.mult)
+    tsc(B("hk", 4, 5), pf(6), pf(6), -1.0 / 128, OP.mult, OP.mult)
+    for t in range(VIS):
+        tsc(B("hk", t, t + 1), B("hk", 4, 5), 97.0 * t - 0.375, None, OP.add)
     tsc(B("SW0"), B("SL"), pf(4), None, OP.mult)
     chain("G", send_each(B("WK0", 0, 2), [(B("WK%d" % q, 0, 2), (rank - q) % N, "aW%d" % q) for q in range(1, 5)], 7.0))
     for a, (lo, hi) in enumerate(PIECES):
@@ -407,11 +414,11 @@ def build(g, rank, T, topo, report=None):
 
     def judge(q):
         cp(B("pg", 14, 16), B("WK%d" % q, 0, 2))
-        tsc(B("SW%d" % q), B("SL"), pg(14), None, OP.mult)
-        tsc(B("DK"), B("DX"), pg(15), None, OP.mult)
+        act(B("SW%d" % q), B("SL"), AF.Identity, 0.0, pg(14))
+        act(B("DK"), B("DX"), AF.Identity, 0.0, pg(15))
         o = B(lease(), 0, 48 * C)
         mm(o, B("BO"), B("DK"), True, True)
-        act(B("KX%d" % q), o, AF.Copy)
+        act(B("KX%d" % q), o, AF.Identity, 0.0, 32.0)
 
     def gather(t, h):
         nv, js = PAR["gv0" if t == 0 else "gv"][h], []
@@ -446,29 +453,28 @@ def build(g, rank, T, topo, report=None):
         z = B(zc, 3 * H, 4 * H)
         cnt = B("Ppc%d" % h, 320, 320 + H)
         test(t, h, z, SO[h], OP.is_gt, AF.Relu, 1.0, 0.0, cnt, gathered[:1])
+        bias[0] = PAR["b"]["ca"][h]
         act(b("op"), cnt, AF.Sign)
-        bk = lease()
+        bk = "Ppc%d" % h
         for j in range(3):
             mm(B(bk, j * H, (j + 1) * H), B("Tr%d" % j), b("op"), True, True)
         act(b("le"), B(bk, 0, 3 * H), AF.Sign, 1.0, -1.0)
-        o = B(lease(), 0, 3 * C)
-        rows(o, "SLL", "le%d" % h, 0, 3 * H, ((B("I"), B("LI3b")), (B("I"), B("c8"))))
-        cp(b("off"), o)
-        tt(b("K4", 0, 3 * C), o, B("LI3f"), OP.subtract)
+        o = B(bk, 416, 416 + 3 * C)
+        rows(o, "SLL", "le%d" % h, 0, 3 * H, ((B("I"), B("c8")),))
+        tsc(b("off"), o, row, None, OP.add)
+        tt(b("K4", 0, 3 * C), o, B("c0"), OP.subtract)
         for j in range(3):
             gtt(B(zc, j * H, (j + 1) * H), B(Ob(t, h)), b("off", j * C, (j + 1) * C), z, OP.min)
-        o = B(lease(), 0, 3 * C)
+        o = B(bk, 434, 434 + 3 * C)
         rows(o, "SW%d" % (t + 1), zc, 0, 3 * H)
         cp(b("ui"), o)
         tsc(b("um"), b("ui"), V - 1, None, OP.bitwise_and)
-        tt(b("sq"), b("um"), b("um"), OP.mult)
-        tsc(b("ba"), b("sq"), 1.0 / 32, 97.0 * t - 0.375, OP.mult, OP.add)
-        bias[0] = PAR["b"]["cl"][h]
+        bias[0] = PAR["b"]["uo"][h]
         o = B(lease(), 0, 4 * C)
         rows(o, "SW0", zc, 0, 4 * H)
         cp(b("ni", 0, 4 * C), o)
         tsc(b("ni", 4 * C, 8 * C), b("ni", 0, 4 * C), 15, None, OP.bitwise_and)
-        bias[0] = PAR["b"]["ca"][h]
+        bias[0] = PAR["b"]["ha"][h]
 
     def empties(t):
         m = lambda a, b: B("mx", a * 12, b * 12)
@@ -488,12 +494,12 @@ def build(g, rank, T, topo, report=None):
         for c in range(nc):
             r = lambda nm: B(nm, 16 * w * c // nc, 16 * w * (c + 1) // nc)
             tw = B("TW", 0, w // nc)
-            j = gtt(r("KU%d" % h), b("um"), tw, r("KX%d" % q), OP.mult)
+            j = gtt(r("KU%d" % h), b("um"), tw, r("KX%d" % q), OP.add)
             if last is not None:
                 order_after(j, last)
-            gtt(r("Hs%d" % h), b("ba"), tw, r("KU%d" % h), OP.add)
-            tsc(r("Hm%d" % h), r("Hs%d" % h), V - 1, None, OP.bitwise_and)
-            last = cp(r("ho%d" % h), r("Hm%d" % h))
+            gtt(r("Hs%d" % h), b("um"), tw, r("KU%d" % h), OP.mult)
+            tsc(r("Hm%d" % h), r("Hs%d" % h), 5, V - 1, OP.arith_shift_right, OP.bitwise_and)
+            last = tsc(r("ho%d" % h), r("Hm%d" % h), 97.0 * t, None, OP.add)
         nv, ns, m0 = 0, 0, M0[h]
         bias[0] = PAR["b"]["cl"][h]
         for m in range(16):
@@ -518,35 +524,40 @@ def build(g, rank, T, topo, report=None):
         nj = lambda j: b("nb", j * C, (j + 1) * C)
         cn = lambda a, e: B("Ppc%d" % h, 3 * H + a * C, 3 * H + e * C)
         if t == 0:
-            tsc(nj(0), cn(0, 1), A[t] - 8.0, None, OP.is_ge)
+            tsc(nj(0), cn(0, 1), A[t] / 2.0 - 4, None, OP.is_ge)
         else:
             tt(nj(0), cn(0, 1), B("bl%d%d" % (t, h), 0, C), OP.is_ge)
-        act(b("cm"), cn(1, 3), AF.Identity, 8.0 - A[t])
+        tsc(b("cm"), cn(1, 3), 4 - A[t] / 2.0, None, OP.add)
         for j in range(3):
             if j == 2:
-                bk = lease()
-                mms(B(bk, 0, C), [(B("I1"), nj(2)), (B("I2"), nj(1)), (B("I3"), nj(0)), (B("I"), B("LI3b", 0, C)), (B("I"), B("c3"))])
-                mm(B(bk, 8, 8 + 3 * C), B("I"), b("nb"), True, True)
-                mms(B(bk, 8 + 3 * C, 8 + 4 * C), [(B("I"), B("one"))] + [(B("nI"), nj(i)) for i in range(3)])
-                cp(b("bo"), B(bk, 0, C))
-                tt(b("pr", 0, 4 * C), B(bk, 8, 8 + 4 * C), b("ni", 4 * C, 8 * C), OP.mult)
-                tt(b("pr", 4 * C, 8 * C), B(bk, 8, 8 + 4 * C), b("K4"), OP.mult)
+                o = B("Ppc%d" % h, 488, 488 + C)
+                mms(o, [(B("I"), B("c3")), (B("I3"), nj(0)), (B("I2"), nj(1)), (B("I1"), nj(2))])
+                tsc(b("bo"), o, row, None, OP.add)
                 gat(PAR["mg"], b("M"), B(Cb(t, h)), b("bo"))
+                bk = lease()
+                mms(B(bk, 3 * C, 4 * C), [(B("nI"), nj(i)) for i in (2, 1, 0)] + [(B("I"), B("one"))])
+                mm(B(bk, 0, 3 * C), B("I"), b("nb"), True, True)
+                tt(b("pr", 0, 4 * C), B(bk, 0, 4 * C), b("ni", 4 * C, 8 * C), OP.mult)
+                tt(b("pr", 4 * C, 8 * C), B(bk, 0, 4 * C), b("K4"), OP.mult)
                 if t == VIS - 1:
                     break
-            o, th = B(lease(), 0, C), b("th", j * C, (j + 1) * C)
-            mm(o, B("GR"), nj(j), True, True)
-            if PAR["th"] == "S":
-                act(th, o, AF.Sign, gth)
-            else:
-                tsc(th, o, gth, None, OP.is_ge)
-            o = B(lease(), 0, C)
+            bk, qn = lease() if j == 2 else "Ppc%d" % h, b("qn", j * C, (j + 1) * C)
+            mm(B(bk, 0, C), B("GRh"), nj(j), True, True)
+            onS = PAR["qs"][j]
+
+            def half_down(x):
+                if onS:
+                    act(b("qb", j * C, (j + 1) * C), B(bk, 0, C), AF.Identity, x + 192.0)
+                    return b("qb", j * C, (j + 1) * C), [(B("I"), B("c192"))]
+                tsc(qn, B(bk, 0, C), x, None, OP.add)
+                return qn, []
+            more = [(B("I"), B("c192"))] if onS else []
             if j < 2:
-                mms(o, [(B("PA"), th)] + [(B("I64"), nj(i)) for i in range(j + 1)])
-                tt(nj(j + 1), b("cm", j * C, (j + 1) * C), o, OP.is_ge)
+                mms(B(bk, 8, 8 + C), [(B("GRh"), nj(j)), (B("I"), b("cm", j * C, (j + 1) * C))] + [(B("I64"), nj(i)) for i in range(j + 1)] + more)
+                tt(nj(j + 1), B(bk, 8, 8 + C), half_down(0.25)[0], OP.is_ge)
             else:
-                mm(o, B("PA"), th, True, True)
-                act(B("bs%d%d" % (t + 1, h), 0, C), o, AF.Identity, A[t + 1] - 8.0)
+                mms(B(bk, 8, 8 + C), [(B("GRh"), nj(j))] + [(B("GRh"), B("eighth"))] * (A[t + 1] % 2) + more)
+                tt(B("bs%d%d" % (t + 1, h), 0, C), half_down(0.25 + A[t + 1] // 2 - 4)[0], B(bk, 8, 8 + C), OP.subtract)
                 k = send(B("bl%d%d" % (t + 1, h), 0, C), B("bs%d%d" % (t + 1, h), 0, C), (rank - 1) % N, "ab%d%d" % (t + 1, h), 4.0)
                 if t < 2 and h == 1:
                     order_after(book(t + 3), k)
@@ -559,6 +570,7 @@ def build(g, rank, T, topo, report=None):
         cp(b("n16"), B(bk, 0, C))
         act(b("put"), B(bk, 0, 2 * C), AF.Copy)
         s = B("s", h, LA, 2)
+        bias[0] = PAR["b"]["su"][h]
         gtt(b("eq"), b("put"), B("TL"), B("KIL"), OP.is_equal)
         gtt(b("dd"), b("put"), B("TK"), s, OP.subtract)
         tt(b("ed"), b("eq"), b("dd"), OP.mult)
@@ -572,6 +584,7 @@ def build(g, rank, T, topo, report=None):
         test(t, h, b("M"), SN[h], OP.is_le, AF.Sign, -1.0, half, cnt)
         act(b("nn"), cnt, AF.Relu, thn[h], -1.0)
         last = ()
+        bias[0] = PAR["b"]["mx"][h]
         for x in range(4):
             bk = lease()
             for a in range(4):
@@ -579,24 +592,52 @@ def build(g, rank, T, topo, report=None):
                 j = mm(B(bk, a * H, (a + 1) * H), B("R", 128 * k, 128 * k + 128), b("nn"), True, False, after=last)
                 mm(B(bk, a * H, (a + 1) * H), B("I"), B(O, k * H, (k + 1) * H), False, True)
             last = (j,)
-            for y in range(2):
-                if x == 0 and y == 0:
-                    for a in range(2):
-                        tt(b("acc", a * H, (a + 1) * H), B(bk, a * H, (a + 1) * H), b("M"), OP.max)
+            acc = lambda y: b("acc", 2 * y * H, (2 * y + 2) * H)
+            ps = lambda lo, hi: B(bk, lo * H, hi * H)
+            if x == 0:
+                for a in range(2):
+                    tt(b("acc", a * H, (a + 1) * H), ps(a, a + 1), b("M"), OP.max)
+                if PAR["a1"] == "S":
+                    act(acc(1), ps(2, 4), AF.Copy)
                 else:
-                    tt(b("acc"), B(bk, 2 * y * H, (2 * y + 2) * H), b("acc"), OP.max)
-        tt(b("cc"), b("acc", 0, H), b("acc", H, 2 * H), OP.max)
-        o = B(lease(), 0, C)
+                    cp(acc(1), ps(2, 4))
+            elif x < 3:
+                for y in range(2):
+                    tt(acc(y), ps(2 * y, 2 * y + 2), acc(y), OP.max)
+            else:
+                tt(acc(0), ps(0, 2), acc(0), OP.max)
+                tt(ps(2, 4), ps(2, 4), acc(1), OP.max)
+                tt(b("acc", 2 * H, 3 * H), ps(2, 3), b("acc", 0, H), OP.max)
+                tt(ps(3, 4), ps(3, 4), b("acc", H, 2 * H), OP.max)
+                tt(b("cc"), ps(3, 4), b("acc", 2 * H, 3 * H), OP.max)
+        bias[0] = PAR["b"]["uc"][h]
+        o = B("Ppc%d" % h, 306, 306 + C)
         rows(o, "SW0", "cc%d" % h, 0, H)
         ci = lambda a: b("ci", a * C, (a + 1) * C)
-        cp(ci(0), o)
-        tsc(ci(1), ci(0), V - 1, None, OP.bitwise_and)
-        tsc(b("hf", 0, C), ci(1), pf(6), 1.0 / 32, OP.add, OP.mult)
-        tt(b("hf", C, 2 * C), b("hf", 0, C), ci(1), OP.mult)
-        tsc(ci(2), b("hf", C, 2 * C), 97.0 * t - 0.375, None, OP.add)
-        tsc(ci(3), ci(2), V - 1, None, OP.bitwise_and)
-        cp(b("hc"), ci(3))
-        if t < VIS - 1:
+        hf = lambda a: b("hf", a * C, (a + 1) * C)
+        if PAR["sq"][h]:
+            tsc(ci(0), o, 1.0 / V, -0.5 + 0.5 / V, OP.mult, OP.add)
+            act(hf(2), o, AF.Identity, pf(7), 1.0 / V)
+            tt(hf(0), hf(2), ci(0), OP.subtract)
+            act(hf(1), hf(0), AF.Square, 0.0, V / 4.0)
+            tsc(ci(2), hf(1), 0.5, B("hk", t, t + 1), OP.mult, OP.add)
+        else:
+            cp(ci(0), o)
+            tsc(ci(1), ci(0), V - 1, None, OP.bitwise_and)
+            tsc(hf(0), ci(1), pf(6), None, OP.add)
+            tt(ci(2), hf(0), ci(1), OP.mult)
+        if PAR["sq"][h]:
+            tsc(ci(3), ci(2), V - 1, None, OP.bitwise_and)
+            cp(b("hc"), ci(3))
+        else:
+            tsc(ci(3), ci(2), 5, V - 1, OP.arith_shift_right, OP.bitwise_and)
+            tsc(b("hc"), ci(3), 97.0 * t, None, OP.add)
+        if t < VIS - 1 and PAR["df"][h]:
+            gat("S", b("df"), B("CL"), b("hc"))
+            o = B("Ppc%d" % h, 0, H)
+            mms(o, ((B("nI"), b("cc")), (B("I"), b("df"))))
+            act(B(Cb(t + 1, h), 3 * H, 4 * H), o, AF.Abs)
+        elif t < VIS - 1:
             gtt(b("df"), B("CL"), b("hc"), b("cc"), OP.subtract)
             act(B(Cb(t + 1, h), 3 * H, 4 * H), b("df"), AF.Abs)
         else:
@@ -608,10 +649,10 @@ def build(g, rank, T, topo, report=None):
         for h in range(2):
             bias[0] = PAR["b"]["ga"][h]
             got.append(gather(t, h))
-        bias[0] = 0.0
+        bias[0] = PAR["b"]["em"][0]
         empties(t)
         for h in range(2):
-            bias[0] = PAR["b"]["ca"][h]
+            bias[0] = PAR["b"]["op"][h]
             cands(t, h, got[h])
             clauses(t, h)
             trials(t, h)
@@ -627,7 +668,7 @@ def build(g, rank, T, topo, report=None):
             near(t, h)
         bias[0] = 0.0
 
-    dma("Y", D("yx", 0, W), B("X", 0, W), "dyx", 5.0)
+    stores = [dma("Y", D("yx", 0, W), B("X", 0, W), "dyx", 5.0)]
     bk = lease()
     for g2 in range(2):
         for c2 in (1, 0):
@@ -637,10 +678,11 @@ def build(g, rank, T, topo, report=None):
     vtr(B("T5"), B("T4"))
     tsc(B("T6"), B("T5"), float(ZB), kempty, OP.is_ge, OP.mult)
     tt(B("T7"), B("T5"), B("T6"), OP.subtract)
-    dma("Y", D("yl", 0, LA), B("T7"), "dyl", 2.2)
+    stores.append(dma("Y", D("yl", 0, LA), B("T7"), "dyl", 2.2))
     gat("S", B("zo"), B("dfl"), B("Tz"), AF.Abs)
-    dma("Y", D("yz", 0, LA), B("zo"), "dyz", 2.2)
+    stores.append(dma("S", D("yz", 0, LA), B("zo"), "dyz", 1.8))
 
+    add("Rend", None, [], [B("zo")], 0.0, sem="-", amt=0, lat=0.0, after=stores)
     if not PLAN:
         PLAN.append(schedule(ops, leases, bank))
     order, where, extra = PLAN[0]
@@ -695,14 +737,22 @@ def schedule(ops, leases, bank):
             succ[j].append((i, lat))
     for i in range(n - 1, -1, -1):
         tail[i] = ops[i]["cost"] + max([tail[k] + lat for k, lat in succ[i]] + [ops[i]["lat"]])
-    key, best = [-tail[i] - ops[i]["bias"] for i in range(n)], None
-    for _ in range(PAR["passes"]):
+    key, best, rng = [-tail[i] - ops[i]["bias"] for i in range(n)], None, np.random.default_rng(PAR["seed"])
+    for x in range(PAR["passes"]):
         start, end = place(ops, pred, succ, key)
-        if best is None or end < best[0]:
-            best = (end, start)
-        back, _e = place(ops, succ, pred, [-(start[i] + ops[i]["cost"] + (0 if succ[i] else ops[i]["lat"])) for i in range(n)])
+        got = banks(ops, leases, bank, pred, succ, start)
+        if best is None or got[0] <= best[0][0]:
+            best = (got, start)
+        start = best[1] if x >= 2 else start
+        shift = rng.normal(0.0, (0.2, 0.5, 1.0, 2.0)[x % 4], max(o["stage"] for o in ops) + 1) * (x >= 2)
+        back, _e = place(ops, succ, pred, [-(start[i] + ops[i]["cost"] + shift[ops[i]["stage"]]) for i in range(n)])
         key = [-(back[i] + ops[i]["cost"]) for i in range(n)]
-    start = best[1]
+    PAR["ideal"] = (end, best[0][0], max(tail))
+    return best[0][1:]
+
+
+def banks(ops, leases, bank, pred, succ, start):
+    n = len(ops)
     left, free, est, where, extra = [len(p) for p in pred], {}, [0.0] * n, {}, []
     holder, since, todo = [None] * PAR["nr"], [0.0] * PAR["nr"], {l: len(x["ops"]) for l, x in leases.items()}
     ready, order = [i for i in range(n) if left[i] == 0], []
@@ -728,8 +778,7 @@ def schedule(ops, leases, bank):
             left[k] -= 1
             if left[k] == 0:
                 ready.append(k)
-    PAR["ideal"] = (best[0], max(free.values()), max(tail))
-    return order, where, extra
+    return max(free.values()), order, where, extra
 
 
 def emit(g, T, ops, order, nsent):
@@ -743,6 +792,8 @@ def emit(g, T, ops, order, nsent):
     for i in order:
         o = ops[i]
         e = o["eng"]
+        if e == "Rend":
+            continue
         if e[0] == "R":
             total[o["sem"]] = o["amt"]
             mark[i] = (o["sem"], o["amt"])

@@ -7,38 +7,44 @@ A = [6, 4, 4, 3]
 ZB = 3072
 H, C = 96, 6
 BW = 4 * H
-PAR = {"so": [3, 2], "sn": [2, 2], "m0": [10, 10], "gv": [0, 3], "gv0": [1, 3], "qs": [1, 1, 1], "a1": "S", "df": [1, 1], "sq": [1, 0], "mg": "S", "chunks": 1, "lat": 0.16, "nr": 6, "xat": 1,
-       "passes": 3, "seed": 0, "grain": 40,
-       "b": {"ga": [3, 6], "ca": [18, 0], "cl": [-2, -16], "tr": [-10, 5], "po": [15, 14], "ne": [0, 6], "op": [0, 3], "ha": [6, 0], "uo": [1, -25], "su": [-6, -3], "mx": [-12, -6], "uc": [0, 15], "em": [-2, -3]}}
-CY, GA = 0.00083, 1.5
+PAR = {"so": [2, 2], "sn": [1, 1], "m0": [11, 12, 0, 11, 12, 0], "gv": [1, 1], "gv0": [2, 2], "so0": [2, 2], "sn3": [2, 2],
+       "a1": ["S", "S"], "df": [0, 0], "pu": [0, 0], "pk": 1, "tf": [1, 1], "mg": "S", "z3": [1, 1], "nd": [2, 4, 4], "sd": [2, 5, 5], "f1": [1, 0, 0], "mc": [2, 0, 0, 2, 0, 0], "ob": [1, 0], "jn": [0, 0], "sp": [1, 2], "sh": 0.0, "mu": [0, 1], "ep": [1, 0], "nr": 6, "xat": 2,
+       "passes": 2500, "seed": 5, "moves": 1500, "heat": 0.0, "cut": 1.5, "land": 5.0, "call": 1.4, "pe": 0.6, "spare": 99.0, "soon": 0.5, "noise": [2.5, 0.04, 0.2], "wide": 0.5, "warm": 0.6, "pace": [(1.0, 1.5, 3.5, 0.21, 0.53, 64), (1.0, 1.2, 3.5, 0.15, 0.6, 48), (1.25, 1.95, 3.5, 0.16, 0.55, 64)],
+       "b": {"ga": [-5, 18], "ca": [26, 2], "cl": [-6, -16], "tr": [-10, 4], "po": [14, 15], "ne": [-15, -2], "op": [10, 13], "ha": [6, 3], "uo": [1, -25], "su": [-13, -9], "mx": [-12, -9], "uc": [12, 10], "em": [-10, -8], "x1": [0, 0], "x2": [0, 0]}}
+ZO, CO, RO = 2 * H, 3 * H, 12 * H
+SETS = ((0, 2), (2, 3))
+CY = 0.00083
 PLAN = []
 CORES = [3, 11, 19, 27, 35, 43, 51, 59]
-CUT = V // 2 + 128
+CUT = V // 2 + 448
 VX = V + 304
-PIECES = ((CUT, 3 * V // 4), (3 * V // 4, VX), (0, V // 4), (V // 4, CUT))
+MID = (CUT + V) // 2
+PIECES = ((CUT, MID), (0, CUT // 3), (MID, V), (CUT // 3, 2 * CUT // 3), (2 * CUT // 3, CUT), (V, VX))
 
 SCRATCH = {}
 _two = lambda l: tuple((n + str(h), c) for n, c in l for h in range(2))
 for _t, _l in (
-        ("bfloat16", (("X", W + 16), ("CL", VX), ("zl", LA), ("zo", LA), ("dfl", LA), ("d", 144), ("ch", 128), ("cl16", 128), ("neg", 2048), ("R", 2048), ("I", 128), ("nI", 128),
-                      ("I64", 128), ("I3", 128), ("I2", 128), ("I1", 128), ("SL", 144), ("SLL", 144), ("SLh", 144), ("BO", 128), ("GR", 128), ("GRh", 128), ("eighth", C), ("c192", C), ("c0", 3 * C),
-                      ("Tg", 128), ("Tr0", 128), ("Tr1", 128), ("Tr2", 128), ("Tri", 128), ("LI3b", 3 * C), ("c8", 3 * C), ("c3", C), ("one", C), ("kpd", 16), ("DX", 48 * C), ("DK", 48 * C))
-         + _two((("Oa", 17 * H), ("Ob", 17 * H), ("Ca", 4 * H), ("Cb", 4 * H), ("cmp", 16 * H), ("op", H), ("le", 3 * H), ("G", 48 * H), ("SG", 12 * H),
-                 ("ge", 3 * H), ("nb", 3 * C), ("cm", 2 * C), ("qb", 3 * C), ("K4", 4 * C), ("pr", 8 * C), ("M", H), ("nn", H), ("acc", 4 * H), ("cc", H), ("df", H), ("eq", H), ("recb", C)))),
-        ("float32", (("PM00", 128), ("PM01", 128), ("PM10", 128), ("PM11", 128), ("pf", 8), ("pg", 16), ("hk", 8), ("c16", 3 * C), ("LI3f", 3 * C), ("KIL", H),
+        ("bfloat16", (("X", W + 16), ("CL", VX), ("zl", LA), ("zo", LA), ("dfl", LA), ("d", 160), ("ch", 128), ("cl16", 128), ("DPc", 3 * H), ("ph", 3 * H), ("mh", 3 * C), ("I4k", 128), ("DPu", H), ("BOh", 128), ("BWs", 128), ("nI64", 128), ("nGI", 128), ("neg", 512), ("one", 512), ("ln0", H), ("R", 2048), ("I", 128), ("nI", 128),
+                      ("I64", 128), ("I3", 128), ("I2", 128), ("I1", 128), ("In", 128), ("SL", 144), ("SLL", 144), ("SLh", 144), ("BO", 128), ("GR", 128), ("GRh", 128), ("GI", 128), ("c192", C), ("cK", 12), ("em", 24), ("Iq", 128), ("SWn", 144), ("SWs", 144),
+                      ("Tg", 128), ("Tr0", 128), ("Tr1", 128), ("Tr2", 128), ("Tri", 128), ("c8", 3 * C), ("rst", BW), ("rs16", 512), ("lane", H), ("kpd", 16), ("DX", 48 * C), ("DK", 48 * C))
+         + _two((("Oa", 17 * H), ("Ob", 17 * H), ("Ca", RO + 8 * H), ("Cb", RO + 8 * H), ("cmp", 16 * H), ("op", H), ("le", 3 * H), ("G", 48 * H), ("SG", 3 * 512),
+                 ("ge", 3 * H), ("nb", 3 * C), ("CT", 7 * C), ("cs", 3 * H), ("qb", 3 * C), ("K4", 4 * C), ("pr", 8 * C), ("M", H), ("nn", H), ("acc", BW), ("ac4", 16 * H), ("cc", H), ("df", H), ("eq", H)))),
+        ("float32", (("PM00", 128), ("PM01", 128), ("PM10", 128), ("PM11", 128), ("pf", 8), ("pg", 16), ("hk", 8), ("th", 16), ("c16", 3 * C), ("LI3f", 3 * C), ("KIL", H), ("KI0", H),
                      ("sae", LA), ("T1", LA), ("T2", LA), ("T3", LA), ("T4", LA), ("T5", LA), ("T6", LA), ("T7", LA), ("s", LA), ("mx", 17 * 12), ("lf", 24))
-         + _two((("KU", 48 * C), ("put", 2 * C), ("dd", H), ("ed", H), ("hf", 3 * C)))),
+         + _two((("KU", 48 * C), ("put", 2 * C), ("dd", H), ("ed", H), ("hf", 3 * C), ("us", H)))),
+        ("float16", _two((("uh", 3 * C),))),
         ("int32", (("pc", 4), ("sln", LA), ("li", 36))
-         + _two((("ui", 3 * C), ("um", 3 * C), ("sq", 3 * C), ("ba", 3 * C), ("Hs", 48 * C), ("Hm", 48 * C), ("ci", 4 * C), ("ni", 8 * C), ("qn", 3 * C)))),
-        ("uint16", (("TW", 3 * C), ("TK", C), ("TL", C), ("TM", 3 * C), ("Tin", 12), ("Tout", 12), ("Tz", 12))
-         + _two((("Tzi", C), ("off", 3 * C), ("ho", 48 * C), ("bo", C), ("hc", C), ("s16", H), ("n16", C))))):
+         + _two((("ui", 7 * C), ("um", 7 * C), ("Hs", 48 * C), ("Hm", 48 * C), ("ci", 4 * C)))),
+        ("uint16", (("TW0", 3 * C), ("TW1", 3 * C), ("TW2", 3 * C), ("TK", C), ("TL", C), ("Tin", 12), ("Tout", 12), ("Tz", 12))
+         + _two((("Tzi", C), ("off", 3 * C), ("ho", 48 * C), ("bo", C), ("hc", C), ("s16", H), ("n16", C), ("o2", H))))):
     for _n, _c in _l:
         SCRATCH[_n] = ("sbuf", [128, _c], _t)
 for _q in range(1, 5):
     SCRATCH["BK%d" % _q] = ("sbuf", [128, VX], "bfloat16")
     SCRATCH["KX%d" % _q] = ("sbuf", [128, 48 * C], "float32")
+SCRATCH["WK0"] = ("sbuf", [128, 4], "int32")
 for _q in range(5):
-    SCRATCH["WK%d" % _q] = ("sbuf", [128, 4], "int32")
+    SCRATCH["WF%d" % _q] = ("sbuf", [128, 4], "float32")
     SCRATCH["SW%d" % _q] = ("sbuf", [128, 144], "bfloat16")
 for _t in range(1, VIS):
     for _h in range(2):
@@ -46,21 +52,22 @@ for _t in range(1, VIS):
         SCRATCH["bl%d%d" % (_t, _h)] = ("sbuf", [128, 8], "float32")
 for _n in ["pc0", "pc1"] + ["pr%d" % _b for _b in range(6)]:
     SCRATCH["P" + _n] = ("psum", [128, 512], "float32")
-OWN = ("X", "CL", "zl", "zo", "sln", "wti", "kpi", "T7", "WK", "BK", "bs", "bl", "Ppc", "Ppr")
+OWN = ("X", "CL", "zl", "zo", "sln", "wti", "kpi", "T7", "WK", "WF", "BK", "bs", "bl", "Ppc", "Ppr")
 LOGICAL, PLACE, _at = dict(SCRATCH), {}, {}
 for _n, (_w, _s, _d) in list(SCRATCH.items()):
     if _n.rstrip("0123456789") in OWN or _n in OWN:
         continue
     _p = "pool_" + _d
     _u = 16 if _d in ("float32", "int32") else 32
-    PLACE[_n] = (_p, _at.get(_p, 0))
-    _at[_p] = (_at.get(_p, 0) + _s[1] + _u - 1) // _u * _u
+    _pad = _u if _n[0] == "O" or _n == "I" else 0
+    PLACE[_n] = (_p, _at.get(_p, 0) + _pad)
+    _at[_p] = (PLACE[_n][1] + _s[1] + _pad + _u - 1) // _u * _u
     del SCRATCH[_n]
 for _p in _at:
     SCRATCH[_p] = ("sbuf", [128, _at[_p]], _p[5:])
 
-SEMAPHORES = ["eV", "eS", "eP", "eG", "sent", "dsl", "dx", "dz", "dwt", "dkp", "dcw", "dyx", "dyl", "dyz"]
-SEMAPHORES += ["dc%d" % a for a in range(4)] + ["aC%d" % a for a in range(4)] + ["aH%d%d" % (q, a) for q in range(1, 5) for a in range(4)]
+SEMAPHORES = ["eV", "eS", "eP", "eG", "sent", "dsl", "dx", "dz", "dwt", "dkp", "dyx", "dyl", "dyz"]
+SEMAPHORES += ["dc%d" % a for a in range(6)] + ["aC%d" % a for a in range(6)] + ["aH%d%d" % (q, a) for q in range(1, 5) for a in range(6)]
 SEMAPHORES += ["aB%d" % q for q in range(2, 5)] + ["aW%d" % q for q in range(1, 5)] + ["ab%d%d" % (t, h) for t in range(1, VIS) for h in range(2)]
 
 
@@ -86,8 +93,8 @@ def hand_on(g, rank, core, T, topo):
         dst = T.cores[(rank - q) % N]
         rid, pid, _se = topo.addr(dst)
         for a, (lo, hi) in enumerate(PIECES):
-            if lo >= CUT:
-                if q == 1:
+            if lo >= CUT and (q > 1 or lo < V):
+                if q == 1 + (lo >= V):
                     g.wait_ge(T.sem["aC%d" % a], n)
                 g.remote_dma(out_ap=T["BK%d" % q][:, lo:hi], in_ap=T.CL[:, lo:hi], remote_sem=T.sem["aH%d%d" % (q, a)], local_sem=T.sem.sent, pid=pid, routing_id=rid,
                              dma_engine_mask=topo.mask(core, dst))
@@ -96,8 +103,10 @@ def hand_on(g, rank, core, T, topo):
 
 
 def build(g, rank, T, topo, report=None):
-    ops, wr, rd, bank, leases, chains, bias = [], {}, {}, {}, {}, {}, [0.0]
-    LAT = PAR["lat"]
+    ops, wr, rd, bank, leases, chains, bias = [], {}, {}, {}, {}, {}, [(0.0, ""), -1]
+
+    def stage(name, h=0, x=0):
+        bias[0] = (PAR["b"][name][h] if name else 0.0, "%s%d%d" % (name, h, x))
 
     def view(buf, p, a, b, step):
         return T[buf][p[0]:p[1], a:b] if step == 1 else T[buf][p[0]:p[1], a:b:step]
@@ -156,8 +165,8 @@ def build(g, rank, T, topo, report=None):
                 wr[name] = [x for x in wr.get(name, []) if not (lo <= x[0] and x[1] <= hi)]
                 rd[name] = [x for x in rd.get(name, []) if not (lo <= x[0] and x[1] <= hi)]
             wr.setdefault(name, []).append((lo, hi, i))
-        ops.append({"eng": eng, "call": call, "deps": deps, "cost": cost, "sem": sem, "amt": amt, "lat": LAT if lat is None else lat, "lease": mine, "bias": bias[0], "stage": i // PAR["grain"],
-                    "lab": (outs or ins)[0][0]})
+        ops.append({"eng": eng, "call": call, "deps": deps, "cost": cost if isinstance(cost, tuple) else (cost, 0, 0, 0), "sem": sem, "amt": amt, "lat": lat, "lease": mine,
+                    "bias": bias[0][0], "stage": bias[0][1] + eng[0], "visit": bias[1], "lab": [r[0] for r in outs + ins if r[0] not in leases][0]})
         return i
 
     def order_after(i, j):
@@ -166,6 +175,7 @@ def build(g, rank, T, topo, report=None):
     def chain(name, i):
         if name in chains:
             order_after(i, chains[name])
+        ops[i]["prev"] = chains.get(name, 0)
         chains[name] = i
         return i
 
@@ -176,7 +186,7 @@ def build(g, rank, T, topo, report=None):
         return r[0] not in LOGICAL or LOGICAL[r[0]][0] == "psum"
 
     def cyc(n):
-        return 0.02 + max(64, n) * CY
+        return (0.02, max(64, n), 0, 0)
 
     val = lambda s: s[3] if isinstance(s, list) else s
 
@@ -195,37 +205,46 @@ def build(g, rank, T, topo, report=None):
         return add("V", f, [o], ins, cyc(i[4] * (0.5 if two(o, i) else 1)))
 
     def gtt(o, w, off, b, op):
-        return add("V", lambda: g.vector.tensor_tensor(o[3], w[3].indirect(off[3]), b[3], op), [o], [w, off, b], 0.05 + o[4] * GA * CY)
+        return add("V", lambda: g.vector.tensor_tensor(o[3], w[3].indirect(off[3]), b[3], op), [o], [w, off, b], (0.05, 0, o[4], 0))
 
     def scat(w, off, i):
-        return add("V", lambda: g.vector.tensor_copy(w[3].indirect(off[3]), i[3]), [[w[0], w[1], w[2], w[3], -1]], [off, i], 0.05 + i[4] * 3 * CY)
+        return add("V", lambda: g.vector.tensor_copy(w[3].indirect(off[3]), i[3]), [[w[0], w[1], w[2], w[3], -1]], [off, i], (0.05, 0, 0, i[4]))
 
     def mem(o, c):
         return add("V", lambda: g.vector.memset(o[3], c), [o], [], cyc(o[4] * 0.5))
+
+    def scan(o, a, b, init, op0, op1):
+        return add("V", lambda: g.vector.tensor_tensor_scan(o[3], a[3], b[3], init, op0, op1), [o], [a, b], cyc(a[4] * (0.5 if two(o, a, b) else 1)))
 
     def vtr(o, i):
         return add("V", lambda: g.vector.transpose(o[3], i[3]), [o], [i], cyc(i[4]))
 
     def act(o, i, f, bias=0.0, scale=1.0):
         ins = [i] + [s for s in (bias, scale) if isinstance(s, list)]
-        return add("S", lambda: g.scalar.activation(o[3], i[3], f, bias=val(bias), scale=val(scale)), [o], ins, 0.05 + max(64, i[4]) * CY)
+        return add("S", lambda: g.scalar.activation(o[3], i[3], f, bias=val(bias), scale=val(scale)), [o], ins, (0.05, max(64, i[4]), 0, 0))
 
     def gat(e, o, w, off, f=AF.Copy):
         if e == "V":
-            return add("V", lambda: g.vector.tensor_copy(o[3], w[3].indirect(off[3])), [o], [w, off], 0.05 + o[4] * GA * CY)
-        return add("S", lambda: g.scalar.activation(o[3], w[3].indirect(off[3]), f), [o], [w, off], 0.065 + o[4] * GA * CY)
+            return add("V", lambda: g.vector.tensor_copy(o[3], w[3].indirect(off[3])), [o], [w, off], (0.05, 0, o[4], 0))
+        return add("S", lambda: g.scalar.activation(o[3], w[3].indirect(off[3]), f), [o], [w, off], (0.065, 0, o[4], 0))
 
-    def mm(o, l, r, start, stop, f32=False, after=()):
-        return add("P", lambda: g.tensor.matmul(o[3], l[3], r[3], start, stop), [o], [l, r], max(64, r[4]) * 0.00042 * (4 if f32 else 1), after=after)
+    def run(ms, f32=False, after=()):
+        return add("P", lambda: [g.tensor.matmul(o[3], l[3], r[3], a, e) for o, l, r, a, e in ms][-1], [m[0] for m in ms], [x for m in ms for x in m[1:3]],
+                   (0.0, 0, 0, 0) + tuple(m[2][4] for m in ms) * (4 if f32 else 1), after=after)
 
-    def mms(o, terms):
-        for x, (l, r) in enumerate(terms):
-            mm(o, l, r, x == 0, x == len(terms) - 1)
+    def mm(o, l, r, start, stop, after=()):
+        return run([(o, l, r, start, stop)], after=after)
+
+    def terms(o, ts, first=True, last=True):
+        return [(o, l, r, first and x == 0, last and x == len(ts) - 1) for x, (l, r) in enumerate(ts)]
+
+    def mms(o, ts, first=True, last=True, f32=False, after=()):
+        return run(terms(o, ts, first, last), f32, after)
 
     E = lambda r, nm="SL": B(nm, 15 - r, 143 - r)
 
-    def rows(o, nm, src, lo, width, extra=()):
-        mms(o, [(E(r, nm), B(src, lo + r, lo + width, 16)) for r in range(16)] + list(extra))
+    def rows(o, nm, src, lo, width, extra=(), first=True, last=True, step=1):
+        mms(o, list(extra) + [(E(r, nm), B(src, lo + r * step, lo + (width - 1) * step + 1, 16 * step)) for r in range(16)], first, last)
 
     def dma(q, o, i, sem, us):
         eng = {"Y": g.sync, "S": g.scalar}[q]
@@ -245,7 +264,7 @@ def build(g, rank, T, topo, report=None):
         m, n = topo.mask(src_core, dst_core), len(topo.engines(src_core, dst_core))
         rid, pid, _se = topo.addr(dst_core)
         j = add("G", lambda: g.remote_dma(out_ap=o[3], in_ap=i[3], remote_sem=T.sem[sem], local_sem=T.sem.sent, pid=pid, routing_id=rid, dma_engine_mask=m),
-                [], [i], 0.5, sem="-", amt=0)
+                [], [i], PAR["call"], sem="-", amt=0)
         landed(j, o, sem, n, us)
         return j
 
@@ -257,7 +276,7 @@ def build(g, rank, T, topo, report=None):
         rid, pid, _se = topo.addr(helper(topo, me))
         sent[0] += len(es)
         return add("G", lambda: g.remote_dma(out_ap=i[3], in_ap=i[3], remote_sem=T.sem["aC%d" % a], local_sem=T.sem.sent, pid=pid, routing_id=rid,
-                                             dma_engine_mask=sum(1 << x for x in es)), [], [i], 0.5, sem="-", amt=0)
+                                             dma_engine_mask=sum(1 << x for x in es)), [], [i], PAR["call"], sem="-", amt=0)
 
     def send_each(i, jobs, us):
         tr, cnt = [], []
@@ -267,52 +286,64 @@ def build(g, rank, T, topo, report=None):
             rid, pid, _se = topo.addr(T.cores[dst])
             tr.append(RemoteDMATransfer(dst_ids=[DstId(rid=rid, pnc=pid)], dma_engine_mask=sum(1 << e for e in es[x * k:x * k + k]), remote_sem=T.sem[sem], src=i[3], dst=o[3]))
             cnt.append(k)
-        j = add("G", lambda: g.remote_dma_fused(tr, local_sem=T.sem.sent), [], [i], 0.7, sem="-", amt=0)
+        j = add("G", lambda: g.remote_dma_fused(tr, local_sem=T.sem.sent), [], [i], 2 * PAR["call"], sem="-", amt=0)
         for (o, dst, sem), k in zip(jobs, cnt):
             landed(j, o, sem, k, us)
         return j
 
     def asel(o, i, pat, cop, fill, base, cmul):
-        return add("G", lambda: g.affine_select(o[3], i[3], pat, cop, fill, base, cmul), [o], [i], 0.17 + 2 * o[4] * CY)
+        return add("G", lambda: g.affine_select(o[3], i[3], pat, cop, fill, base, cmul), [o], [i], (0.17, 2 * o[4], 0, 0))
+
+    def gcopy(o, i):
+        return asel(o, i, [[0, o[4]]], OP.is_ge, 0.0, 0, 0)
+
+    def scopy(o, i):
+        return act(o, i, AF.Copy)
 
     def iota(o, pat, base, cmul):
         if LOGICAL[o[0]][2] == "int32":
             f = lambda: g.iota(o[3], pat, base, cmul)
         else:
             f = lambda: g.iota(o[3], pat, base, cmul, allow_small_or_imprecise_dtypes=True)
-        return add("G", f, [o], [], 0.13 + 2 * o[4] * CY)
+        j = add("G", f, [o], [], (0.13, 2 * o[4], 0, 0))
+        return j if sent[0] else chain("G", j)
 
-    M0, SO, SN = PAR["m0"], PAR["so"], PAR["sn"]
+    M0 = [[PAR["m0"][3 * h:3 * h + 3] for h in range(2)]] * VIS
+    ring = [0, 0]
+    SO = [PAR["so0"]] + [PAR["so"]] * 3
+    SN = [PAR["sn"]] * 3 + [PAR["sn3"]]
 
     dma("Y", B("sln"), D("sl", 0, LA), "dsl", 2.0)
     dma("S", B("WK0", 1, 2), D("kp", 0, 1), "dkp", 2.0)
     dma("S", B("WK0", 0, 1), D("wt", 0, 1), "dwt", 2.0)
+    dma("S", B("zl"), D("z0", 0, LA), "dz", 2.2)
     for a, (lo, hi) in enumerate(PIECES):
         if a == PAR["xat"]:
-            dma("Y", B("X", 0, W), D("x0", 0, W), "dx", 4.5)
-            dma("Y", B("zl"), D("z0", 0, LA), "dz", 4.5)
-        dma("Y", B("CL", lo, min(hi, V)), D("cl", lo, min(hi, V)), "dc%d" % a, 3.0 + a + (3.0 if a >= PAR["xat"] else 0.0))
-        if hi > V:
-            dma("S", B("CL", V, hi), D("cl", 0, hi - V), "dcw", 3.0)
+            dma("Y", B("X", 0, W), D("x0", 0, W), "dx", 4.3 + 0.8 * a)
+        dma("Y", B("CL", lo, hi), D("cl", lo % V, lo % V + hi - lo), "dc%d" % a, 2.5 + 0.8 * a + (3.0 if a >= PAR["xat"] else 0.0))
 
     iota(B("pc", 0, 1), [[0, 1]], 0, 1)
-    iota(B("d"), [[1, 144]], 0, -1)
+    iota(B("d"), [[1, 160]], -16, -1)
     iota(B("c16"), [[16, 3 * C]], 0, 0)
-    iota(B("cl16"), [[0, 8], [1, 16]], 0, 0)
     iota(B("ch"), [[1, 8], [0, 16]], 0, 0)
+    iota(B("cl16"), [[0, 8], [1, 16]], 0, 0)
+    for j0, j1 in SETS:
+        iota(B("DX", 16 * C * j0, 16 * C * j1), [[1, 16], [0, (j1 - j0) * C]], 0, 0)
     pc, pf, pg = (lambda a: B("pc", a, a + 1)), (lambda a: B("pf", a, a + 1)), (lambda a: B("pg", a, a + 1))
     tsc(pc(1), pc(0), 15, None, OP.bitwise_and)
     tsc(pc(2), pc(0), 4, None, OP.arith_shift_right)
     tsc(pc(3), pc(0), 4, 1, OP.arith_shift_right, OP.bitwise_and)
     cp(B("pf", 0, 4), B("pc", 0, 4))
     row, grp, odd = pf(1), pf(2), pf(3)
-    even, kempty, half, r15, gth, sgn, r6, r16 = [pg(a) for a in range(8)]
-    thn, thrc = (pg(10), pg(11)), (pg(12), pg(13))
-    tsc(even, odd, -1.0, 1.0, OP.mult, OP.add)
-    tsc(kempty, row, -1.0, float(ZB + 16), OP.mult, OP.add)
+    even, kempty, half, r15, r96, r6 = [pg(a) for a in range(6)]
+    line = lambda o, i, a, b: act(o, i, AF.Identity, float(b), float(a))
+    fill = lambda o, v: iota(o, [[0, o[4]]], v, 0)
+    line(even, odd, -1, 1)
+    line(kempty, row, -1, ZB + 16)
+    tsc(B("I", -16, 144), B("d"), 0.0, None, OP.is_equal)
     for g2 in range(2):
         for c2 in range(2):
-            tsc(B("PM%d%d" % (g2, c2)), B("d", 0, 128), 16.0 * (g2 - c2), (even, odd)[c2], OP.is_equal, OP.mult)
+            act(B("PM%d%d" % (g2, c2)), B("I", 16 * (c2 - g2), 16 * (c2 - g2) + 128), AF.Identity, 0.0, (even, odd)[c2])
 
     tsc(B("LI3f", 0, 3 * C), B("c16"), row, None, OP.add)
     e = lambda w: B("LI3f", 0, w)
@@ -327,82 +358,134 @@ def build(g, rank, T, topo, report=None):
         tsc(B(name, 0, w), B("lf", 0, w), float(a), None, OP.mult)
     mixed("Tin", 12, 6, 32, -191)
     for h in range(2):
-        tsc(r16, row, 16.0 * h, None, OP.add)
-        tsc(B("Tzi%d" % h), B("c16", 0, C), 2.0, r16, OP.mult, OP.add)
-        tsc(B("recb%d" % h), B("Tzi%d" % h), 16.0, None, OP.mult)
-    mixed("TW", 3 * C, 3 * C, 1, -3 * C)
-    mixed("TK", C, C, 1, -C)
-    tsc(B("TL"), B("TK"), float(C), None, OP.add)
+        line(pg(6 + h), row, 1, 16 * h)
+        tsc(B("Tzi%d" % h), B("c16", 0, C), 2.0, pg(6 + h), OP.mult, OP.add)
+    mixed("TK", C, C, 2, -2 * C)
+    tsc(B("TL"), B("TK"), 1.0, None, OP.add)
+    mem(B("ph"), 0.5)
+    mem(B("mh"), -0.5)
+    line(B("I4k"), B("I"), V, 0)
     tsc(B("sae"), B("sln"), 0.0, kempty, OP.is_lt, OP.mult)
     tt(B("T1"), B("sln"), B("sae"), OP.add)
     vtr(B("T2"), B("T1"))
     gat("V", B("T3"), B("T2"), B("Tin"))
     for h in range(2):
         bk = lease()
-        for g2 in range(2):
-            mm(B(bk, 0, H), B("PM%d%d" % (g2, h)), B("T3", g2 * H, g2 * H + H), g2 == 0, g2 == 1, True)
+        mms(B(bk, 0, H), [(B("PM%d%d" % (g2, h)), B("T3", g2 * H, g2 * H + H)) for g2 in range(2)], f32=True)
         cp(B("s16%d" % h), B(bk, 0, H))
-        cp(B("s", h, LA, 2), B(bk, 0, H))
-        gat("S", B("Ca%d" % h, 3 * H, 4 * H), B("zl"), B("Tzi%d" % h))
-        for nm in ("Oa%d", "Ob%d"):
-            mem(B(nm % h, 16 * H, 17 * H), -1.0)
+        act(B("s", h, LA, 2), B(bk, 0, H), AF.Copy)
+        gat("S", B("Ca%d" % h, ZO, ZO + H), B("zl"), B("Tzi%d" % h))
+        mem(B("Oa%d" % h, 16 * H, 17 * H), -1.0)
     mem(B("X", W, W + 16), 0.0)
-    tsc(B("I"), B("d", 0, 128), 0.0, None, OP.is_equal)
-    tsc(r15, row, -1.0, 15.0, OP.mult, OP.add)
-    tsc(B("SL"), B("d"), r15, None, OP.is_equal)
+    line(r15, row, -1, 15)
+    tsc(B("SL"), B("d", 16, 160), r15, None, OP.is_equal)
     tsc(B("BO"), B("ch"), grp, None, OP.is_equal)
     tsc(B("GR"), B("cl16"), row, None, OP.is_equal)
-    tsc(B("Tg"), B("d", 0, 128), 0.0, None, OP.is_ge)
-    tt(B("Tri"), B("Tg"), B("BO"), OP.mult)
+    chain("G", asel(B("Tri"), B("BO"), [[1, 128]], OP.is_ge, 0.0, 0, -1))
     for j in range(3):
         act(B("Tr%d" % j), B("Tri"), AF.Identity, 0.0, 1.0 / (j + 0.5))
-    for nm, v in (("nI", -1.0), ("I64", -64.0), ("I3", -3.0 * H), ("I2", -2.0 * H), ("I1", -1.0 * H)):
+    for nm, v in (("nI", -1.0), ("I64", -64.0), ("I3", 3.0 * H), ("I2", 2.0 * H), ("I1", 1.0 * H), ("In", -1.0 * H), ("Iq", 1.0 / 256)):
         act(B(nm), B("I"), AF.Identity, 0.0, v)
     act(B("SLL"), B("SL"), AF.Identity, 0.0, H / 2.0)
-    act(B("SLh"), B("SL"), AF.Identity, 0.0, 0.25)
     for j in range(3):
         act(B("c8", j * C, (j + 1) * C), B("c16", 0, C), AF.Identity, 8.0 * H)
-        act(B("c0", j * C, (j + 1) * C), B("c16", 0, C), AF.Copy)
-    act(B("c3"), B("c16", 0, C), AF.Identity, 3.0 * H)
-    mem(B("one"), 1.0)
-    mem(half, 0.5)
-    mem(B("neg"), -512.0)
     for h in range(2):
-        tsc(thn[h], row, 16 - 4 * SN[h] - 0.5, -3.0, OP.is_ge, OP.mult)
-        tsc(thrc[h], row, M0[h] - 0.5, 8.0, OP.is_ge, OP.mult)
-    tsc(B("pg", 10, 12), B("pg", 10, 12), 12.5, None, OP.add)
-    tsc(B("pg", 12, 14), B("pg", 12, 14), -7.5, None, OP.add)
-    act(B("GRh"), B("GR"), AF.Identity, 0.0, -0.5)
-    mem(B("eighth"), 0.125)
-    mem(B("c192"), 192.0)
-    cp(B("pf", 4, 6), B("WK0", 0, 2))
-    tsc(B("kpd", 0, 1), B("GR", 0, 1), pf(5), 32.0, OP.mult, OP.mult)
+        act(B("cK", h, 12, 2), B("c16", 0, C), AF.Identity, 15.0 * H)
+    line(half, row, 0, 0.5)
+    mem(B("neg"), -512.0)
+    made = {}
+
+    def thr(kind, n):
+        if (kind, n) not in made:
+            o = made[kind, n] = B("th", len(made), len(made) + 1)
+            if kind == "n":
+                tsc(o, row, 16 - 4 * n - 0.5, -3.0, OP.is_ge, OP.mult)
+                act(o, o, AF.Identity, 12.5)
+            else:
+                tsc(o, row, n - 0.5, 8.0, OP.is_lt, OP.mult)
+                act(o, o, AF.Identity, -7.5)
+        return made[kind, n]
+    for t in range(VIS):
+        for h in range(2):
+            thr("n", SN[t][h])
+            for x in range(len(SETS)):
+                thr("c", 16 - M0[t][h][x])
+    act(B("GRh"), B("GR", 0, 128), AF.Identity, 0.0, -0.5)
+    if PAR["pk"] or max(PAR["pu"]):
+        bk = lease()
+        run([m for a in range(3) for m in terms(B(bk, a * H, (a + 1) * H), [(B("I64"), B("GR", 0, H)), (B("I", 1, 129), B("GR", 0, H))])])
+        line(B("DPc"), B(bk, 0, 3 * H), 16, 0)
+        line(B("DPu"), B(bk, 0, H), 256, 0)
+    line(B("SLh"), B("SL"), 0.25, 0)
+    tsc(pg(8), row, 14.5, 16.0 * PAR["pk"], OP.is_lt, OP.mult)
+    line(pg(10), pg(8), -1, 192)
+    act(B("c192"), B("c16", 0, C), AF.Identity, pg(10), 0.0)
+    line(B("th", 15, 16), pg(8), 1, A[0] / 2.0 - 4)
+    for t in range(1, VIS):
+        line(B("th", 11 + t, 12 + t), pg(8), 1, A[t] / 2.0 - 196)
+    line(B("BOh"), B("BO"), 0.25, 0)
+    tsc(B("WF0", 0, 1), B("WK0", 0, 1), 1.0 / V, None, OP.mult)
+    cp(B("WF0", 1, 2), B("WK0", 1, 2))
+    act(B("kpd", 0, 1), B("GR", 0, 1), AF.Identity, 0.0, B("WF0", 1, 2))
     bk = lease()
     mm(B(bk, 0, 1), B("BO"), B("kpd", 0, 1), True, True)
-    cp(pf(6), B(bk, 0, 1))
-    tsc(pf(7), pf(6), 0.5 / V, None, OP.mult)
-    tsc(B("hk", 4, 5), pf(6), pf(6), -1.0 / 128, OP.mult, OP.mult)
+    line(pf(7), B(bk, 0, 1), 4, 0)
+    act(B("hk", 4, 5), pf(7), AF.Square)
     for t in range(VIS):
-        tsc(B("hk", t, t + 1), B("hk", 4, 5), 97.0 * t - 0.375, None, OP.add)
-    tsc(B("SW0"), B("SL"), pf(4), None, OP.mult)
-    chain("G", send_each(B("WK0", 0, 2), [(B("WK%d" % q, 0, 2), (rank - q) % N, "aW%d" % q) for q in range(1, 5)], 7.0))
+        line(B("hk", t, t + 1), B("hk", 4, 5), -0.5, 97.0 * t - 0.375)
+    if min(PAR["pu"]) == 0:
+        act(B("SWs"), B("SL"), AF.Identity, 0.0, B("WF0", 0, 1))
+    if max(PAR["pu"]):
+        act(B("BWs"), B("BO"), AF.Identity, 0.0, B("WF0", 0, 1))
+    tsc(B("li", 35, 36), B("WK0", 0, 1), 15, None, OP.bitwise_and)
+    tsc(pg(9), B("li", 35, 36), 256.0, None, OP.mult)
+    act(B("SWn"), B("SL"), AF.Identity, 0.0, pg(9))
+    chain("G", send_each(B("WF0", 0, 2), [(B("WF%d" % q, 0, 2), (rank - q) % N, "aW%d" % q) for q in range(1, 5)], 7.0))
     for a, (lo, hi) in enumerate(PIECES):
         if lo >= CUT:
             last = chain("G", hand(B("CL", lo, hi), a))
-            for q in range(1, 5):
-                add("RaH%d%d" % (q, a), None, [B("BK%d" % q, lo, hi)], [], 0.0, sem="aH%d%d" % (q, a), amt=len(topo.engines(helper(topo, me), T.cores[(rank + q) % N])),
-                    lat=5.0 * q + 3, after=(last,))
+            for q in range(1 + (lo >= V), 5):
+                add("RaH%d%d" % (q, a), None, [B("BK%d" % q, lo, hi)], [], 0.0, sem="aH%d%d" % (q, a),
+                    amt=len(topo.engines(helper(topo, me), T.cores[(rank + q) % N])), lat=8.0 * q, after=(last,))
         else:
-            last = chain("G", send(B("BK1", lo, hi), B("CL", lo, hi), (rank - 1) % N, "aC%d" % a, 4.0))
-    iota(B("DX"), [[1, 16], [0, 3 * C]], 0, 0)
+            last = chain("G", send(B("BK1", lo, hi), B("CL", lo, hi), (rank - 1) % N, "aC%d" % a, PAR["land"]))
     tsc(B("DX"), B("DX"), row, None, OP.is_equal)
-    order_after(asel(B("R"), B("neg"), [[-1, 16], [-16, 8], [0, 16]], OP.is_equal, 0.0, 0, 1), last)
-    order_after(iota(B("KIL"), [[H, 16], [0, C]], 0, 0), last)
-    order_after(iota(B("li", 0, 12), [[1, C], [H, 2]], 0, 0), last)
-    tsc(r6, row, 6.0, None, OP.mult)
-    tsc(B("Tout"), B("li", 0, 12), r6, None, OP.add)
-    order_after(iota(B("li", 12, 24), [[16, C], [H, 2]], 0, 0), last)
-    tsc(B("Tz"), B("li", 12, 24), row, None, OP.add)
+    late = lambda j: order_after(j, last)
+    bk = lease()
+    mms(B(bk, 0, 128), [(B("I"), B("GRh")), (B("I"), B("I64"))])
+    line(B("GI"), B(bk, 0, 128), 1, 0)
+    line(B("nGI"), B(bk, 0, 128), -1, 0)
+    line(B("nI64"), B("I"), 64, 0)
+    for h in range(2):
+        mem(B("CT%d" % h, 2 * C, 7 * C), 0.0)
+        line(B("CT%d" % h, 0, C), B("c16", 0, C), 1, 0)
+        line(B("CT%d" % h, C, 2 * C), B("c16", 0, C), 0, 1)
+        tsc(B("CT%d" % h, 5 * C, 7 * C, 2), B("Tzi%d" % h), 16.0, None, OP.mult)
+        late(fill(B("Ob%d" % h, 16 * H, 17 * H), -1))
+        if PAR["ob"][h]:
+            late(fill(B("Oa%d" % h, -16, 0), -1))
+            late(fill(B("Ob%d" % h, -16, 0), -1))
+    late(iota(B("KI0"), [[6, 16], [1, C]], 0, 0))
+    if min(PAR["ob"]) == 0:
+        for a in range(4):
+            late(asel(B("R", 512 * a, 512 * a + 512), B("neg"), [[-1, 4], [-16, 8], [0, 16]], OP.is_equal, 0.0, -4 * a, 1))
+        mem(B("rst"), 1.0)
+        mem(B("rst", 0, BW, 4), 0.0)
+    if max(PAR["ob"]):
+        mem(B("rs16"), 1.0)
+        mem(B("rs16", 0, 512, 16), 0.0)
+        line(r96, row, H, 16)
+        late(iota(B("ln0"), [[1, H]], 0, 0))
+    late(iota(B("li", 0, 12), [[1, C], [H, 2]], 0, 0))
+    line(r6, row, 6, 0)
+    late(iota(B("li", 12, 24), [[16, C], [H, 2]], 0, 0))
+
+    def behind_first_clauses():
+        order_after(line(B("KIL"), B("KI0"), 1.0 / 16, 0), chains["cS"])
+        if max(PAR["ob"]):
+            order_after(line(B("lane"), B("ln0"), 1.0 / 64, 0), chains["cS"])
+        order_after(tsc(B("Tout"), B("li", 0, 12), r6, None, OP.add), chains["cV"])
+        order_after(tsc(B("Tz"), B("li", 12, 24), row, None, OP.add), chains["cV"])
 
     def book(q):
         return send(B("BK%d" % q, 0, CUT), B("CL", 0, CUT), (rank - q) % N, "aB%d" % q, 14.0)
@@ -413,9 +496,8 @@ def build(g, rank, T, topo, report=None):
     hb = lambda h: (lambda n, *a: B(n + str(h), *a))
 
     def judge(q):
-        cp(B("pg", 14, 16), B("WK%d" % q, 0, 2))
-        act(B("SW%d" % q), B("SL"), AF.Identity, 0.0, pg(14))
-        act(B("DK"), B("DX"), AF.Identity, 0.0, pg(15))
+        act(B("SW%d" % q), B("SL"), AF.Identity, 0.0, B("WF%d" % q, 0, 1))
+        act(B("DK"), B("DX"), AF.Identity, 0.0, B("WF%d" % q, 1, 2))
         o = B(lease(), 0, 48 * C)
         mm(o, B("BO"), B("DK"), True, True)
         act(B("KX%d" % q), o, AF.Identity, 0.0, 32.0)
@@ -430,8 +512,7 @@ def build(g, rank, T, topo, report=None):
         O = Ob(t, h)
         if ns < 4:
             rep = lease()
-            for a in range(4):
-                mm(B(rep, a * H, (a + 1) * H), B("I"), rec, True, True, after=after)
+            run([(B(rep, a * H, (a + 1) * H), B("I"), rec, True, True) for a in range(4)], after=after)
         order = []
         for x in range(4):
             order += [b for b in (x if x < 4 - ns else None, 4 - ns + x if x < ns else None) if b is not None]
@@ -441,40 +522,42 @@ def build(g, rank, T, topo, report=None):
                 tt(o, B(O, BW * b, BW * b + BW), B(rep, 0, BW), opv)
             else:
                 bk = lease()
-                mm(B(bk, 0, BW), B("I"), B(O, BW * b, BW * b + BW), True, False, after=[j for lo, hi, j in wr[rec[0]] if lo < rec[2] and rec[1] < hi])
-                for a in range(4):
-                    mm(B(bk, a * H, (a + 1) * H), B("nI"), rec, False, a == 3)
+                run([(B(bk, 0, BW), B("I"), B(O, BW * b, BW * b + BW), True, False)] + [(B(bk, a * H, (a + 1) * H), B("nI"), rec, False, a == 3) for a in range(4)])
                 act(o, B(bk, 0, BW), fS, bias, scale)
-            for k in range(4 * b, 4 * b + 4):
-                mm(cnt, E(k), B("cmp%d" % h, k * H, (k + 1) * H), x == 0 and k == 4 * b, x == 3 and k == 4 * b + 3)
+            mms(cnt, [(E(k), B("cmp%d" % h, k * H, (k + 1) * H)) for k in range(4 * b, 4 * b + 4)], x == 0, x == 3)
 
     def cands(t, h, gathered):
         b, zc = hb(h), Cb(t, h)
-        z = B(zc, 3 * H, 4 * H)
+        z = B(zc, ZO, CO)
+        if PAR["z3"][h] and t:
+            for a in range(2):
+                gcopy(B(zc, a * H, (a + 1) * H), z)
         cnt = B("Ppc%d" % h, 320, 320 + H)
-        test(t, h, z, SO[h], OP.is_gt, AF.Relu, 1.0, 0.0, cnt, gathered[:1])
-        bias[0] = PAR["b"]["ca"][h]
+        test(t, h, z, SO[t][h], OP.is_gt, AF.Relu, 1.0, 0.0, cnt, gathered[:1])
+        stage("ca", h)
         act(b("op"), cnt, AF.Sign)
         bk = "Ppc%d" % h
-        for j in range(3):
-            mm(B(bk, j * H, (j + 1) * H), B("Tr%d" % j), b("op"), True, True)
+        run([(B(bk, j * H, (j + 1) * H), B("Tr%d" % j), b("op"), True, True) for j in range(3)])
         act(b("le"), B(bk, 0, 3 * H), AF.Sign, 1.0, -1.0)
         o = B(bk, 416, 416 + 3 * C)
         rows(o, "SLL", "le%d" % h, 0, 3 * H, ((B("I"), B("c8")),))
         tsc(b("off"), o, row, None, OP.add)
-        tt(b("K4", 0, 3 * C), o, B("c0"), OP.subtract)
-        for j in range(3):
-            gtt(B(zc, j * H, (j + 1) * H), B(Ob(t, h)), b("off", j * C, (j + 1) * C), z, OP.min)
-        o = B(bk, 434, 434 + 3 * C)
-        rows(o, "SW%d" % (t + 1), zc, 0, 3 * H)
-        cp(b("ui"), o)
-        tsc(b("um"), b("ui"), V - 1, None, OP.bitwise_and)
-        bias[0] = PAR["b"]["uo"][h]
-        o = B(lease(), 0, 4 * C)
-        rows(o, "SW0", zc, 0, 4 * H)
-        cp(b("ni", 0, 4 * C), o)
-        tsc(b("ni", 4 * C, 8 * C), b("ni", 0, 4 * C), 15, None, OP.bitwise_and)
-        bias[0] = PAR["b"]["ha"][h]
+        act(b("K4", C, 4 * C), o, AF.Copy)
+        if PAR["z3"][h] and t:
+            gtt(B(zc, CO, CO + 3 * H), B(Ob(t, h)), b("off"), B(zc, 0, CO), OP.min)
+        else:
+            for j in range(3):
+                gtt(B(zc, CO + j * H, CO + (j + 1) * H), B(Ob(t, h)), b("off", j * C, (j + 1) * C), z, OP.min)
+        bk = lease()
+        rows(B(bk, 0, 3 * C), "SW%d" % (t + 1), zc, CO, 3 * H, ((B("I"), B("mh")),))
+        tsc(b("ui", 0, 3 * C), B(bk, 0, 3 * C), 0.5 / V, None, OP.add)
+        tt(b("uh"), B(bk, 0, 3 * C), b("ui", 0, 3 * C), OP.subtract)
+        if True:
+            stage("uo", h)
+            o = B(lease(), 0, 4 * C)
+            rows(o, "SWn", zc, ZO, 4 * H)
+            cp(b("ui", 3 * C, 7 * C), o)
+            tsc(b("um", 3 * C, 7 * C), b("ui", 3 * C, 7 * C), V - 1, None, OP.bitwise_and)
 
     def empties(t):
         m = lambda a, b: B("mx", a * 12, b * 12)
@@ -482,197 +565,243 @@ def build(g, rank, T, topo, report=None):
         tt(m(8, 12), m(0, 4), m(4, 8), OP.max)
         tt(m(12, 14), m(8, 10), m(10, 12), OP.max)
         tt(m(14, 15), m(12, 13), m(13, 14), OP.max)
-        tsc(m(15, 16), m(14, 15), float(ZB), float(ZB + 15 - t), OP.is_lt, OP.mult)
-        tt(m(16, 17), m(14, 15), m(15, 16), OP.max)
+        tsc(B("em", 0, 12), m(14, 15), float(ZB), -1.0, OP.subtract, OP.max)
+        act(B("em", 12, 24), B("em", 0, 12), AF.Relu, 0.0, t - 16.0)
+        bk = lease()
+        mms(B(bk, 0, 12), [(B("I"), B("cK")), (B("In"), B("em", 0, 12)), (B("In"), B("em", 12, 24))])
         for h in range(2):
-            act(B("K4%d" % h, 3 * C, 4 * C), B("mx", 192 + h, 204, 2), AF.Identity, float(H * (ZB + 15)), -1.0 * H)
+            act(B("K4%d" % h, 0, C), B(bk, h, 12, 2), AF.Copy)
 
-    def clauses(t, h):
-        b, q, cand, w, n = hb(h), t + 1, B(Cb(t, h), 0, 3 * H), 3 * C, 3 * H
-        cnt = B("Ppc%d" % h, 0, n)
-        last, nc = None, PAR["chunks"]
-        for c in range(nc):
-            r = lambda nm: B(nm, 16 * w * c // nc, 16 * w * (c + 1) // nc)
-            tw = B("TW", 0, w // nc)
-            j = gtt(r("KU%d" % h), b("um"), tw, r("KX%d" % q), OP.add)
-            if last is not None:
-                order_after(j, last)
-            gtt(r("Hs%d" % h), b("um"), tw, r("KU%d" % h), OP.mult)
-            tsc(r("Hm%d" % h), r("Hs%d" % h), 5, V - 1, OP.arith_shift_right, OP.bitwise_and)
-            last = tsc(r("ho%d" % h), r("Hm%d" % h), 97.0 * t, None, OP.add)
-        nv, ns, m0 = 0, 0, M0[h]
-        bias[0] = PAR["b"]["cl"][h]
-        for m in range(16):
-            off, gm = b("ho", m * w, (m + 1) * w), b("G", m * n, (m + 1) * n)
-            if (16 - m) * (16 - m0) // 16 == (15 - m) * (16 - m0) // 16:
-                chain("cV", gtt(gm, B("BK%d" % q), off, cand, OP.is_le))
-                at, nv = nv, nv + 1
+    def clauses(t, h, x, bk):
+        b, q, zc, (j0, j1) = hb(h), t + 1, Cb(t, h), SETS[x]
+        w, n = (j1 - j0) * C, (j1 - j0) * H
+        cand, cnt, BK = B(zc, CO + j0 * H, CO + j1 * H), B(bk, 0, n), B("BK%d" % q, 0, VX if t else V)
+        stage("ha", h, x)
+        r = lambda nm, lo=0, hi=16: B(nm, 16 * C * j0 + lo * w, 16 * C * j0 + hi * w)
+        u = lease()
+        run([(B(u, 0, 16 * w), B("I4k"), B("ph", 0, 16 * w), True, False)] + [(B(u, m * w, (m + 1) * w), B("I4k"), b("uh", j0 * C, j1 * C), False, m == 15) for m in range(16)])
+        tt(r("KU%d" % h), B(u, 0, 16 * w), r("KX%d" % q), OP.add)
+        tt(r("Hs%d" % h), B(u, 0, 16 * w), r("KU%d" % h), OP.mult)
+        tsc(r("Hm%d" % h), r("Hs%d" % h), 5, V - 1, OP.arith_shift_right, OP.bitwise_and)
+        tsc(r("ho%d" % h), r("Hm%d" % h), 97.0 * t, None, OP.add)
+        ms, nd, sd = 16 - M0[t][h][x], PAR["nd"][x], min(PAR["sd"][x], 512 // n)
+        at = CO + j0 * H if j1 == 3 else RO + j0 * H
+        got = 1 if j1 == 3 else 0
+        while got < nd and nd > 1:
+            k = max(1, min(got, nd - got))
+            (gcopy if t else scopy)(B(zc, at + got * n, at + (got + k) * n), B(zc, at, at + k * n) if got > 1 else cand)
+            got += k
+        stage("cl", h, x)
+        mv = ms + PAR["mc"][3 * h + x]
+        first = mv + PAR["f1"][x] * (nd > 1)
+        calls = [((m + 1 - mv) / (16 - ms), "V", m, m + 1) for m in range(mv, first)]
+        calls += [((min(m + nd, 16) - mv) / (16 - ms), "V", m, min(m + nd, 16)) for m in range(first, 16, nd)]
+        calls += [(min(m + sd, ms) / mv + PAR["sh"], "S", m, min(m + sd, ms)) for m in range(0, ms, sd)]
+        calls += [(min(m + sd, mv) / mv + PAR["sh"], "X", m, min(m + sd, mv)) for m in range(ms, mv, sd)]
+        done, G, rep = 0, lambda lo, hi: b("G", 16 * H * j0 + lo * n, 16 * H * j0 + hi * n), None
+        for _k, e, lo, hi in sorted(calls):
+            k = hi - lo
+            if e == "V":
+                chain("cV", gtt(G(lo, hi), BK, r("ho%d" % h, lo, hi), B(zc, at, at + k * n) if k > 1 else cand, OP.is_le))
             else:
-                sg = b("SG", ns % 4 * n, (ns % 4 + 1) * n)
-                chain("cS", gat("S", sg, B("BK%d" % q), off))
-                o = B(lease(), 0, n)
-                mms(o, ((B("I"), sg), (B("nI"), cand)))
-                act(gm, o, AF.Sign, half, -1.0)
-                at, ns = m0 + ns, ns + 1
-            mm(cnt, E(at), gm, m == 0, m == 15)
-        bias[0] = PAR["b"]["tr"][h]
-        act(b("ge"), cnt, AF.Sign, thrc[h])
-        rows(B("Ppc%d" % h, n, n + w), "SLh", "ge%d" % h, 0, n)
+                ring[h] = (ring[h] + 1) % 3
+                sg = b("SG", 512 * ring[h], 512 * ring[h] + k * n)
+                j = chain("cS", gat("S", sg, BK, r("ho%d" % h, lo, hi)))
+            if e == "X":
+                if rep is None:
+                    rep = lease()
+                    run([(B(rep, a * n, (a + 1) * n), B("I"), cand, True, True) for a in range(k)], after=[ops[j]["prev"]])
+                chain("cV", tt(G(lo, hi), sg, B(rep, 0, k * n), OP.is_le))
+            elif e == "S":
+                o = lease()
+                run([(B(o, 0, k * n), B("I"), sg, True, False)] + [(B(o, a * n, (a + 1) * n), B("nI"), cand, False, a == k - 1) for a in range(k)])
+                act(G(lo, hi), B(o, 0, k * n), AF.Sign, half, -1.0)
+            mms(cnt, [(E(m), G(m, m + 1)) for m in range(lo, hi)], done == 0, done + k == 16)
+            done += k
+        stage("tr", h, x)
+        act(b("ge", j0 * H, j1 * H), cnt, AF.Sign, thr("c", ms))
 
     def trials(t, h):
         b = hb(h)
         nj = lambda j: b("nb", j * C, (j + 1) * C)
         cn = lambda a, e: B("Ppc%d" % h, 3 * H + a * C, 3 * H + e * C)
-        if t == 0:
-            tsc(nj(0), cn(0, 1), A[t] / 2.0 - 4, None, OP.is_ge)
-        else:
-            tt(nj(0), cn(0, 1), B("bl%d%d" % (t, h), 0, C), OP.is_ge)
-        tsc(b("cm"), cn(1, 3), 4 - A[t] / 2.0, None, OP.add)
-        for j in range(3):
-            if j == 2:
-                o = B("Ppc%d" % h, 488, 488 + C)
-                mms(o, [(B("I"), B("c3")), (B("I3"), nj(0)), (B("I2"), nj(1)), (B("I1"), nj(2))])
-                tsc(b("bo"), o, row, None, OP.add)
-                gat(PAR["mg"], b("M"), B(Cb(t, h)), b("bo"))
-                bk = lease()
-                mms(B(bk, 3 * C, 4 * C), [(B("nI"), nj(i)) for i in (2, 1, 0)] + [(B("I"), B("one"))])
-                mm(B(bk, 0, 3 * C), B("I"), b("nb"), True, True)
-                tt(b("pr", 0, 4 * C), B(bk, 0, 4 * C), b("ni", 4 * C, 8 * C), OP.mult)
-                tt(b("pr", 4 * C, 8 * C), B(bk, 0, 4 * C), b("K4"), OP.mult)
-                if t == VIS - 1:
-                    break
-            bk, qn = lease() if j == 2 else "Ppc%d" % h, b("qn", j * C, (j + 1) * C)
-            mm(B(bk, 0, C), B("GRh"), nj(j), True, True)
-            onS = PAR["qs"][j]
-
-            def half_down(x):
-                if onS:
-                    act(b("qb", j * C, (j + 1) * C), B(bk, 0, C), AF.Identity, x + 192.0)
-                    return b("qb", j * C, (j + 1) * C), [(B("I"), B("c192"))]
-                tsc(qn, B(bk, 0, C), x, None, OP.add)
-                return qn, []
-            more = [(B("I"), B("c192"))] if onS else []
-            if j < 2:
-                mms(B(bk, 8, 8 + C), [(B("GRh"), nj(j)), (B("I"), b("cm", j * C, (j + 1) * C))] + [(B("I64"), nj(i)) for i in range(j + 1)] + more)
-                tt(nj(j + 1), B(bk, 8, 8 + C), half_down(0.25)[0], OP.is_ge)
-            else:
-                mms(B(bk, 8, 8 + C), [(B("GRh"), nj(j))] + [(B("GRh"), B("eighth"))] * (A[t + 1] % 2) + more)
-                tt(B("bs%d%d" % (t + 1, h), 0, C), half_down(0.25 + A[t + 1] // 2 - 4)[0], B(bk, 8, 8 + C), OP.subtract)
-                k = send(B("bl%d%d" % (t + 1, h), 0, C), B("bs%d%d" % (t + 1, h), 0, C), (rank - 1) % N, "ab%d%d" % (t + 1, h), 4.0)
-                if t < 2 and h == 1:
-                    order_after(book(t + 3), k)
+        qb = lambda j: b("qb", j * C, (j + 1) * C)
+        bk = None
+        for x, (j0, j1) in enumerate(SETS):
+            cb = lease() if x else "Ppc%d" % h
+            clauses(t, h, x, cb)
+            if t + h + x == 0:
+                behind_first_clauses()
+            if PAR["jn"][h]:
+                j0, j1 = (0, 3) if j1 == 3 else (0, 0)
+            for j in range(j0, j0 if PAR["pk"] else j1):
+                early, late = [(B("I"), B("c192"))] + [(B("I64"), nj(0))] * (j - 1), [(B("GI"), nj(j - 1))]
+                if j == j0:
+                    o, all_, alone = B(cb, 3 * H, 3 * H + C), B(cb, 3 * H, 3 * H + (j1 - j0) * C), j1 - j0 == 1
+                    rows(all_, "SLh", "ge%d" % h, j0 * H, (j1 - j0) * H, early if j and alone else (), last=j == 0)
+                    if j:
+                        mms(o, late if alone else early + late, first=False)
+                else:
+                    o = cn(4, 5)
+                    mms(o, early + [(B("I"), b("cs", (j - j0 - 1) * C, (j - j0) * C))] + late)
+                if j:
+                    tt(nj(j), o, qb(j - 1), OP.is_gt if A[t] % 2 else OP.is_ge)
+                elif t == 0:
+                    tsc(nj(0), o, A[t] / 2.0 - 4, None, OP.is_ge)
+                else:
+                    tt(nj(0), o, B("bl%d%d" % (t, h), 0, C), OP.is_ge)
+                if j == j0 and j1 - j0 > 1:
+                    act(b("cs", 0, (j1 - j0 - 1) * C), B(cb, 3 * H + C, 3 * H + (j1 - j0) * C), AF.Copy)
+                if j < 2:
+                    bk = bk or lease()
+                    mm(B(bk, 0, C), B("GRh"), nj(j), True, True)
+                    act(qb(j), B(bk, 0, C), AF.Identity, 192.25 + A[t] // 2 - 4)
+            if not PAR["pk"]:
+                continue
+            if j1 > j0:
+                o = B(cb, 0, (j1 - j0) * H)
+                mm(o, B("BOh"), b("ge", j0 * H, j1 * H), True, True)
+                scan(b("cs", j0 * H, j1 * H), B("DPc", 0, (j1 - j0) * H), o, 0.0, OP.add, OP.max)
+            for j in range(j0, j1):
+                cs, ge = b("cs", j * H + 15, (j + 1) * H, 16), OP.is_gt if A[t] % 2 else OP.is_ge
+                if j == 0 and t == 0:
+                    tsc(nj(0), cs, B("th", 15, 16), None, OP.is_ge)
+                elif j == 0:
+                    tt(nj(0), cs, B("bl%d%d" % (t, h), 0, C), OP.is_ge)
+                elif j == 2 and PAR["tf"][h]:
+                    mms(cn(5, 6), [(B("nI"), B("c192")), (B("nI64"), nj(0)), (B("nGI"), nj(1)), (B("I"), qb(1))])
+                    tt(nj(j), cs, cn(5, 6), ge)
+                else:
+                    mms(cn(4, 5), [(B("I"), B("c192")), (B("I"), cs)] + [(B("I64"), nj(0))] * (j - 1) + [(B("GI"), nj(j - 1))])
+                    tt(nj(j), cn(4, 5), qb(j - 1), ge)
+                if j < 2:
+                    bk = bk or lease()
+                    mm(B(bk, 0, C), B("GRh"), nj(j), True, True)
+                    act(qb(j), B(bk, 0, C), AF.Identity, 192.25 + A[t] // 2 - 4)
+        sel = lambda a, e: B(bk, (1 + a) * C, (1 + e) * C)
+        part = lambda j: [(B(bk, 0, C), B("I%d" % (j + 1)), nj(j), False, False), (sel(0, 1), B("nI"), nj(j), False, False)]
+        run([(B(bk, 0, 5 * C), B("I"), b("CT", 0, 5 * C), True, False)] + part(0) + part(1))
+        run(part(2) + [(sel(1, 4), B("I"), b("nb"), False, True)])
+        tsc(b("bo"), B(bk, 0, C), row, None, OP.add)
+        gat(PAR["mg"], b("M"), B(Cb(t, h), ZO, CO + 3 * H), b("bo"))
+        stage("po", h, 1)
+        tt(b("pr", 0, 8 * C, 2), sel(0, 4), b("um", 3 * C, 7 * C), OP.mult)
+        tt(b("pr", 1, 8 * C, 2), sel(0, 4), b("K4"), OP.mult)
+        o = cn(6, 8)
+        mms(o, [(B("I"), b("CT", 5 * C, 7 * C))] + [(B("Iq"), b("pr", 2 * i * C, 2 * (i + 1) * C)) for i in range(4)])
+        cp(b("n16"), B("Ppc%d" % h, 3 * H + 6 * C, 3 * H + 8 * C, 2))
+        act(b("put"), o, AF.Copy)
+        if t < VIS - 1:
+            stage("uo", h, 1)
+            bk = lease()
+            mm(B(bk, 0, C), B("GRh"), nj(2), True, True)
+            act(qb(2), B(bk, 0, C), AF.Identity, 192.25)
+            mms(B(bk, 0, C), [(B("GRh"), nj(2)), (B("nI"), qb(2))])
+            act(B("bs%d%d" % (t + 1, h), 0, C), B(bk, 0, C), AF.Identity, B("th", 11 + t + 1, 12 + t + 1), -1.0)
+            k = send(B("bl%d%d" % (t + 1, h), 0, C), B("bs%d%d" % (t + 1, h), 0, C), (rank - 1) % N, "ab%d%d" % (t + 1, h), 4.0)
+            if t < 2 and h == 0:
+                chains["book"] = book(t + 3)
+                order_after(chains["book"], k)
+            elif t < 2:
+                order_after(k, chains["book"])
 
     def post(t, h):
         b = hb(h)
-        bk = lease()
-        mms(B(bk, 0, C), [(B("I"), b("pr", j * C, (j + 1) * C)) for j in range(4)] + [(B("I"), b("recb"))])
-        mms(B(bk, C, 2 * C), [(B("I"), b("pr", j * C, (j + 1) * C)) for j in range(4, 8)])
-        cp(b("n16"), B(bk, 0, C))
-        act(b("put"), B(bk, 0, 2 * C), AF.Copy)
         s = B("s", h, LA, 2)
-        bias[0] = PAR["b"]["su"][h]
+        stage("su", h)
         gtt(b("eq"), b("put"), B("TL"), B("KIL"), OP.is_equal)
         gtt(b("dd"), b("put"), B("TK"), s, OP.subtract)
-        tt(b("ed"), b("eq"), b("dd"), OP.mult)
-        tt(s, s, b("ed"), OP.add)
+        ed = B(lease(), 0, H) if PAR["ep"][h] else b("ed")
+        tt(ed, b("eq"), b("dd"), OP.mult)
+        tt(s, ed, s, OP.add)
         if t < VIS - 1:
             cp(b("s16"), s)
 
     def near(t, h):
         b, O = hb(h), Ob(t, h)
         cnt = B("Ppc%d" % h, 416, 416 + H)
-        test(t, h, b("M"), SN[h], OP.is_le, AF.Sign, -1.0, half, cnt)
-        act(b("nn"), cnt, AF.Relu, thn[h], -1.0)
+        test(t, h, b("M"), SN[t][h], OP.is_le, AF.Sign, -1.0, half, cnt)
+        act(b("nn"), cnt, AF.Relu, thr("n", SN[t][h]), -1.0)
+        stage("mx", h)
         last = ()
-        bias[0] = PAR["b"]["mx"][h]
-        for x in range(4):
+        if PAR["ob"][h]:
             bk = lease()
-            for a in range(4):
-                k = 4 * x + a
-                j = mm(B(bk, a * H, (a + 1) * H), B("R", 128 * k, 128 * k + 128), b("nn"), True, False, after=last)
-                mm(B(bk, a * H, (a + 1) * H), B("I"), B(O, k * H, (k + 1) * H), False, True)
-            last = (j,)
-            acc = lambda y: b("acc", 2 * y * H, (2 * y + 2) * H)
-            ps = lambda lo, hi: B(bk, lo * H, hi * H)
-            if x == 0:
-                for a in range(2):
-                    tt(b("acc", a * H, (a + 1) * H), ps(a, a + 1), b("M"), OP.max)
-                if PAR["a1"] == "S":
-                    act(acc(1), ps(2, 4), AF.Copy)
-                else:
-                    cp(acc(1), ps(2, 4))
-            elif x < 3:
-                for y in range(2):
-                    tt(acc(y), ps(2 * y, 2 * y + 2), acc(y), OP.max)
+            mms(B(bk, 0, H), [(B("I"), B("lane")), (B("I64"), b("nn"))])
+            mm(B(bk, BW, BW + H), B("I"), b("M"), True, True)
+            tsc(b("o2"), B(bk, 0, H), 64.0, r96, OP.mult, OP.add)
+            for x in range(3):
+                gat("V" if x < PAR["ob"][h] - 1 else "S", b("cmp", 512 * x, 512 * x + 512), B(O, -16, 16 * H), b("o2", 32 * x, 32 * x + 32))
+                scan(b("ac4", 512 * x, 512 * x + 512), B("rs16"), b("cmp", 512 * x, 512 * x + 512), 0.0, OP.mult, OP.max)
+            tt(b("cc"), B(bk, BW, BW + H), b("ac4", 15, 16 * H, 16), OP.max)
+        for x in range(0 if PAR["ob"][h] else 4):
+            bk = lease()
+            ms = [m for k in range(4 * x, 4 * x + 4) for m in terms(B(bk, k % 4, BW, 4), [(B("R", 128 * k, 128 * k + 128), b("nn")), (B("I"), B(O, k * H, (k + 1) * H))])]
+            last = (run(ms + [(B(bk, BW, BW + H), B("I"), b("M"), True, True)] * (x == 3), after=last),)
+            if x > 0:
+                for y in range(PAR["sp"][h]):
+                    w = BW // PAR["sp"][h]
+                    tt(b("acc", y * w, (y + 1) * w), B(bk, y * w, (y + 1) * w), b("acc", y * w, (y + 1) * w), OP.max)
+            elif PAR["a1"][h] == "S":
+                act(b("acc"), B(bk, 0, BW), AF.Relu)
             else:
-                tt(acc(0), ps(0, 2), acc(0), OP.max)
-                tt(ps(2, 4), ps(2, 4), acc(1), OP.max)
-                tt(b("acc", 2 * H, 3 * H), ps(2, 3), b("acc", 0, H), OP.max)
-                tt(ps(3, 4), ps(3, 4), b("acc", H, 2 * H), OP.max)
-                tt(b("cc"), ps(3, 4), b("acc", 2 * H, 3 * H), OP.max)
-        bias[0] = PAR["b"]["uc"][h]
-        o = B("Ppc%d" % h, 306, 306 + C)
-        rows(o, "SW0", "cc%d" % h, 0, H)
+                tsc(b("acc"), B(bk, 0, BW), 0.0, None, OP.max)
+        if not PAR["ob"][h]:
+            scan(b("ac4", 0, BW), B("rst"), b("acc"), 0.0, OP.mult, OP.max)
+            tt(b("cc"), B(bk, BW, BW + H), b("ac4", 3, BW, 4), OP.max)
+        stage("uc", h)
+        if PAR["pu"][h]:
+            mm(B("Ppc%d" % h, 0, H), B("BWs"), b("cc"), True, True)
+            scan(b("us"), B("DPu"), B("Ppc%d" % h, 0, H), 0.0, OP.add, OP.max)
+            o = b("us", 15, H, 16)
+        else:
+            o = B("Ppc%d" % h, 306, 306 + C)
+            rows(o, "SWs", "cc%d" % h, 0, H)
         ci = lambda a: b("ci", a * C, (a + 1) * C)
         hf = lambda a: b("hf", a * C, (a + 1) * C)
-        if PAR["sq"][h]:
-            tsc(ci(0), o, 1.0 / V, -0.5 + 0.5 / V, OP.mult, OP.add)
-            act(hf(2), o, AF.Identity, pf(7), 1.0 / V)
-            tt(hf(0), hf(2), ci(0), OP.subtract)
-            act(hf(1), hf(0), AF.Square, 0.0, V / 4.0)
-            tsc(ci(2), hf(1), 0.5, B("hk", t, t + 1), OP.mult, OP.add)
-        else:
-            cp(ci(0), o)
-            tsc(ci(1), ci(0), V - 1, None, OP.bitwise_and)
-            tsc(hf(0), ci(1), pf(6), None, OP.add)
-            tt(ci(2), hf(0), ci(1), OP.mult)
-        if PAR["sq"][h]:
-            tsc(ci(3), ci(2), V - 1, None, OP.bitwise_and)
-            cp(b("hc"), ci(3))
-        else:
-            tsc(ci(3), ci(2), 5, V - 1, OP.arith_shift_right, OP.bitwise_and)
-            tsc(b("hc"), ci(3), 97.0 * t, None, OP.add)
+        tsc(ci(0), o, -0.5 + 0.5 / V, None, OP.add)
+        tt(hf(0), o, ci(0), OP.subtract)
+        act(hf(1), hf(0), AF.Square, pf(7), V / 4.0)
+        tsc(ci(2), hf(1), 0.5, B("hk", t, t + 1), OP.mult, OP.add)
+        tsc(ci(3), ci(2), V - 1, None, OP.bitwise_and)
+        cp(b("hc"), ci(3))
         if t < VIS - 1 and PAR["df"][h]:
             gat("S", b("df"), B("CL"), b("hc"))
             o = B("Ppc%d" % h, 0, H)
             mms(o, ((B("nI"), b("cc")), (B("I"), b("df"))))
-            act(B(Cb(t + 1, h), 3 * H, 4 * H), o, AF.Abs)
+            act(B(Cb(t + 1, h), ZO, ZO + H), o, AF.Abs)
         elif t < VIS - 1:
             gtt(b("df"), B("CL"), b("hc"), b("cc"), OP.subtract)
-            act(B(Cb(t + 1, h), 3 * H, 4 * H), b("df"), AF.Abs)
+            act(B(Cb(t + 1, h), ZO, ZO + H), b("df"), AF.Abs)
         else:
             gtt(B("dfl", h * H, (h + 1) * H), B("CL"), b("hc"), b("cc"), OP.subtract)
 
     judge(1)
     for t in range(VIS):
-        got = []
+        got, bias[1] = [], t
         for h in range(2):
-            bias[0] = PAR["b"]["ga"][h]
+            stage("ga", h)
             got.append(gather(t, h))
-        bias[0] = PAR["b"]["em"][0]
+        stage("em")
         empties(t)
         for h in range(2):
-            bias[0] = PAR["b"]["op"][h]
+            stage("op", h)
             cands(t, h, got[h])
-            clauses(t, h)
             trials(t, h)
-            bias[0] = PAR["b"]["po"][h]
             post(t, h)
-        bias[0] = 0.0
+        stage("")
         if t < VIS - 1:
             judge(t + 2)
         for h in range(2):
-            bias[0] = PAR["b"]["po"][h]
+            stage("po", h)
             scat(B("X"), B("n16%d" % h), B("M%d" % h))
-            bias[0] = PAR["b"]["ne"][h]
+            stage("ne", h)
             near(t, h)
-        bias[0] = 0.0
+        stage("")
 
     stores = [dma("Y", D("yx", 0, W), B("X", 0, W), "dyx", 5.0)]
     bk = lease()
     for g2 in range(2):
-        for c2 in (1, 0):
-            mm(B(bk, g2 * H, g2 * H + H), B("PM%d%d" % (c2, g2)), B("s", c2, LA, 2), c2 == 1, c2 == 0, True)
+        mms(B(bk, g2 * H, g2 * H + H), [(B("PM%d%d" % (c2, g2)), B("s", c2, LA, 2)) for c2 in (1, 0)], f32=True)
     act(B("T3"), B(bk, 0, LA), AF.Copy)
     gat("S", B("T4"), B("T3"), B("Tout"))
     vtr(B("T5"), B("T4"))
@@ -685,38 +814,36 @@ def build(g, rank, T, topo, report=None):
     add("Rend", None, [], [B("zo")], 0.0, sem="-", amt=0, lat=0.0, after=stores)
     if not PLAN:
         PLAN.append(schedule(ops, leases, bank))
-    order, where, extra = PLAN[0]
+    order, where, extra, times = PLAN[0]
     for i, j in extra:
         ops[i]["deps"][j] = True
     for name, b in where.items():
         for r, p, step in leases[name]["regs"]:
             r[3] = view("Ppr%d" % b, p, r[1], r[2], step)
-    emit(g, T, ops, order, sent[0])
+    emit(g, T, ops, order, sent[0], times)
     if report is not None:
         report.append((ops, order))
 
 
 def place(ops, pred, succ, key):
-    left, est, start, busy = [len(p) for p in pred], [0.0] * len(ops), [0.0] * len(ops), {}
+    left, est, start, busy = [len(p) for p in pred], [0.0] * len(ops), [0.0] * len(ops), {o["eng"]: [] for o in ops}
     ready = sorted((key[i], i) for i in range(len(ops)) if left[i] == 0)
     while ready:
         i = ready.pop(0)[1]
         c, s = ops[i]["cost"], est[i]
-        q = busy.setdefault(ops[i]["eng"], [])
-        lo, hi = 0, len(q)
-        while lo < hi:
-            mid = (lo + hi) // 2
-            if q[mid][1] <= s:
-                lo = mid + 1
-            else:
-                hi = mid
-        while lo < len(q) and q[lo][0] < s + c:
-            s = max(s, q[lo][1])
+        q = busy[ops[i]["eng"]]
+        n = lo = len(q)
+        while lo and q[lo - 1][1] > s:
+            lo -= 1
+        while lo < n and q[lo][0] < s + c:
+            s = q[lo][1]
             lo += 1
-        q.insert(lo, (s, s + c))
+        e = s + c
+        q.insert(lo, (s, e))
         start[i] = s
         for k, lat in succ[i]:
-            est[k] = max(est[k], s + c + lat)
+            if e + lat > est[k]:
+                est[k] = e + lat
             left[k] -= 1
             if left[k] == 0:
                 x = (key[k], k)
@@ -724,12 +851,21 @@ def place(ops, pred, succ, key):
                 while at and ready[at - 1] > x:
                     at -= 1
                 ready.insert(at, x)
-    return start, max(start[i] + ops[i]["cost"] + ops[i]["lat"] for i in range(len(ops)))
+    return start, 0.0
 
 
 def schedule(ops, leases, bank):
     n = len(ops)
-    pred, succ, tail = [[] for _ in range(n)], [[] for _ in range(n)], [0.0] * n
+    price = lambda c, k, ga, sc, wake, pe, least: c[0] + CY * k * (c[1] + ga * c[2] + sc * c[3] + pe * sum(max(least, x) for x in c[4:]))
+    ops = [dict(o, cost=price(o["cost"], *PAR["pace"][0]), lat=PAR["pace"][0][3] if o["lat"] is None else o["lat"], raw=o) for o in ops]
+    pred, succ, tail, done = [[] for _ in range(n)], [[] for _ in range(n)], [0.0] * n, [0] * n
+    for i, o in enumerate(ops):
+        held = [j for j, w in o["deps"].items() if w or o["eng"][0] == "R" or ops[j]["eng"] == o["eng"]]
+        for j in held:
+            done[i] |= done[j]
+        o["deps"] = {j: w for j, w in o["deps"].items() if not done[i] >> j & 1}
+        for j in held:
+            done[i] |= int(o["raw"]["deps"][j] or o["eng"][0] == "R") << j
     for i, o in enumerate(ops):
         for j, w in o["deps"].items():
             lat = ops[j]["lat"] if w or ops[j]["eng"] != o["eng"] else 0.0
@@ -737,30 +873,170 @@ def schedule(ops, leases, bank):
             succ[j].append((i, lat))
     for i in range(n - 1, -1, -1):
         tail[i] = ops[i]["cost"] + max([tail[k] + lat for k, lat in succ[i]] + [ops[i]["lat"]])
+    plain, eng = [], [o["eng"] for o in ops]
+    for pace in PAR["pace"]:
+        lat = [pace[3] if o["raw"]["lat"] is None else o["lat"] for o in ops]
+        waits = [[(j, lat[j] if w or o["eng"][0] == "R" else 0.0) for j, w in o["deps"].items() if w or o["eng"][0] == "R" or ops[j]["eng"] == o["eng"]] for o in ops]
+        plain.append(([price(o["raw"]["cost"], *pace) for o in ops], waits, lat))
+
+    def with_banks(extra):
+        out = []
+        for cost, waits, lat in plain:
+            waits = list(waits)
+            for i, j in extra:
+                waits[i] = waits[i] + [(j, lat[j])]
+            out.append((cost, waits))
+        return out
     key, best, rng = [-tail[i] - ops[i]["bias"] for i in range(n)], None, np.random.default_rng(PAR["seed"])
+    names = sorted(set(o["stage"] for o in ops))
+    kind = [names.index(o["stage"]) for o in ops]
     for x in range(PAR["passes"]):
         start, end = place(ops, pred, succ, key)
         got = banks(ops, leases, bank, pred, succ, start)
-        if best is None or got[0] <= best[0][0]:
-            best = (got, start)
-        start = best[1] if x >= 2 else start
-        shift = rng.normal(0.0, (0.2, 0.5, 1.0, 2.0)[x % 4], max(o["stage"] for o in ops) + 1) * (x >= 2)
-        back, _e = place(ops, succ, pred, [-(start[i] + ops[i]["cost"] + shift[ops[i]["stage"]]) for i in range(n)])
+        worth = 1e9
+        if best is None or got[0] < best[1][0] + PAR["cut"]:
+            worth = sum(replay(eng, c, w, got[1])[0][-1] / p[0] for (c, w), p in zip(with_banks(got[3]), PAR["pace"]))
+        if best is None or worth <= best[0] + PAR["warm"] * rng.random():
+            best = (worth, got, start)
+            if x == 0 or worth < top[0]:
+                top = best
+        start = best[2] if x >= 2 else start
+        shift = rng.normal(0.0, PAR["noise"][0], len(names)) * (rng.random(len(names)) < PAR["noise"][1]) * (x >= 2)
+        if x >= 2 and rng.random() < PAR["noise"][2]:
+            key = [start[i] + shift[kind[i]] for i in range(n)]
+            continue
+        back, _e = place(ops, succ, pred, [-(start[i] + ops[i]["cost"] + shift[kind[i]]) for i in range(n)])
         key = [-(back[i] + ops[i]["cost"]) for i in range(n)]
-    PAR["ideal"] = (end, best[0][0], max(tail))
-    return best[0][1:]
+    best = top[1]
+    _end, order, where, extra = best
+    paces = with_banks(extra)
+    before, behind = [set(o["deps"]) for o in ops], [set() for o in ops]
+    for i, j in extra:
+        before[i].add(j)
+    for i in range(n):
+        for j in before[i]:
+            behind[j].add(i)
+    same, seen = {}, {}
+    for i, o in enumerate(ops):
+        k = (o["eng"], o["lab"].replace("b", "a"), o["visit"])
+        seen[k] = seen.get(k, 0) + 1
+        o["twin"] = (k[0], k[1], seen[k])
+        same.setdefault(o["twin"], []).append(i)
+    order, ends = polish(eng, paces, before, behind, order, [same[o["twin"]] for o in ops])
+    PAR["ideal"] = (end, best[0], max(tail), ends)
+    PAR["dbg"] = (ops, paces, order, before)
+    times = [(replay(eng, c, w, order)[0], c) for c, w in paces]
+    order.sort(key=lambda i: 0)
+    return order, where, extra, times
+
+
+def replay(eng, cost, waits, order):
+    end, by, last = [0.0] * len(eng), [-1] * len(eng), {}
+    for i in order:
+        j = last.get(eng[i], -1)
+        s = end[j] if j >= 0 else 0.0
+        for k, lat in waits[i]:
+            if end[k] + lat > s:
+                s, j = end[k] + lat, k
+        end[i], by[i], last[eng[i]] = s + cost[i], j, i
+    return end, by
+
+
+def in_order(key, before, behind):
+    left, out = [len(p) for p in before], []
+    late = [False] * len(key)
+    for i in sorted(range(len(key)), key=lambda j: key[j]):
+        late[i] = True
+        todo = [i] if left[i] == 0 else []
+        while todo:
+            j = todo.pop()
+            out.append(j)
+            for k in behind[j]:
+                left[k] -= 1
+                if left[k] == 0 and late[k]:
+                    todo.append(k)
+    return out
+
+
+def polish(eng, paces, before, behind, order, twins):
+    rng, tip = np.random.default_rng(PAR["seed"]), eng.index("Rend")
+    got = [replay(eng, c, w, order) for c, w in paces]
+    first = [e[tip] for e, by in got]
+    worth = lambda g: sum((e[tip] + PAR["soon"] * sum(e) / len(e)) / f for (e, by), f in zip(g, first))
+    now = worth(got)
+    for x in range(PAR["moves"]):
+        end, by = got[x % len(paces)]
+        pairs, i = [], tip
+        while by[i] >= 0:
+            if eng[by[i]] == eng[i] and by[i] not in before[i]:
+                pairs.append((by[i], i))
+            i = by[i]
+        if not pairs:
+            break
+        a, b = pairs[int(rng.integers(len(pairs)))]
+        pa, pb = order.index(a), order.index(b)
+        far = int(rng.integers(3))
+        if rng.random() < PAR["wide"]:
+            cost, up = paces[x % len(paces)][0], rng.random() < 0.5
+            key = [e - c for e, c in zip(end, cost)]
+            span, step = 4.0 * rng.random(), 0.2 + 2.0 * rng.random() ** 2
+            todo = list(twins[b if up else a]) if rng.random() < 0.6 else [b if up else a]
+            move = {i: key[i] for i in todo}
+            while todo:
+                i = todo.pop()
+                for j in (before if up else behind)[i]:
+                    if j not in move and abs(key[j] - move[i]) < span:
+                        move[j] = move[i]
+                        todo.append(j)
+            for i in move:
+                key[i] += -step if up else step
+            new = in_order(key, before, behind)
+        elif x // len(paces) % 2:
+            while far and pa > 0:
+                pa -= 1
+                far -= eng[order[pa]] == eng[b]
+            a, move = order[pa], {b}
+            for i in reversed(order[pa:pb]):
+                if behind[i] & move:
+                    move.add(i)
+            if a in move:
+                continue
+            new = order[:pa] + [i for i in order[pa:pb + 1] if i in move] + [i for i in order[pa:pb + 1] if i not in move] + order[pb + 1:]
+        else:
+            while far and pb < len(order) - 1:
+                pb += 1
+                far -= eng[order[pb]] == eng[a]
+            b, move = order[pb], {a}
+            for i in order[pa + 1:pb + 1]:
+                if before[i] & move:
+                    move.add(i)
+            if b in move:
+                continue
+            new = order[:pa] + [i for i in order[pa:pb + 1] if i not in move] + [i for i in order[pa:pb + 1] if i in move] + order[pb + 1:]
+        trial = [replay(eng, c, w, new) for c, w in paces]
+        if worth(trial) <= now + PAR["heat"] * (1 - x / PAR["moves"]) * rng.random():
+            order, got, now = new, trial, worth(trial)
+    return order, [round(e[tip], 1) for e, by in got]
 
 
 def banks(ops, leases, bank, pred, succ, start):
     n = len(ops)
     left, free, est, where, extra = [len(p) for p in pred], {}, [0.0] * n, {}, []
     holder, since, todo = [None] * PAR["nr"], [0.0] * PAR["nr"], {l: len(x["ops"]) for l, x in leases.items()}
-    ready, order = [i for i in range(n) if left[i] == 0], []
-    while ready:
-        idle = [b for b, l in enumerate(holder) if l is None or todo[l] == 0]
-        i = min((start[i], i) for i in ready if idle or ops[i]["lease"] is None or ops[i]["lease"] in where)[1]
+    rest, order = sorted(range(n), key=lambda i: (-start[i], -i)), []
+    while rest:
+        at, idle = len(rest) - 1, None
+        while True:
+            i = rest[at]
+            l = ops[i]["lease"]
+            if left[i] == 0 and l is not None and l not in where and idle is None:
+                idle = [b for b, x in enumerate(holder) if x is None or todo[x] == 0]
+            if left[i] == 0 and (l is None or l in where or idle):
+                break
+            at -= 1
+        del rest[at]
         o = ops[i]
-        s, l = max(free.get(o["eng"], 0.0), est[i]), o["lease"]
+        s = max(free.get(o["eng"], 0.0), est[i])
         if l is not None and l not in where:
             b = min(idle, key=lambda x: since[x])
             s = max(s, since[b])
@@ -772,23 +1048,21 @@ def banks(ops, leases, bank, pred, succ, start):
             todo[l] -= 1
             since[where[l]] = max(since[where[l]], end + o["lat"])
         order.append(i)
-        ready.remove(i)
         for k, lat in succ[i]:
-            est[k] = max(est[k], end + lat)
+            if end + lat > est[k]:
+                est[k] = end + lat
             left[k] -= 1
-            if left[k] == 0:
-                ready.append(k)
     return max(free.values()), order, where, extra
 
 
-def emit(g, T, ops, order, nsent):
+def emit(g, T, ops, order, nsent, times):
     queue = {"V": g.vector, "S": g.scalar, "P": g.tensor, "G": g, "Y": g.sync}
     need = set()
     for o in ops:
         for j, w in o["deps"].items():
             if w:
                 need.add(j)
-    total, mark, know, snap = {}, {}, {}, {}
+    total, mark, marks, know, snap = {}, {}, {}, {}, {}
     for i in order:
         o = ops[i]
         e = o["eng"]
@@ -810,6 +1084,8 @@ def emit(g, T, ops, order, nsent):
             if any(s2 != s and snap[want[s2][1]].get(s, 0) >= want[s][0] for s2 in want):
                 del want[s]
         for s, (v, j) in want.items():
+            while s in marks and v < len(marks[s]) and all(end[marks[s][v]] + PAR["spare"] <= end[i] - cost[i] for end, cost in times):
+                v, j = v + 1, marks[s][v]
             queue[e].wait_ge(T.sem[s], v)
             k[s] = max(k.get(s, 0), v)
             for s2, v2 in snap[j].items():
@@ -826,6 +1102,7 @@ def emit(g, T, ops, order, nsent):
             ins.then_inc(T.sem[s], 1)
             total[s] = total.get(s, 0) + 1
             mark[i] = (s, total[s])
+            marks.setdefault(s, []).append(i)
         else:
             continue
         snap[i] = dict(k)

import numpy as np
from concourse.bass import DstId, RemoteDMATransfer
from concourse.mybir import AluOpType as OP, ActivationFunctionType as AF

N, LA, W, V, VIS = 8, 192, 3072, 4096, 4
A = [6, 4, 4, 3]
ZB = 3072
H, C = 96, 6
BW = 4 * H
PAR = {"so": [2, 2], "sn": [1, 1], "m0": [11, 12, 0, 11, 12, 0], "gv": [1, 1], "gv0": [2, 2], "so0": [2, 2], "sn3": [2, 2],
       "a1": ["S", "S"], "df": [0, 0], "pu": [0, 0], "pk": 1, "tf": [1, 1], "mg": "S", "z3": [1, 1], "nd": [2, 4, 4], "sd": [2, 5, 5], "f1": [1, 0, 0], "mc": [2, 0, 0, 2, 0, 0], "ob": [1, 0], "jn": [0, 0], "sp": [1, 2], "sh": 0.0, "mu": [0, 1], "ep": [1, 0], "nr": 6, "xat": 2,
       "passes": 2500, "seed": 5, "moves": 1500, "heat": 0.0, "cut": 1.5, "land": 5.0, "call": 1.4, "pe": 0.6, "spare": 99.0, "soon": 0.5, "noise": [2.5, 0.04, 0.2], "wide": 0.5, "warm": 0.6, "pace": [(1.0, 1.5, 3.5, 0.21, 0.53, 64), (1.0, 1.2, 3.5, 0.15, 0.6, 48), (1.25, 1.95, 3.5, 0.16, 0.55, 64)],
       "b": {"ga": [-5, 18], "ca": [26, 2], "cl": [-6, -16], "tr": [-10, 4], "po": [14, 15], "ne": [-15, -2], "op": [10, 13], "ha": [6, 3], "uo": [1, -25], "su": [-13, -9], "mx": [-12, -9], "uc": [12, 10], "em": [-10, -8], "x1": [0, 0], "x2": [0, 0]}}
ZO, CO, RO = 2 * H, 3 * H, 12 * H
SETS = ((0, 2), (2, 3))
CY = 0.00083
PLAN = []
CORES = [3, 11, 19, 27, 35, 43, 51, 59]
CUT = V // 2 + 448
VX = V + 304
MID = (CUT + V) // 2
PIECES = ((CUT, MID), (0, CUT // 3), (MID, V), (CUT // 3, 2 * CUT // 3), (2 * CUT // 3, CUT), (V, VX))

SCRATCH = {}
_two = lambda l: tuple((n + str(h), c) for n, c in l for h in range(2))
for _t, _l in (
        ("bfloat16", (("X", W + 16), ("CL", VX), ("zl", LA), ("zo", LA), ("dfl", LA), ("d", 160), ("ch", 128), ("cl16", 128), ("DPc", 3 * H), ("ph", 3 * H), ("mh", 3 * C), ("I4k", 128), ("DPu", H), ("BOh", 128), ("BWs", 128), ("nI64", 128), ("nGI", 128), ("neg", 512), ("one", 512), ("ln0", H), ("R", 2048), ("I", 128), ("nI", 128),
                      ("I64", 128), ("I3", 128), ("I2", 128), ("I1", 128), ("In", 128), ("SL", 144), ("SLL", 144), ("SLh", 144), ("BO", 128), ("GR", 128), ("GRh", 128), ("GI", 128), ("c192", C), ("cK", 12), ("em", 24), ("Iq", 128), ("SWn", 144), ("SWs", 144),
                      ("Tg", 128), ("Tr0", 128), ("Tr1", 128), ("Tr2", 128), ("Tri", 128), ("c8", 3 * C), ("rst", BW), ("rs16", 512), ("lane", H), ("kpd", 16), ("DX", 48 * C), ("DK", 48 * C))
         + _two((("Oa", 17 * H), ("Ob", 17 * H), ("Ca", RO + 8 * H), ("Cb", RO + 8 * H), ("cmp", 16 * H), ("op", H), ("le", 3 * H), ("G", 48 * H), ("SG", 3 * 512),
                 ("ge", 3 * H), ("nb", 3 * C), ("CT", 7 * C), ("cs", 3 * H), ("qb", 3 * C), ("K4", 4 * C), ("pr", 8 * C), ("M", H), ("nn", H), ("acc", BW), ("ac4", 16 * H), ("cc", H), ("df", H), ("eq", H)))),
        ("float32", (("PM00", 128), ("PM01", 128), ("PM10", 128), ("PM11", 128), ("pf", 8), ("pg", 16), ("hk", 8), ("th", 16), ("c16", 3 * C), ("LI3f", 3 * C), ("KIL", H), ("KI0", H),
                     ("sae", LA), ("T1", LA), ("T2", LA), ("T3", LA), ("T4", LA), ("T5", LA), ("T6", LA), ("T7", LA), ("s", LA), ("mx", 17 * 12), ("lf", 24))
         + _two((("KU", 48 * C), ("put", 2 * C), ("dd", H), ("ed", H), ("hf", 3 * C), ("us", H)))),
        ("float16", _two((("uh", 3 * C),))),
        ("int32", (("pc", 4), ("sln", LA), ("li", 36))
         + _two((("ui", 7 * C), ("um", 7 * C), ("Hs", 48 * C), ("Hm", 48 * C), ("ci", 4 * C)))),
        ("uint16", (("TW0", 3 * C), ("TW1", 3 * C), ("TW2", 3 * C), ("TK", C), ("TL", C), ("Tin", 12), ("Tout", 12), ("Tz", 12))
         + _two((("Tzi", C), ("off", 3 * C), ("ho", 48 * C), ("bo", C), ("hc", C), ("s16", H), ("n16", C), ("o2", H))))):
    for _n, _c in _l:
        SCRATCH[_n] = ("sbuf", [128, _c], _t)
for _q in range(1, 5):
    SCRATCH["BK%d" % _q] = ("sbuf", [128, VX], "bfloat16")
    SCRATCH["KX%d" % _q] = ("sbuf", [128, 48 * C], "float32")
SCRATCH["WK0"] = ("sbuf", [128, 4], "int32")
for _q in range(5):
    SCRATCH["WF%d" % _q] = ("sbuf", [128, 4], "float32")
    SCRATCH["SW%d" % _q] = ("sbuf", [128, 144], "bfloat16")
for _t in range(1, VIS):
    for _h in range(2):
        SCRATCH["bs%d%d" % (_t, _h)] = ("sbuf", [128, 8], "float32")
        SCRATCH["bl%d%d" % (_t, _h)] = ("sbuf", [128, 8], "float32")
for _n in ["pc0", "pc1"] + ["pr%d" % _b for _b in range(6)]:
    SCRATCH["P" + _n] = ("psum", [128, 512], "float32")
OWN = ("X", "CL", "zl", "zo", "sln", "wti", "kpi", "T7", "WK", "WF", "BK", "bs", "bl", "Ppc", "Ppr")
LOGICAL, PLACE, _at = dict(SCRATCH), {}, {}
for _n, (_w, _s, _d) in list(SCRATCH.items()):
    if _n.rstrip("0123456789") in OWN or _n in OWN:
        continue
    _p = "pool_" + _d
    _u = 16 if _d in ("float32", "int32") else 32
    _pad = _u if _n[0] == "O" or _n == "I" else 0
    PLACE[_n] = (_p, _at.get(_p, 0) + _pad)
    _at[_p] = (PLACE[_n][1] + _s[1] + _pad + _u - 1) // _u * _u
    del SCRATCH[_n]
for _p in _at:
    SCRATCH[_p] = ("sbuf", [128, _at[_p]], _p[5:])

SEMAPHORES = ["eV", "eS", "eP", "eG", "sent", "dsl", "dx", "dz", "dwt", "dkp", "dyx", "dyl", "dyz"]
SEMAPHORES += ["dc%d" % a for a in range(6)] + ["aC%d" % a for a in range(6)] + ["aH%d%d" % (q, a) for q in range(1, 5) for a in range(6)]
SEMAPHORES += ["aB%d" % q for q in range(2, 5)] + ["aW%d" % q for q in range(1, 5)] + ["ab%d%d" % (t, h) for t in range(1, VIS) for h in range(2)]


def helper(topo, core):
    mate = [c for c in CORES if topo.mates(topo.chip(core), topo.chip(c))][0]
    return [c for c in topo.cores_of(core) if topo.die(c) != topo.die(core) and topo.may_write(c, mate)][0]


def rank_program(g, core, T, topo):
    rank = T.rank_of(core)
    if rank is not None:
        return build(g, rank, T, topo)
    for rank, home in enumerate(T.cores):
        if helper(topo, home) == core and CUT < V:
            hand_on(g, rank, core, T, topo)


def hand_on(g, rank, core, T, topo):
    home, sent = T.cores[rank], 0
    far = topo.engines(home, T.cores[(rank - 1) % N])
    n = len([x for x in topo.engines(home, core) if x not in far])
    for q in range(1, 5):
        dst = T.cores[(rank - q) % N]
        rid, pid, _se = topo.addr(dst)
        for a, (lo, hi) in enumerate(PIECES):
            if lo >= CUT and (q > 1 or lo < V):
                if q == 1 + (lo >= V):
                    g.wait_ge(T.sem["aC%d" % a], n)
                g.remote_dma(out_ap=T["BK%d" % q][:, lo:hi], in_ap=T.CL[:, lo:hi], remote_sem=T.sem["aH%d%d" % (q, a)], local_sem=T.sem.sent, pid=pid, routing_id=rid,
                             dma_engine_mask=topo.mask(core, dst))
                sent += len(topo.engines(core, dst))
    g.wait_ge(T.sem.sent, sent)


def build(g, rank, T, topo, report=None):
    ops, wr, rd, bank, leases, chains, bias = [], {}, {}, {}, {}, {}, [(0.0, ""), -1]

    def stage(name, h=0, x=0):
        bias[0] = (PAR["b"][name][h] if name else 0.0, "%s%d%d" % (name, h, x))

    def view(buf, p, a, b, step):
        return T[buf][p[0]:p[1], a:b] if step == 1 else T[buf][p[0]:p[1], a:b:step]

    def B(name, lo=0, hi=None, step=1, p=(0, 128)):
        if name in leases:
            r = [name, lo, hi, None, (hi - lo + step - 1) // step]
            leases[name]["regs"].append((r, p, step))
            return r
        if hi is None:
            hi = LOGICAL[name][1][1]
        buf, at = PLACE.get(name, (name, 0))
        return [name, lo, hi, view(buf, p, at + lo, at + hi, step), (hi - lo + step - 1) // step]

    def lease():
        name = "P#%d" % len(leases)
        leases[name] = {"regs": [], "ops": []}
        return name

    def add(eng, call, outs, ins, cost, sem=None, amt=1, lat=None, after=()):
        i, deps, mine = len(ops), {}, None

        def dep(j, wait):
            if j != i:
                deps[j] = deps.get(j, False) or wait
        for reg, isw in [(r, False) for r in ins] + [(r, True) for r in outs]:
            name, lo, hi = reg[0], reg[1], reg[2]
            psum = name[0] == "P" and name[1] in "p#"
            for (a, b, j) in wr.get(name, []):
                if a < hi and lo < b:
                    dep(j, not (psum and eng == "P" and ops[j]["eng"] == "P"))
            if isw:
                for (a, b, j) in rd.get(name, []):
                    if a < hi and lo < b:
                        dep(j, True)
            if psum:
                e, run, prev = bank.setdefault(name, (eng, [], []))
                if e != eng:
                    e, run, prev = bank[name] = (eng, [], run)
                for j in prev:
                    dep(j, True)
                if eng == "P" and run:
                    dep(run[-1], False)
                if i not in run:
                    run.append(i)
                if name in leases and i not in leases[name]["ops"]:
                    leases[name]["ops"].append(i)
                    mine = name
        for j in after:
            dep(j, False)
        for reg in ins:
            rd.setdefault(reg[0], []).append((reg[1], reg[2], i))
        for reg in outs:
            name, lo, hi = reg[0], reg[1], reg[2]
            if reg[4] == hi - lo:
                wr[name] = [x for x in wr.get(name, []) if not (lo <= x[0] and x[1] <= hi)]
                rd[name] = [x for x in rd.get(name, []) if not (lo <= x[0] and x[1] <= hi)]
            wr.setdefault(name, []).append((lo, hi, i))
        ops.append({"eng": eng, "call": call, "deps": deps, "cost": cost if isinstance(cost, tuple) else (cost, 0, 0, 0), "sem": sem, "amt": amt, "lat": lat, "lease": mine,
                    "bias": bias[0][0], "stage": bias[0][1] + eng[0], "visit": bias[1], "lab": [r[0] for r in outs + ins if r[0] not in leases][0]})
        return i

    def order_after(i, j):
        ops[i]["deps"].setdefault(j, False)

    def chain(name, i):
        if name in chains:
            order_after(i, chains[name])
        ops[i]["prev"] = chains.get(name, 0)
        chains[name] = i
        return i

    def two(*rs):
        return all(r[0] in LOGICAL and LOGICAL[r[0]][2] in ("bfloat16", "uint16") for r in rs)

    def psum(r):
        return r[0] not in LOGICAL or LOGICAL[r[0]][0] == "psum"

    def cyc(n):
        return (0.02, max(64, n), 0, 0)

    val = lambda s: s[3] if isinstance(s, list) else s

    def cp(o, i):
        return add("V", lambda: g.vector.tensor_copy(o[3], i[3]), [o], [i], cyc(i[4] * (0.5 if two(o, i) else 1)))

    def tt(o, a, b, op):
        return add("V", lambda: g.vector.tensor_tensor(o[3], a[3], b[3], op), [o], [a, b], cyc(a[4] if psum(a) or psum(b) else 2 * a[4]))

    def tsc(o, i, s1, s2, op0, op1=None):
        ins = [i] + [s for s in (s1, s2) if isinstance(s, list)]
        if op1 is None:
            f = lambda: g.vector.tensor_scalar(o[3], i[3], val(s1), None, op0)
        else:
            f = lambda: g.vector.tensor_scalar(o[3], i[3], val(s1), val(s2), op0, op1)
        return add("V", f, [o], ins, cyc(i[4] * (0.5 if two(o, i) else 1)))

    def gtt(o, w, off, b, op):
        return add("V", lambda: g.vector.tensor_tensor(o[3], w[3].indirect(off[3]), b[3], op), [o], [w, off, b], (0.05, 0, o[4], 0))

    def scat(w, off, i):
        return add("V", lambda: g.vector.tensor_copy(w[3].indirect(off[3]), i[3]), [[w[0], w[1], w[2], w[3], -1]], [off, i], (0.05, 0, 0, i[4]))

    def mem(o, c):
        return add("V", lambda: g.vector.memset(o[3], c), [o], [], cyc(o[4] * 0.5))

    def scan(o, a, b, init, op0, op1):
        return add("V", lambda: g.vector.tensor_tensor_scan(o[3], a[3], b[3], init, op0, op1), [o], [a, b], cyc(a[4] * (0.5 if two(o, a, b) else 1)))

    def vtr(o, i):
        return add("V", lambda: g.vector.transpose(o[3], i[3]), [o], [i], cyc(i[4]))

    def act(o, i, f, bias=0.0, scale=1.0):
        ins = [i] + [s for s in (bias, scale) if isinstance(s, list)]
        return add("S", lambda: g.scalar.activation(o[3], i[3], f, bias=val(bias), scale=val(scale)), [o], ins, (0.05, max(64, i[4]), 0, 0))

    def gat(e, o, w, off, f=AF.Copy):
        if e == "V":
            return add("V", lambda: g.vector.tensor_copy(o[3], w[3].indirect(off[3])), [o], [w, off], (0.05, 0, o[4], 0))
        return add("S", lambda: g.scalar.activation(o[3], w[3].indirect(off[3]), f), [o], [w, off], (0.065, 0, o[4], 0))

    def run(ms, f32=False, after=()):
        return add("P", lambda: [g.tensor.matmul(o[3], l[3], r[3], a, e) for o, l, r, a, e in ms][-1], [m[0] for m in ms], [x for m in ms for x in m[1:3]],
                   (0.0, 0, 0, 0) + tuple(m[2][4] for m in ms) * (4 if f32 else 1), after=after)

    def mm(o, l, r, start, stop, after=()):
        return run([(o, l, r, start, stop)], after=after)

    def terms(o, ts, first=True, last=True):
        return [(o, l, r, first and x == 0, last and x == len(ts) - 1) for x, (l, r) in enumerate(ts)]

    def mms(o, ts, first=True, last=True, f32=False, after=()):
        return run(terms(o, ts, first, last), f32, after)

    E = lambda r, nm="SL": B(nm, 15 - r, 143 - r)

    def rows(o, nm, src, lo, width, extra=(), first=True, last=True, step=1):
        mms(o, list(extra) + [(E(r, nm), B(src, lo + r * step, lo + (width - 1) * step + 1, 16 * step)) for r in range(16)], first, last)

    def dma(q, o, i, sem, us):
        eng = {"Y": g.sync, "S": g.scalar}[q]
        return chain("d" + q, add(q, lambda: eng.dma_start(o[3], i[3]), [o] if o[0] in LOGICAL else [], [i], 0.06, sem=sem, amt=16, lat=us))

    def D(name, lo, hi):
        return [name, lo, hi, T[name][:, lo:hi] if hi - lo < T[name].shape[1] else T[name][:], hi - lo]

    sent = [0]

    def landed(j, o, sem, n, us):
        sent[0] += n
        add("R" + sem, None, [o], [], 0.0, sem=sem, amt=n, lat=us, after=(j,))

    def send(o, i, dst, sem, us):
        src_core, dst_core = T.cores[rank], T.cores[dst]
        m, n = topo.mask(src_core, dst_core), len(topo.engines(src_core, dst_core))
        rid, pid, _se = topo.addr(dst_core)
        j = add("G", lambda: g.remote_dma(out_ap=o[3], in_ap=i[3], remote_sem=T.sem[sem], local_sem=T.sem.sent, pid=pid, routing_id=rid, dma_engine_mask=m),
                [], [i], PAR["call"], sem="-", amt=0)
        landed(j, o, sem, n, us)
        return j

    me = T.cores[rank]

    def hand(i, a):
        far = topo.engines(me, T.cores[(rank - 1) % N])
        es = [x for x in topo.engines(me, helper(topo, me)) if x not in far]
        rid, pid, _se = topo.addr(helper(topo, me))
        sent[0] += len(es)
        return add("G", lambda: g.remote_dma(out_ap=i[3], in_ap=i[3], remote_sem=T.sem["aC%d" % a], local_sem=T.sem.sent, pid=pid, routing_id=rid,
                                             dma_engine_mask=sum(1 << x for x in es)), [], [i], PAR["call"], sem="-", amt=0)

    def send_each(i, jobs, us):
        tr, cnt = [], []
        for x, (o, dst, sem) in enumerate(jobs):
            es = topo.engines(T.cores[rank], T.cores[dst])
            k = len(es) // len(jobs)
            rid, pid, _se = topo.addr(T.cores[dst])
            tr.append(RemoteDMATransfer(dst_ids=[DstId(rid=rid, pnc=pid)], dma_engine_mask=sum(1 << e for e in es[x * k:x * k + k]), remote_sem=T.sem[sem], src=i[3], dst=o[3]))
            cnt.append(k)
        j = add("G", lambda: g.remote_dma_fused(tr, local_sem=T.sem.sent), [], [i], 2 * PAR["call"], sem="-", amt=0)
        for (o, dst, sem), k in zip(jobs, cnt):
            landed(j, o, sem, k, us)
        return j

    def asel(o, i, pat, cop, fill, base, cmul):
        return add("G", lambda: g.affine_select(o[3], i[3], pat, cop, fill, base, cmul), [o], [i], (0.17, 2 * o[4], 0, 0))

    def gcopy(o, i):
        return asel(o, i, [[0, o[4]]], OP.is_ge, 0.0, 0, 0)

    def scopy(o, i):
        return act(o, i, AF.Copy)

    def iota(o, pat, base, cmul):
        if LOGICAL[o[0]][2] == "int32":
            f = lambda: g.iota(o[3], pat, base, cmul)
        else:
            f = lambda: g.iota(o[3], pat, base, cmul, allow_small_or_imprecise_dtypes=True)
        j = add("G", f, [o], [], (0.13, 2 * o[4], 0, 0))
        return j if sent[0] else chain("G", j)

    M0 = [[PAR["m0"][3 * h:3 * h + 3] for h in range(2)]] * VIS
    ring = [0, 0]
    SO = [PAR["so0"]] + [PAR["so"]] * 3
    SN = [PAR["sn"]] * 3 + [PAR["sn3"]]

    dma("Y", B("sln"), D("sl", 0, LA), "dsl", 2.0)
    dma("S", B("WK0", 1, 2), D("kp", 0, 1), "dkp", 2.0)
    dma("S", B("WK0", 0, 1), D("wt", 0, 1), "dwt", 2.0)
    dma("S", B("zl"), D("z0", 0, LA), "dz", 2.2)
    for a, (lo, hi) in enumerate(PIECES):
        if a == PAR["xat"]:
            dma("Y", B("X", 0, W), D("x0", 0, W), "dx", 4.3 + 0.8 * a)
        dma("Y", B("CL", lo, hi), D("cl", lo % V, lo % V + hi - lo), "dc%d" % a, 2.5 + 0.8 * a + (3.0 if a >= PAR["xat"] else 0.0))

    iota(B("pc", 0, 1), [[0, 1]], 0, 1)
    iota(B("d"), [[1, 160]], -16, -1)
    iota(B("c16"), [[16, 3 * C]], 0, 0)
    iota(B("ch"), [[1, 8], [0, 16]], 0, 0)
    iota(B("cl16"), [[0, 8], [1, 16]], 0, 0)
    for j0, j1 in SETS:
        iota(B("DX", 16 * C * j0, 16 * C * j1), [[1, 16], [0, (j1 - j0) * C]], 0, 0)
    pc, pf, pg = (lambda a: B("pc", a, a + 1)), (lambda a: B("pf", a, a + 1)), (lambda a: B("pg", a, a + 1))
    tsc(pc(1), pc(0), 15, None, OP.bitwise_and)
    tsc(pc(2), pc(0), 4, None, OP.arith_shift_right)
    tsc(pc(3), pc(0), 4, 1, OP.arith_shift_right, OP.bitwise_and)
    cp(B("pf", 0, 4), B("pc", 0, 4))
    row, grp, odd = pf(1), pf(2), pf(3)
    even, kempty, half, r15, r96, r6 = [pg(a) for a in range(6)]
    line = lambda o, i, a, b: act(o, i, AF.Identity, float(b), float(a))
    fill = lambda o, v: iota(o, [[0, o[4]]], v, 0)
    line(even, odd, -1, 1)
    line(kempty, row, -1, ZB + 16)
    tsc(B("I", -16, 144), B("d"), 0.0, None, OP.is_equal)
    for g2 in range(2):
        for c2 in range(2):
            act(B("PM%d%d" % (g2, c2)), B("I", 16 * (c2 - g2), 16 * (c2 - g2) + 128), AF.Identity, 0.0, (even, odd)[c2])

    tsc(B("LI3f", 0, 3 * C), B("c16"), row, None, OP.add)
    e = lambda w: B("LI3f", 0, w)

    def quot(o, w, k):
        tsc(o, e(w), 1.0 / k, -0.5 + 0.5 / k, OP.mult, OP.add)

    def mixed(name, w, k, a, b):
        quot(B("li", 18, 18 + w), w, k)
        tsc(B("lf", 0, w), B("li", 18, 18 + w), float(b) / a, None, OP.mult)
        tt(B("lf", 0, w), B("lf", 0, w), e(w), OP.add)
        tsc(B(name, 0, w), B("lf", 0, w), float(a), None, OP.mult)
    mixed("Tin", 12, 6, 32, -191)
    for h in range(2):
        line(pg(6 + h), row, 1, 16 * h)
        tsc(B("Tzi%d" % h), B("c16", 0, C), 2.0, pg(6 + h), OP.mult, OP.add)
    mixed("TK", C, C, 2, -2 * C)
    tsc(B("TL"), B("TK"), 1.0, None, OP.add)
    mem(B("ph"), 0.5)
    mem(B("mh"), -0.5)
    line(B("I4k"), B("I"), V, 0)
    tsc(B("sae"), B("sln"), 0.0, kempty, OP.is_lt, OP.mult)
    tt(B("T1"), B("sln"), B("sae"), OP.add)
    vtr(B("T2"), B("T1"))
    gat("V", B("T3"), B("T2"), B("Tin"))
    for h in range(2):
        bk = lease()
        mms(B(bk, 0, H), [(B("PM%d%d" % (g2, h)), B("T3", g2 * H, g2 * H + H)) for g2 in range(2)], f32=True)
        cp(B("s16%d" % h), B(bk, 0, H))
        act(B("s", h, LA, 2), B(bk, 0, H), AF.Copy)
        gat("S", B("Ca%d" % h, ZO, ZO + H), B("zl"), B("Tzi%d" % h))
        mem(B("Oa%d" % h, 16 * H, 17 * H), -1.0)
    mem(B("X", W, W + 16), 0.0)
    line(r15, row, -1, 15)
    tsc(B("SL"), B("d", 16, 160), r15, None, OP.is_equal)
    tsc(B("BO"), B("ch"), grp, None, OP.is_equal)
    tsc(B("GR"), B("cl16"), row, None, OP.is_equal)
    chain("G", asel(B("Tri"), B("BO"), [[1, 128]], OP.is_ge, 0.0, 0, -1))
    for j in range(3):
        act(B("Tr%d" % j), B("Tri"), AF.Identity, 0.0, 1.0 / (j + 0.5))
    for nm, v in (("nI", -1.0), ("I64", -64.0), ("I3", 3.0 * H), ("I2", 2.0 * H), ("I1", 1.0 * H), ("In", -1.0 * H), ("Iq", 1.0 / 256)):
        act(B(nm), B("I"), AF.Identity, 0.0, v)
    act(B("SLL"), B("SL"), AF.Identity, 0.0, H / 2.0)
    for j in range(3):
        act(B("c8", j * C, (j + 1) * C), B("c16", 0, C), AF.Identity, 8.0 * H)
    for h in range(2):
        act(B("cK", h, 12, 2), B("c16", 0, C), AF.Identity, 15.0 * H)
    line(half, row, 0, 0.5)
    mem(B("neg"), -512.0)
    made = {}

    def thr(kind, n):
        if (kind, n) not in made:
            o = made[kind, n] = B("th", len(made), len(made) + 1)
            if kind == "n":
                tsc(o, row, 16 - 4 * n - 0.5, -3.0, OP.is_ge, OP.mult)
                act(o, o, AF.Identity, 12.5)
            else:
                tsc(o, row, n - 0.5, 8.0, OP.is_lt, OP.mult)
                act(o, o, AF.Identity, -7.5)
        return made[kind, n]
    for t in range(VIS):
        for h in range(2):
            thr("n", SN[t][h])
            for x in range(len(SETS)):
                thr("c", 16 - M0[t][h][x])
    act(B("GRh"), B("GR", 0, 128), AF.Identity, 0.0, -0.5)
    if PAR["pk"] or max(PAR["pu"]):
        bk = lease()
        run([m for a in range(3) for m in terms(B(bk, a * H, (a + 1) * H), [(B("I64"), B("GR", 0, H)), (B("I", 1, 129), B("GR", 0, H))])])
        line(B("DPc"), B(bk, 0, 3 * H), 16, 0)
        line(B("DPu"), B(bk, 0, H), 256, 0)
    line(B("SLh"), B("SL"), 0.25, 0)
    tsc(pg(8), row, 14.5, 16.0 * PAR["pk"], OP.is_lt, OP.mult)
    line(pg(10), pg(8), -1, 192)
    act(B("c192"), B("c16", 0, C), AF.Identity, pg(10), 0.0)
    line(B("th", 15, 16), pg(8), 1, A[0] / 2.0 - 4)
    for t in range(1, VIS):
        line(B("th", 11 + t, 12 + t), pg(8), 1, A[t] / 2.0 - 196)
    line(B("BOh"), B("BO"), 0.25, 0)
    tsc(B("WF0", 0, 1), B("WK0", 0, 1), 1.0 / V, None, OP.mult)
    cp(B("WF0", 1, 2), B("WK0", 1, 2))
    act(B("kpd", 0, 1), B("GR", 0, 1), AF.Identity, 0.0, B("WF0", 1, 2))
    bk = lease()
    mm(B(bk, 0, 1), B("BO"), B("kpd", 0, 1), True, True)
    line(pf(7), B(bk, 0, 1), 4, 0)
    act(B("hk", 4, 5), pf(7), AF.Square)
    for t in range(VIS):
        line(B("hk", t, t + 1), B("hk", 4, 5), -0.5, 97.0 * t - 0.375)
    if min(PAR["pu"]) == 0:
        act(B("SWs"), B("SL"), AF.Identity, 0.0, B("WF0", 0, 1))
    if max(PAR["pu"]):
        act(B("BWs"), B("BO"), AF.Identity, 0.0, B("WF0", 0, 1))
    tsc(B("li", 35, 36), B("WK0", 0, 1), 15, None, OP.bitwise_and)
    tsc(pg(9), B("li", 35, 36), 256.0, None, OP.mult)
    act(B("SWn"), B("SL"), AF.Identity, 0.0, pg(9))
    chain("G", send_each(B("WF0", 0, 2), [(B("WF%d" % q, 0, 2), (rank - q) % N, "aW%d" % q) for q in range(1, 5)], 7.0))
    for a, (lo, hi) in enumerate(PIECES):
        if lo >= CUT:
            last = chain("G", hand(B("CL", lo, hi), a))
            for q in range(1 + (lo >= V), 5):
                add("RaH%d%d" % (q, a), None, [B("BK%d" % q, lo, hi)], [], 0.0, sem="aH%d%d" % (q, a),
                    amt=len(topo.engines(helper(topo, me), T.cores[(rank + q) % N])), lat=8.0 * q, after=(last,))
        else:
            last = chain("G", send(B("BK1", lo, hi), B("CL", lo, hi), (rank - 1) % N, "aC%d" % a, PAR["land"]))
    tsc(B("DX"), B("DX"), row, None, OP.is_equal)
    late = lambda j: order_after(j, last)
    bk = lease()
    mms(B(bk, 0, 128), [(B("I"), B("GRh")), (B("I"), B("I64"))])
    line(B("GI"), B(bk, 0, 128), 1, 0)
    line(B("nGI"), B(bk, 0, 128), -1, 0)
    line(B("nI64"), B("I"), 64, 0)
    for h in range(2):
        mem(B("CT%d" % h, 2 * C, 7 * C), 0.0)
        line(B("CT%d" % h, 0, C), B("c16", 0, C), 1, 0)
        line(B("CT%d" % h, C, 2 * C), B("c16", 0, C), 0, 1)
        tsc(B("CT%d" % h, 5 * C, 7 * C, 2), B("Tzi%d" % h), 16.0, None, OP.mult)
        late(fill(B("Ob%d" % h, 16 * H, 17 * H), -1))
        if PAR["ob"][h]:
            late(fill(B("Oa%d" % h, -16, 0), -1))
            late(fill(B("Ob%d" % h, -16, 0), -1))
    late(iota(B("KI0"), [[6, 16], [1, C]], 0, 0))
    if min(PAR["ob"]) == 0:
        for a in range(4):
            late(asel(B("R", 512 * a, 512 * a + 512), B("neg"), [[-1, 4], [-16, 8], [0, 16]], OP.is_equal, 0.0, -4 * a, 1))
        mem(B("rst"), 1.0)
        mem(B("rst", 0, BW, 4), 0.0)
    if max(PAR["ob"]):
        mem(B("rs16"), 1.0)
        mem(B("rs16", 0, 512, 16), 0.0)
        line(r96, row, H, 16)
        late(iota(B("ln0"), [[1, H]], 0, 0))
    late(iota(B("li", 0, 12), [[1, C], [H, 2]], 0, 0))
    line(r6, row, 6, 0)
    late(iota(B("li", 12, 24), [[16, C], [H, 2]], 0, 0))

    def behind_first_clauses():
        order_after(line(B("KIL"), B("KI0"), 1.0 / 16, 0), chains["cS"])
        if max(PAR["ob"]):
            order_after(line(B("lane"), B("ln0"), 1.0 / 64, 0), chains["cS"])
        order_after(tsc(B("Tout"), B("li", 0, 12), r6, None, OP.add), chains["cV"])
        order_after(tsc(B("Tz"), B("li", 12, 24), row, None, OP.add), chains["cV"])

    def book(q):
        return send(B("BK%d" % q, 0, CUT), B("CL", 0, CUT), (rank - q) % N, "aB%d" % q, 14.0)
    order_after(book(2), last)

    Ob = lambda t, h: "O" + "ab"[t % 2] + str(h)
    Cb = lambda t, h: "C" + "ab"[t % 2] + str(h)
    hb = lambda h: (lambda n, *a: B(n + str(h), *a))

    def judge(q):
        act(B("SW%d" % q), B("SL"), AF.Identity, 0.0, B("WF%d" % q, 0, 1))
        act(B("DK"), B("DX"), AF.Identity, 0.0, B("WF%d" % q, 1, 2))
        o = B(lease(), 0, 48 * C)
        mm(o, B("BO"), B("DK"), True, True)
        act(B("KX%d" % q), o, AF.Identity, 0.0, 32.0)

    def gather(t, h):
        nv, js = PAR["gv0" if t == 0 else "gv"][h], []
        for b in range(4):
            js.append(gat("V" if b < nv else "S", B(Ob(t, h), BW * b, BW * b + BW), B("X"), B("s16%d" % h, 24 * b, 24 * b + 24)))
        return js

    def test(t, h, rec, ns, opv, fS, scale, bias, cnt, after=()):
        O = Ob(t, h)
        if ns < 4:
            rep = lease()
            run([(B(rep, a * H, (a + 1) * H), B("I"), rec, True, True) for a in range(4)], after=after)
        order = []
        for x in range(4):
            order += [b for b in (x if x < 4 - ns else None, 4 - ns + x if x < ns else None) if b is not None]
        for x, b in enumerate(order):
            o = B("cmp%d" % h, BW * b, BW * b + BW)
            if b < 4 - ns:
                tt(o, B(O, BW * b, BW * b + BW), B(rep, 0, BW), opv)
            else:
                bk = lease()
                run([(B(bk, 0, BW), B("I"), B(O, BW * b, BW * b + BW), True, False)] + [(B(bk, a * H, (a + 1) * H), B("nI"), rec, False, a == 3) for a in range(4)])
                act(o, B(bk, 0, BW), fS, bias, scale)
            mms(cnt, [(E(k), B("cmp%d" % h, k * H, (k + 1) * H)) for k in range(4 * b, 4 * b + 4)], x == 0, x == 3)

    def cands(t, h, gathered):
        b, zc = hb(h), Cb(t, h)
        z = B(zc, ZO, CO)
        if PAR["z3"][h] and t:
            for a in range(2):
                gcopy(B(zc, a * H, (a + 1) * H), z)
        cnt = B("Ppc%d" % h, 320, 320 + H)
        test(t, h, z, SO[t][h], OP.is_gt, AF.Relu, 1.0, 0.0, cnt, gathered[:1])
        stage("ca", h)
        act(b("op"), cnt, AF.Sign)
        bk = "Ppc%d" % h
        run([(B(bk, j * H, (j + 1) * H), B("Tr%d" % j), b("op"), True, True) for j in range(3)])
        act(b("le"), B(bk, 0, 3 * H), AF.Sign, 1.0, -1.0)
        o = B(bk, 416, 416 + 3 * C)
        rows(o, "SLL", "le%d" % h, 0, 3 * H, ((B("I"), B("c8")),))
        tsc(b("off"), o, row, None, OP.add)
        act(b("K4", C, 4 * C), o, AF.Copy)
        if PAR["z3"][h] and t:
            gtt(B(zc, CO, CO + 3 * H), B(Ob(t, h)), b("off"), B(zc, 0, CO), OP.min)
        else:
            for j in range(3):
                gtt(B(zc, CO + j * H, CO + (j + 1) * H), B(Ob(t, h)), b("off", j * C, (j + 1) * C), z, OP.min)
        bk = lease()
        rows(B(bk, 0, 3 * C), "SW%d" % (t + 1), zc, CO, 3 * H, ((B("I"), B("mh")),))
        tsc(b("ui", 0, 3 * C), B(bk, 0, 3 * C), 0.5 / V, None, OP.add)
        tt(b("uh"), B(bk, 0, 3 * C), b("ui", 0, 3 * C), OP.subtract)
        if True:
            stage("uo", h)
            o = B(lease(), 0, 4 * C)
            rows(o, "SWn", zc, ZO, 4 * H)
            cp(b("ui", 3 * C, 7 * C), o)
            tsc(b("um", 3 * C, 7 * C), b("ui", 3 * C, 7 * C), V - 1, None, OP.bitwise_and)

    def empties(t):
        m = lambda a, b: B("mx", a * 12, b * 12)
        tt(m(0, 8), B("s", 0, 96), B("s", 96, 192), OP.max)
        tt(m(8, 12), m(0, 4), m(4, 8), OP.max)
        tt(m(12, 14), m(8, 10), m(10, 12), OP.max)
        tt(m(14, 15), m(12, 13), m(13, 14), OP.max)
        tsc(B("em", 0, 12), m(14, 15), float(ZB), -1.0, OP.subtract, OP.max)
        act(B("em", 12, 24), B("em", 0, 12), AF.Relu, 0.0, t - 16.0)
        bk = lease()
        mms(B(bk, 0, 12), [(B("I"), B("cK")), (B("In"), B("em", 0, 12)), (B("In"), B("em", 12, 24))])
        for h in range(2):
            act(B("K4%d" % h, 0, C), B(bk, h, 12, 2), AF.Copy)

    def clauses(t, h, x, bk):
        b, q, zc, (j0, j1) = hb(h), t + 1, Cb(t, h), SETS[x]
        w, n = (j1 - j0) * C, (j1 - j0) * H
        cand, cnt, BK = B(zc, CO + j0 * H, CO + j1 * H), B(bk, 0, n), B("BK%d" % q, 0, VX if t else V)
        stage("ha", h, x)
        r = lambda nm, lo=0, hi=16: B(nm, 16 * C * j0 + lo * w, 16 * C * j0 + hi * w)
        u = lease()
        run([(B(u, 0, 16 * w), B("I4k"), B("ph", 0, 16 * w), True, False)] + [(B(u, m * w, (m + 1) * w), B("I4k"), b("uh", j0 * C, j1 * C), False, m == 15) for m in range(16)])
        tt(r("KU%d" % h), B(u, 0, 16 * w), r("KX%d" % q), OP.add)
        tt(r("Hs%d" % h), B(u, 0, 16 * w), r("KU%d" % h), OP.mult)
        tsc(r("Hm%d" % h), r("Hs%d" % h), 5, V - 1, OP.arith_shift_right, OP.bitwise_and)
        tsc(r("ho%d" % h), r("Hm%d" % h), 97.0 * t, None, OP.add)
        ms, nd, sd = 16 - M0[t][h][x], PAR["nd"][x], min(PAR["sd"][x], 512 // n)
        at = CO + j0 * H if j1 == 3 else RO + j0 * H
        got = 1 if j1 == 3 else 0
        while got < nd and nd > 1:
            k = max(1, min(got, nd - got))
            (gcopy if t else scopy)(B(zc, at + got * n, at + (got + k) * n), B(zc, at, at + k * n) if got > 1 else cand)
            got += k
        stage("cl", h, x)
        mv = ms + PAR["mc"][3 * h + x]
        first = mv + PAR["f1"][x] * (nd > 1)
        calls = [((m + 1 - mv) / (16 - ms), "V", m, m + 1) for m in range(mv, first)]
        calls += [((min(m + nd, 16) - mv) / (16 - ms), "V", m, min(m + nd, 16)) for m in range(first, 16, nd)]
        calls += [(min(m + sd, ms) / mv + PAR["sh"], "S", m, min(m + sd, ms)) for m in range(0, ms, sd)]
        calls += [(min(m + sd, mv) / mv + PAR["sh"], "X", m, min(m + sd, mv)) for m in range(ms, mv, sd)]
        done, G, rep = 0, lambda lo, hi: b("G", 16 * H * j0 + lo * n, 16 * H * j0 + hi * n), None
        for _k, e, lo, hi in sorted(calls):
            k = hi - lo
            if e == "V":
                chain("cV", gtt(G(lo, hi), BK, r("ho%d" % h, lo, hi), B(zc, at, at + k * n) if k > 1 else cand, OP.is_le))
            else:
                ring[h] = (ring[h] + 1) % 3
                sg = b("SG", 512 * ring[h], 512 * ring[h] + k * n)
                j = chain("cS", gat("S", sg, BK, r("ho%d" % h, lo, hi)))
            if e == "X":
                if rep is None:
                    rep = lease()
                    run([(B(rep, a * n, (a + 1) * n), B("I"), cand, True, True) for a in range(k)], after=[ops[j]["prev"]])
                chain("cV", tt(G(lo, hi), sg, B(rep, 0, k * n), OP.is_le))
            elif e == "S":
                o = lease()
                run([(B(o, 0, k * n), B("I"), sg, True, False)] + [(B(o, a * n, (a + 1) * n), B("nI"), cand, False, a == k - 1) for a in range(k)])
                act(G(lo, hi), B(o, 0, k * n), AF.Sign, half, -1.0)
            mms(cnt, [(E(m), G(m, m + 1)) for m in range(lo, hi)], done == 0, done + k == 16)
            done += k
        stage("tr", h, x)
        act(b("ge", j0 * H, j1 * H), cnt, AF.Sign, thr("c", ms))

    def trials(t, h):
        b = hb(h)
        nj = lambda j: b("nb", j * C, (j + 1) * C)
        cn = lambda a, e: B("Ppc%d" % h, 3 * H + a * C, 3 * H + e * C)
        qb = lambda j: b("qb", j * C, (j + 1) * C)
        bk = None
        for x, (j0, j1) in enumerate(SETS):
            cb = lease() if x else "Ppc%d" % h
            clauses(t, h, x, cb)
            if t + h + x == 0:
                behind_first_clauses()
            if PAR["jn"][h]:
                j0, j1 = (0, 3) if j1 == 3 else (0, 0)
            for j in range(j0, j0 if PAR["pk"] else j1):
                early, late = [(B("I"), B("c192"))] + [(B("I64"), nj(0))] * (j - 1), [(B("GI"), nj(j - 1))]
                if j == j0:
                    o, all_, alone = B(cb, 3 * H, 3 * H + C), B(cb, 3 * H, 3 * H + (j1 - j0) * C), j1 - j0 == 1
                    rows(all_, "SLh", "ge%d" % h, j0 * H, (j1 - j0) * H, early if j and alone else (), last=j == 0)
                    if j:
                        mms(o, late if alone else early + late, first=False)
                else:
                    o = cn(4, 5)
                    mms(o, early + [(B("I"), b("cs", (j - j0 - 1) * C, (j - j0) * C))] + late)
                if j:
                    tt(nj(j), o, qb(j - 1), OP.is_gt if A[t] % 2 else OP.is_ge)
                elif t == 0:
                    tsc(nj(0), o, A[t] / 2.0 - 4, None, OP.is_ge)
                else:
                    tt(nj(0), o, B("bl%d%d" % (t, h), 0, C), OP.is_ge)
                if j == j0 and j1 - j0 > 1:
                    act(b("cs", 0, (j1 - j0 - 1) * C), B(cb, 3 * H + C, 3 * H + (j1 - j0) * C), AF.Copy)
                if j < 2:
                    bk = bk or lease()
                    mm(B(bk, 0, C), B("GRh"), nj(j), True, True)
                    act(qb(j), B(bk, 0, C), AF.Identity, 192.25 + A[t] // 2 - 4)
            if not PAR["pk"]:
                continue
            if j1 > j0:
                o = B(cb, 0, (j1 - j0) * H)
                mm(o, B("BOh"), b("ge", j0 * H, j1 * H), True, True)
                scan(b("cs", j0 * H, j1 * H), B("DPc", 0, (j1 - j0) * H), o, 0.0, OP.add, OP.max)
            for j in range(j0, j1):
                cs, ge = b("cs", j * H + 15, (j + 1) * H, 16), OP.is_gt if A[t] % 2 else OP.is_ge
                if j == 0 and t == 0:
                    tsc(nj(0), cs, B("th", 15, 16), None, OP.is_ge)
                elif j == 0:
                    tt(nj(0), cs, B("bl%d%d" % (t, h), 0, C), OP.is_ge)
                elif j == 2 and PAR["tf"][h]:
                    mms(cn(5, 6), [(B("nI"), B("c192")), (B("nI64"), nj(0)), (B("nGI"), nj(1)), (B("I"), qb(1))])
                    tt(nj(j), cs, cn(5, 6), ge)
                else:
                    mms(cn(4, 5), [(B("I"), B("c192")), (B("I"), cs)] + [(B("I64"), nj(0))] * (j - 1) + [(B("GI"), nj(j - 1))])
                    tt(nj(j), cn(4, 5), qb(j - 1), ge)
                if j < 2:
                    bk = bk or lease()
                    mm(B(bk, 0, C), B("GRh"), nj(j), True, True)
                    act(qb(j), B(bk, 0, C), AF.Identity, 192.25 + A[t] // 2 - 4)
        sel = lambda a, e: B(bk, (1 + a) * C, (1 + e) * C)
        part = lambda j: [(B(bk, 0, C), B("I%d" % (j + 1)), nj(j), False, False), (sel(0, 1), B("nI"), nj(j), False, False)]
        run([(B(bk, 0, 5 * C), B("I"), b("CT", 0, 5 * C), True, False)] + part(0) + part(1))
        run(part(2) + [(sel(1, 4), B("I"), b("nb"), False, True)])
        tsc(b("bo"), B(bk, 0, C), row, None, OP.add)
        gat(PAR["mg"], b("M"), B(Cb(t, h), ZO, CO + 3 * H), b("bo"))
        stage("po", h, 1)
        tt(b("pr", 0, 8 * C, 2), sel(0, 4), b("um", 3 * C, 7 * C), OP.mult)
        tt(b("pr", 1, 8 * C, 2), sel(0, 4), b("K4"), OP.mult)
        o = cn(6, 8)
        mms(o, [(B("I"), b("CT", 5 * C, 7 * C))] + [(B("Iq"), b("pr", 2 * i * C, 2 * (i + 1) * C)) for i in range(4)])
        cp(b("n16"), B("Ppc%d" % h, 3 * H + 6 * C, 3 * H + 8 * C, 2))
        act(b("put"), o, AF.Copy)
        if t < VIS - 1:
            stage("uo", h, 1)
            bk = lease()
            mm(B(bk, 0, C), B("GRh"), nj(2), True, True)
            act(qb(2), B(bk, 0, C), AF.Identity, 192.25)
            mms(B(bk, 0, C), [(B("GRh"), nj(2)), (B("nI"), qb(2))])
            act(B("bs%d%d" % (t + 1, h), 0, C), B(bk, 0, C), AF.Identity, B("th", 11 + t + 1, 12 + t + 1), -1.0)
            k = send(B("bl%d%d" % (t + 1, h), 0, C), B("bs%d%d" % (t + 1, h), 0, C), (rank - 1) % N, "ab%d%d" % (t + 1, h), 4.0)
            if t < 2 and h == 0:
                chains["book"] = book(t + 3)
                order_after(chains["book"], k)
            elif t < 2:
                order_after(k, chains["book"])

    def post(t, h):
        b = hb(h)
        s = B("s", h, LA, 2)
        stage("su", h)
        gtt(b("eq"), b("put"), B("TL"), B("KIL"), OP.is_equal)
        gtt(b("dd"), b("put"), B("TK"), s, OP.subtract)
        ed = B(lease(), 0, H) if PAR["ep"][h] else b("ed")
        tt(ed, b("eq"), b("dd"), OP.mult)
        tt(s, ed, s, OP.add)
        if t < VIS - 1:
            cp(b("s16"), s)

    def near(t, h):
        b, O = hb(h), Ob(t, h)
        cnt = B("Ppc%d" % h, 416, 416 + H)
        test(t, h, b("M"), SN[t][h], OP.is_le, AF.Sign, -1.0, half, cnt)
        act(b("nn"), cnt, AF.Relu, thr("n", SN[t][h]), -1.0)
        stage("mx", h)
        last = ()
        if PAR["ob"][h]:
            bk = lease()
            mms(B(bk, 0, H), [(B("I"), B("lane")), (B("I64"), b("nn"))])
            mm(B(bk, BW, BW + H), B("I"), b("M"), True, True)
            tsc(b("o2"), B(bk, 0, H), 64.0, r96, OP.mult, OP.add)
            for x in range(3):
                gat("V" if x < PAR["ob"][h] - 1 else "S", b("cmp", 512 * x, 512 * x + 512), B(O, -16, 16 * H), b("o2", 32 * x, 32 * x + 32))
                scan(b("ac4", 512 * x, 512 * x + 512), B("rs16"), b("cmp", 512 * x, 512 * x + 512), 0.0, OP.mult, OP.max)
            tt(b("cc"), B(bk, BW, BW + H), b("ac4", 15, 16 * H, 16), OP.max)
        for x in range(0 if PAR["ob"][h] else 4):
            bk = lease()
            ms = [m for k in range(4 * x, 4 * x + 4) for m in terms(B(bk, k % 4, BW, 4), [(B("R", 128 * k, 128 * k + 128), b("nn")), (B("I"), B(O, k * H, (k + 1) * H))])]
            last = (run(ms + [(B(bk, BW, BW + H), B("I"), b("M"), True, True)] * (x == 3), after=last),)
            if x > 0:
                for y in range(PAR["sp"][h]):
                    w = BW // PAR["sp"][h]
                    tt(b("acc", y * w, (y + 1) * w), B(bk, y * w, (y + 1) * w), b("acc", y * w, (y + 1) * w), OP.max)
            elif PAR["a1"][h] == "S":
                act(b("acc"), B(bk, 0, BW), AF.Relu)
            else:
                tsc(b("acc"), B(bk, 0, BW), 0.0, None, OP.max)
        if not PAR["ob"][h]:
            scan(b("ac4", 0, BW), B("rst"), b("acc"), 0.0, OP.mult, OP.max)
            tt(b("cc"), B(bk, BW, BW + H), b("ac4", 3, BW, 4), OP.max)
        stage("uc", h)
        if PAR["pu"][h]:
            mm(B("Ppc%d" % h, 0, H), B("BWs"), b("cc"), True, True)
            scan(b("us"), B("DPu"), B("Ppc%d" % h, 0, H), 0.0, OP.add, OP.max)
            o = b("us", 15, H, 16)
        else:
            o = B("Ppc%d" % h, 306, 306 + C)
            rows(o, "SWs", "cc%d" % h, 0, H)
        ci = lambda a: b("ci", a * C, (a + 1) * C)
        hf = lambda a: b("hf", a * C, (a + 1) * C)
        tsc(ci(0), o, -0.5 + 0.5 / V, None, OP.add)
        tt(hf(0), o, ci(0), OP.subtract)
        act(hf(1), hf(0), AF.Square, pf(7), V / 4.0)
        tsc(ci(2), hf(1), 0.5, B("hk", t, t + 1), OP.mult, OP.add)
        tsc(ci(3), ci(2), V - 1, None, OP.bitwise_and)
        cp(b("hc"), ci(3))
        if t < VIS - 1 and PAR["df"][h]:
            gat("S", b("df"), B("CL"), b("hc"))
            o = B("Ppc%d" % h, 0, H)
            mms(o, ((B("nI"), b("cc")), (B("I"), b("df"))))
            act(B(Cb(t + 1, h), ZO, ZO + H), o, AF.Abs)
        elif t < VIS - 1:
            gtt(b("df"), B("CL"), b("hc"), b("cc"), OP.subtract)
            act(B(Cb(t + 1, h), ZO, ZO + H), b("df"), AF.Abs)
        else:
            gtt(B("dfl", h * H, (h + 1) * H), B("CL"), b("hc"), b("cc"), OP.subtract)

    judge(1)
    for t in range(VIS):
        got, bias[1] = [], t
        for h in range(2):
            stage("ga", h)
            got.append(gather(t, h))
        stage("em")
        empties(t)
        for h in range(2):
            stage("op", h)
            cands(t, h, got[h])
            trials(t, h)
            post(t, h)
        stage("")
        if t < VIS - 1:
            judge(t + 2)
        for h in range(2):
            stage("po", h)
            scat(B("X"), B("n16%d" % h), B("M%d" % h))
            stage("ne", h)
            near(t, h)
        stage("")

    stores = [dma("Y", D("yx", 0, W), B("X", 0, W), "dyx", 5.0)]
    bk = lease()
    for g2 in range(2):
        mms(B(bk, g2 * H, g2 * H + H), [(B("PM%d%d" % (c2, g2)), B("s", c2, LA, 2)) for c2 in (1, 0)], f32=True)
    act(B("T3"), B(bk, 0, LA), AF.Copy)
    gat("S", B("T4"), B("T3"), B("Tout"))
    vtr(B("T5"), B("T4"))
    tsc(B("T6"), B("T5"), float(ZB), kempty, OP.is_ge, OP.mult)
    tt(B("T7"), B("T5"), B("T6"), OP.subtract)
    stores.append(dma("Y", D("yl", 0, LA), B("T7"), "dyl", 2.2))
    gat("S", B("zo"), B("dfl"), B("Tz"), AF.Abs)
    stores.append(dma("S", D("yz", 0, LA), B("zo"), "dyz", 1.8))

    add("Rend", None, [], [B("zo")], 0.0, sem="-", amt=0, lat=0.0, after=stores)
    if not PLAN:
        PLAN.append(schedule(ops, leases, bank))
    order, where, extra, times = PLAN[0]
    for i, j in extra:
        ops[i]["deps"][j] = True
    for name, b in where.items():
        for r, p, step in leases[name]["regs"]:
            r[3] = view("Ppr%d" % b, p, r[1], r[2], step)
    emit(g, T, ops, order, sent[0], times)
    if report is not None:
        report.append((ops, order))


def place(ops, pred, succ, key):
    left, est, start, busy = [len(p) for p in pred], [0.0] * len(ops), [0.0] * len(ops), {o["eng"]: [] for o in ops}
    ready = sorted((key[i], i) for i in range(len(ops)) if left[i] == 0)
    while ready:
        i = ready.pop(0)[1]
        c, s = ops[i]["cost"], est[i]
        q = busy[ops[i]["eng"]]
        n = lo = len(q)
        while lo and q[lo - 1][1] > s:
            lo -= 1
        while lo < n and q[lo][0] < s + c:
            s = q[lo][1]
            lo += 1
        e = s + c
        q.insert(lo, (s, e))
        start[i] = s
        for k, lat in succ[i]:
            if e + lat > est[k]:
                est[k] = e + lat
            left[k] -= 1
            if left[k] == 0:
                x = (key[k], k)
                at = len(ready)
                while at and ready[at - 1] > x:
                    at -= 1
                ready.insert(at, x)
    return start, 0.0


def schedule(ops, leases, bank):
    n = len(ops)
    price = lambda c, k, ga, sc, wake, pe, least: c[0] + CY * k * (c[1] + ga * c[2] + sc * c[3] + pe * sum(max(least, x) for x in c[4:]))
    ops = [dict(o, cost=price(o["cost"], *PAR["pace"][0]), lat=PAR["pace"][0][3] if o["lat"] is None else o["lat"], raw=o) for o in ops]
    pred, succ, tail, done = [[] for _ in range(n)], [[] for _ in range(n)], [0.0] * n, [0] * n
    for i, o in enumerate(ops):
        held = [j for j, w in o["deps"].items() if w or o["eng"][0] == "R" or ops[j]["eng"] == o["eng"]]
        for j in held:
            done[i] |= done[j]
        o["deps"] = {j: w for j, w in o["deps"].items() if not done[i] >> j & 1}
        for j in held:
            done[i] |= int(o["raw"]["deps"][j] or o["eng"][0] == "R") << j
    for i, o in enumerate(ops):
        for j, w in o["deps"].items():
            lat = ops[j]["lat"] if w or ops[j]["eng"] != o["eng"] else 0.0
            pred[i].append((j, lat))
            succ[j].append((i, lat))
    for i in range(n - 1, -1, -1):
        tail[i] = ops[i]["cost"] + max([tail[k] + lat for k, lat in succ[i]] + [ops[i]["lat"]])
    plain, eng = [], [o["eng"] for o in ops]
    for pace in PAR["pace"]:
        lat = [pace[3] if o["raw"]["lat"] is None else o["lat"] for o in ops]
        waits = [[(j, lat[j] if w or o["eng"][0] == "R" else 0.0) for j, w in o["deps"].items() if w or o["eng"][0] == "R" or ops[j]["eng"] == o["eng"]] for o in ops]
        plain.append(([price(o["raw"]["cost"], *pace) for o in ops], waits, lat))

    def with_banks(extra):
        out = []
        for cost, waits, lat in plain:
            waits = list(waits)
            for i, j in extra:
                waits[i] = waits[i] + [(j, lat[j])]
            out.append((cost, waits))
        return out
    key, best, rng = [-tail[i] - ops[i]["bias"] for i in range(n)], None, np.random.default_rng(PAR["seed"])
    names = sorted(set(o["stage"] for o in ops))
    kind = [names.index(o["stage"]) for o in ops]
    for x in range(PAR["passes"]):
        start, end = place(ops, pred, succ, key)
        got = banks(ops, leases, bank, pred, succ, start)
        worth = 1e9
        if best is None or got[0] < best[1][0] + PAR["cut"]:
            worth = sum(replay(eng, c, w, got[1])[0][-1] / p[0] for (c, w), p in zip(with_banks(got[3]), PAR["pace"]))
        if best is None or worth <= best[0] + PAR["warm"] * rng.random():
            best = (worth, got, start)
            if x == 0 or worth < top[0]:
                top = best
        start = best[2] if x >= 2 else start
        shift = rng.normal(0.0, PAR["noise"][0], len(names)) * (rng.random(len(names)) < PAR["noise"][1]) * (x >= 2)
        if x >= 2 and rng.random() < PAR["noise"][2]:
            key = [start[i] + shift[kind[i]] for i in range(n)]
            continue
        back, _e = place(ops, succ, pred, [-(start[i] + ops[i]["cost"] + shift[kind[i]]) for i in range(n)])
        key = [-(back[i] + ops[i]["cost"]) for i in range(n)]
    best = top[1]
    _end, order, where, extra = best
    paces = with_banks(extra)
    before, behind = [set(o["deps"]) for o in ops], [set() for o in ops]
    for i, j in extra:
        before[i].add(j)
    for i in range(n):
        for j in before[i]:
            behind[j].add(i)
    same, seen = {}, {}
    for i, o in enumerate(ops):
        k = (o["eng"], o["lab"].replace("b", "a"), o["visit"])
        seen[k] = seen.get(k, 0) + 1
        o["twin"] = (k[0], k[1], seen[k])
        same.setdefault(o["twin"], []).append(i)
    order, ends = polish(eng, paces, before, behind, order, [same[o["twin"]] for o in ops])
    PAR["ideal"] = (end, best[0], max(tail), ends)
    PAR["dbg"] = (ops, paces, order, before)
    times = [(replay(eng, c, w, order)[0], c) for c, w in paces]
    order.sort(key=lambda i: 0)
    return order, where, extra, times


def replay(eng, cost, waits, order):
    end, by, last = [0.0] * len(eng), [-1] * len(eng), {}
    for i in order:
        j = last.get(eng[i], -1)
        s = end[j] if j >= 0 else 0.0
        for k, lat in waits[i]:
            if end[k] + lat > s:
                s, j = end[k] + lat, k
        end[i], by[i], last[eng[i]] = s + cost[i], j, i
    return end, by


def in_order(key, before, behind):
    left, out = [len(p) for p in before], []
    late = [False] * len(key)
    for i in sorted(range(len(key)), key=lambda j: key[j]):
        late[i] = True
        todo = [i] if left[i] == 0 else []
        while todo:
            j = todo.pop()
            out.append(j)
            for k in behind[j]:
                left[k] -= 1
                if left[k] == 0 and late[k]:
                    todo.append(k)
    return out


def polish(eng, paces, before, behind, order, twins):
    rng, tip = np.random.default_rng(PAR["seed"]), eng.index("Rend")
    got = [replay(eng, c, w, order) for c, w in paces]
    first = [e[tip] for e, by in got]
    worth = lambda g: sum((e[tip] + PAR["soon"] * sum(e) / len(e)) / f for (e, by), f in zip(g, first))
    now = worth(got)
    for x in range(PAR["moves"]):
        end, by = got[x % len(paces)]
        pairs, i = [], tip
        while by[i] >= 0:
            if eng[by[i]] == eng[i] and by[i] not in before[i]:
                pairs.append((by[i], i))
            i = by[i]
        if not pairs:
            break
        a, b = pairs[int(rng.integers(len(pairs)))]
        pa, pb = order.index(a), order.index(b)
        far = int(rng.integers(3))
        if rng.random() < PAR["wide"]:
            cost, up = paces[x % len(paces)][0], rng.random() < 0.5
            key = [e - c for e, c in zip(end, cost)]
            span, step = 4.0 * rng.random(), 0.2 + 2.0 * rng.random() ** 2
            todo = list(twins[b if up else a]) if rng.random() < 0.6 else [b if up else a]
            move = {i: key[i] for i in todo}
            while todo:
                i = todo.pop()
                for j in (before if up else behind)[i]:
                    if j not in move and abs(key[j] - move[i]) < span:
                        move[j] = move[i]
                        todo.append(j)
            for i in move:
                key[i] += -step if up else step
            new = in_order(key, before, behind)
        elif x // len(paces) % 2:
            while far and pa > 0:
                pa -= 1
                far -= eng[order[pa]] == eng[b]
            a, move = order[pa], {b}
            for i in reversed(order[pa:pb]):
                if behind[i] & move:
                    move.add(i)
            if a in move:
                continue
            new = order[:pa] + [i for i in order[pa:pb + 1] if i in move] + [i for i in order[pa:pb + 1] if i not in move] + order[pb + 1:]
        else:
            while far and pb < len(order) - 1:
                pb += 1
                far -= eng[order[pb]] == eng[a]
            b, move = order[pb], {a}
            for i in order[pa + 1:pb + 1]:
                if before[i] & move:
                    move.add(i)
            if b in move:
                continue
            new = order[:pa] + [i for i in order[pa:pb + 1] if i not in move] + [i for i in order[pa:pb + 1] if i in move] + order[pb + 1:]
        trial = [replay(eng, c, w, new) for c, w in paces]
        if worth(trial) <= now + PAR["heat"] * (1 - x / PAR["moves"]) * rng.random():
            order, got, now = new, trial, worth(trial)
    return order, [round(e[tip], 1) for e, by in got]


def banks(ops, leases, bank, pred, succ, start):
    n = len(ops)
    left, free, est, where, extra = [len(p) for p in pred], {}, [0.0] * n, {}, []
    holder, since, todo = [None] * PAR["nr"], [0.0] * PAR["nr"], {l: len(x["ops"]) for l, x in leases.items()}
    rest, order = sorted(range(n), key=lambda i: (-start[i], -i)), []
    while rest:
        at, idle = len(rest) - 1, None
        while True:
            i = rest[at]
            l = ops[i]["lease"]
            if left[i] == 0 and l is not None and l not in where and idle is None:
                idle = [b for b, x in enumerate(holder) if x is None or todo[x] == 0]
            if left[i] == 0 and (l is None or l in where or idle):
                break
            at -= 1
        del rest[at]
        o = ops[i]
        s = max(free.get(o["eng"], 0.0), est[i])
        if l is not None and l not in where:
            b = min(idle, key=lambda x: since[x])
            s = max(s, since[b])
            if holder[b] is not None:
                extra += [(i, j) for j in bank[holder[b]][1]]
            holder[b], where[l] = l, b
        end = free[o["eng"]] = s + o["cost"]
        if l is not None:
            todo[l] -= 1
            since[where[l]] = max(since[where[l]], end + o["lat"])
        order.append(i)
        for k, lat in succ[i]:
            if end + lat > est[k]:
                est[k] = end + lat
            left[k] -= 1
    return max(free.values()), order, where, extra


def emit(g, T, ops, order, nsent, times):
    queue = {"V": g.vector, "S": g.scalar, "P": g.tensor, "G": g, "Y": g.sync}
    need = set()
    for o in ops:
        for j, w in o["deps"].items():
            if w:
                need.add(j)
    total, mark, marks, know, snap = {}, {}, {}, {}, {}
    for i in order:
        o = ops[i]
        e = o["eng"]
        if e == "Rend":
            continue
        if e[0] == "R":
            total[o["sem"]] = o["amt"]
            mark[i] = (o["sem"], o["amt"])
            snap[i] = {}
            continue
        k = know.setdefault(e, {})
        want = {}
        for j, w in o["deps"].items():
            if w:
                s, v = mark[j]
                if k.get(s, 0) < v and want.get(s, (0, 0))[0] < v:
                    want[s] = (v, j)
        for s in list(want):
            if any(s2 != s and snap[want[s2][1]].get(s, 0) >= want[s][0] for s2 in want):
                del want[s]
        for s, (v, j) in want.items():
            while s in marks and v < len(marks[s]) and all(end[marks[s][v]] + PAR["spare"] <= end[i] - cost[i] for end, cost in times):
                v, j = v + 1, marks[s][v]
            queue[e].wait_ge(T.sem[s], v)
            k[s] = max(k.get(s, 0), v)
            for s2, v2 in snap[j].items():
                k[s2] = max(k.get(s2, 0), v2)
        ins = o["call"]()
        if o["sem"] == "-":
            continue
        if o["sem"] is not None:
            ins.then_inc(T.sem[o["sem"]], o["amt"])
            total[o["sem"]] = o["amt"]
            mark[i] = (o["sem"], o["amt"])
        elif i in need:
            s = "e" + e
            ins.then_inc(T.sem[s], 1)
            total[s] = total.get(s, 0) + 1
            mark[i] = (s, total[s])
            marks.setdefault(s, []).append(i)
        else:
            continue
        snap[i] = dict(k)
    for s, v in total.items():
        if know.get("G", {}).get(s, 0) < v:
            g.wait_ge(T.sem[s], v)
    g.wait_ge(T.sem.sent, nsent)
